import numpy as np
import ml_dtypes


def mxq(x, axis, fmt="e4m3"):
    dtype, down = {"e4m3": (ml_dtypes.float8_e4m3fn, 7), "e5m2": (ml_dtypes.float8_e5m2, 14)}[fmt]
    v = np.moveaxis(np.asarray(x, np.float32).astype(ml_dtypes.bfloat16).astype(np.float64), axis, -1)
    blocks = v.reshape(v.shape[:-1] + (-1, 32))
    amax = np.abs(blocks).max(-1, keepdims=True)
    byte = np.maximum(np.where(amax > 0, np.frexp(amax)[1] - 1 + 127, 0) - down, 1)
    scale = np.exp2(byte - 127.0)
    codes = (blocks / scale).astype(np.float32).astype(dtype).astype(np.float64)
    return np.moveaxis((codes * scale).reshape(v.shape), -1, axis)


WIDE = False


def mx_kscale(k):
    if not WIDE:
        return np.ones(k)
    levels = np.array([30, -30])
    if k % 512:
        return np.exp2(np.random.permutation(np.resize(levels, k // 32))).repeat(32)
    a = np.empty((k // 512, 16))
    for p in range(k // 512):
        a[p, :8] = np.random.permutation(np.resize(levels, 8))
        for g in range(8):
            far = levels[np.abs(levels - a[p, g]) >= 10]
            a[p, g + 8] = far[np.random.randint(len(far))]
    return np.exp2(a.ravel()).repeat(32)


def f64(x):
    return np.asarray(x).astype(np.float64)


def striped(idx):
    return np.tile(idx.reshape(-1, 16).T, (8, 1)).astype(np.uint16)


def unstriped(offs):
    return offs[:16].T.reshape(-1).astype(np.int64)


def bf(x):
    return np.asarray(x, np.float32).astype(ml_dtypes.bfloat16)


E2M1 = np.array([0.0, 0.5, 1.0, 1.5, 2.0, 3.0, 4.0, 6.0, -0.0, -0.5, -1.0, -1.5, -2.0, -3.0, -4.0, -6.0])


def pack_weight(w, fmt):
    k, n = w.shape
    w = f64(bf(w)).reshape(k // 32, 32, n)
    amax = np.abs(w).max(1)
    if fmt in ("e4m3", "e5m2"):
        byte = np.frexp(amax)[1] - 1 + 127 - (7 if fmt == "e4m3" else 14)
    else:
        mant, ex = np.frexp(amax / 6.0)
        byte = np.where(mant > 0.5, ex, ex - 1) + 127
    byte = np.clip(np.where(amax > 0, byte, 1), 1, 254)
    scaled = (w * np.exp2(127.0 - byte)[:, None, :]).reshape(k, n).astype(np.float32)
    by_word = np.ascontiguousarray(scaled.reshape(k // 512, 128, 4, n).transpose(0, 1, 3, 2))
    if fmt in ("e4m3", "e5m2"):
        words = by_word.astype(ml_dtypes.float8_e4m3fn if fmt == "e4m3" else ml_dtypes.float8_e5m2).view(np.uint8)
    else:
        c = by_word.astype(ml_dtypes.float4_e2m1fn).view(np.uint8) & 0xF
        words = c[..., 0::2] | (c[..., 1::2] << 4)
    return np.ascontiguousarray(words), np.ascontiguousarray(byte.astype(np.uint8).reshape(k // 512, 16, n))


def unpack_weight(words, scales, fmt):
    g, p, n, _ = words.shape
    if fmt in ("e4m3", "e5m2"):
        vals = np.ascontiguousarray(words).view(ml_dtypes.float8_e4m3fn if fmt == "e4m3" else ml_dtypes.float8_e5m2).astype(np.float64)
    else:
        nib = np.empty((g, p, n, 4), np.uint8)
        nib[..., 0::2] = words & 0xF
        nib[..., 1::2] = words >> 4
        vals = E2M1[nib]
    vals = vals * np.repeat(np.exp2(scales.astype(np.float64) - 127.0), 8, axis=1)[..., None]
    return vals.transpose(0, 1, 3, 2).reshape(g * 512, n)


K, H, N, T, S, T2 = 512, 1536, 1024, 2048, 1024, 2048

def setup_inputs():
    n = np.random.standard_normal
    s = mx_kscale(K)[:, None]
    u = mx_kscale(H)[:, None]
    tab = n((K, T)) * np.exp(1.0 * n((1, T))) * s
    tab_words, tab_scales = pack_weight(tab, "e5m2")
    w2 = n((K, H)) / np.sqrt(K) * u.T / s
    w1 = n((H, N)) / np.sqrt(H) / u
    w1_words, w1_scales = pack_weight(w1, "e4m3")
    return {
        "tab_words": tab_words, "tab_scales": tab_scales,
        "offs": striped(np.random.permutation(T)[:S]),
        "offs2": striped(np.random.permutation(T2)[:S]),
        "w2": w2.astype(np.float32),
        "w1_words": w1_words, "w1_scales": w1_scales,
        "sT": np.tanh(0.8 * n((H, T))).astype(np.float32),
        "wgo": np.exp(0.3 * n((128, S))).astype(np.float32),
    }

def reference(tab_words, tab_scales, offs, offs2, w2, w1_words, w1_scales, sT, wgo):
    v = unpack_weight(tab_words, tab_scales, "e5m2")[:, unstriped(offs)]
    s_ = f64(sT)[:, unstriped(offs)]
    d = mxq(f64(w2), 0, "e4m3").T @ v
    h = d * ((1.0 - s_) * (1.0 + s_))
    w1 = unpack_weight(w1_words, w1_scales, "e4m3")
    y = w1.T @ mxq(h, 0, "e4m3")
    out = np.zeros((N, T2))
    out[:, unstriped(offs2)] = np.tile(f64(wgo), (N // 128, 1)) * y
    return out

@@ -1,0 +1,242 @@
+from contextlib import ExitStack
+
+import concourse.mybir as mybir
+
+K, H, N, T, S, T2 = 512, 1536, 1024, 2048, 1024, 2048
+FLOPS = 2 * K * H * S + 2 * H * N * S
+
+F32 = mybir.dt.float32
+BF16 = mybir.dt.bfloat16
+I32 = mybir.dt.int32
+U32 = mybir.dt.uint32
+U16 = mybir.dt.uint16
+U8 = mybir.dt.uint8
+E4M3 = mybir.dt.float8_e4m3fn_x4
+E5M2 = mybir.dt.float8_e5m2_x4
+ACT = mybir.ActivationFunctionType
+ALU = mybir.AluOpType
+
+P = 128
+PACK = 4
+PASS = P * PACK
+PASSES = H // PASS
+HALF = 512
+HALVES = S // HALF
+BLOCKS = N // P
+PER_COLUMN = 16
+SPLIT_BLOCKS = 2
+
+
+def tile_list_fibre_equaliser_backward_kernel(
+    tc, tab_words, tab_scales, offs, offs2, w2, w1_words, w1_scales, sT, wgo, out
+):
+    nc = tc.nc
+    with ExitStack() as ctx:
+        keep = ctx.enter_context(tc.tile_pool(name="keep", bufs=1))
+        rows = ctx.enter_context(tc.tile_pool(name="rows", bufs=9))
+        ring = ctx.enter_context(tc.tile_pool(name="ring", bufs=3))
+        psum = ctx.enter_context(tc.psum_pool(name="psum", bufs=4))
+
+        idx = keep.tile([P, S // PER_COLUMN], U16, name="idx")
+        idx2 = keep.tile([P, S // PER_COLUMN], U16, name="idx2")
+        tab_w = keep.tile([P, T], I32, name="tab_w")
+        tab_s = keep.tile([P, T], U8, name="tab_s")
+        v_w = keep.tile([P, S], U32, name="v_w", align_bytes=64)
+        v_s = keep.tile([P, S], U8, name="v_s", align_bytes=64)
+        w1_w = keep.tile([P, PASSES, N], I32, name="w1_w", align_bytes=64)
+        w1_s = keep.tile([P, N], U8, name="w1_s", align_bytes=64)
+        wgo_sb = keep.tile([P, S], F32, name="wgo_sb")
+        frames = [keep.tile([P, T2], F32, name="frame%d" % f) for f in range(2)]
+
+        def listed(tile, cols):
+            return tile[:, cols.start // PER_COLUMN : cols.stop // PER_COLUMN]
+
+        nc.vector.memset(tab_s[:].bitcast(I32), 0)
+        nc.vector.memset(w1_s[:].bitcast(I32), 0)
+        for frame in frames:
+            nc.vector.memset(frame[:], 0.0)
+
+        s_rows = sT.rearrange("(a p t) c -> a t p c", p=P, t=PACK)
+        s_sb = {}
+        w2_raw = {}
+
+        def load_s(a, t):
+            s_sb[a, t] = rows.tile([P, T], F32, name="s_sb", tag="row")
+            nc.sync.dma_start(s_sb[a, t][:], s_rows[a, t])
+
+        def load_w2(a):
+            w2_raw[a] = ring.tile([P, PACK, PASS], F32, name="w2_raw")
+            nc.sync.dma_start(
+                w2_raw[a][:], w2[:, a * PASS : (a + 1) * PASS].rearrange("(p j) c -> p j c", j=PACK)
+            )
+
+        nc.sync.dma_start(idx[:], offs)
+        nc.sync.dma_start(tab_w[:], tab_words[0].rearrange("p t i -> p (t i)").bitcast(I32))
+        for q in range(4):
+            nc.scalar.dma_start(
+                tab_s[32 * q : 32 * q + 4, :].bitcast(I32), tab_scales[0, 4 * q : 4 * q + 4, :].bitcast(I32)
+            )
+        for a in range(PASSES):
+            load_s(a, 0)
+            load_w2(a)
+            for t in range(1, PACK):
+                load_s(a, t)
+        for q in range(4):
+            nc.sync.dma_start(
+                w1_s[32 * q : 32 * q + 4 * PASSES, :].bitcast(I32),
+                w1_scales[:, 4 * q : 4 * q + 4, :].bitcast(I32),
+            )
+        nc.sync.dma_start(w1_w[:], w1_words.rearrange("a p n i -> p a (n i)").bitcast(I32))
+        nc.sync.dma_start(idx2[:], offs2)
+        nc.sync.dma_start(wgo_sb[:], wgo)
+
+        last_frame = rows.tile([P, T2], F32, name="last_frame", tag="row")
+        nc.gpsimd.memset(last_frame[:], 0.0)
+        frames.append(last_frame)
+
+        w2_w, w2_s, h_w, h_s, h_rows, h_words = {}, {}, {}, {}, {}, {}
+        w2_grouped, squares = {}, {}
+
+        def round_w2(a):
+            w2_grouped[a] = ring.tile([P, PASS * PACK], BF16, name="w2_grouped", align_bytes=64, tag="grouped")
+            nc.scalar.copy(
+                w2_grouped[a][:].rearrange("p (t m j) -> p m j t", t=PACK, j=PACK),
+                w2_raw[a][:].rearrange("p j (m t) -> p m j t", t=PACK),
+            )
+
+        def quantize_w2(a):
+            w2_w[a] = keep.tile([P, PASS], U32, name="w2_w%d" % a, align_bytes=64)
+            w2_s[a] = keep.tile([P, PASS], U8, name="w2_s%d" % a, align_bytes=64)
+            nc.vector.quantize_mx(out=w2_w[a][:].bitcast(E4M3), scales=w2_s[a][:], in_=w2_grouped[a][:])
+
+        def gather_s(a, t, cols):
+            width = cols.stop - cols.start
+            picked = ring.tile([P, width], F32, name="picked", tag="picked")
+            nc.vector.tensor_copy(picked[:], s_sb[a, t][:].indirect(listed(idx, cols)))
+            square = ring.tile([P, width], F32, name="square", tag="square")
+            nc.scalar.activation(square[:], picked[:], ACT.Square)
+            for half in range(cols.start // HALF, cols.stop // HALF):
+                lo = half * HALF - cols.start
+                squares[a, t, half] = square[:, lo : lo + HALF]
+
+        def derivative(a, t, half):
+            cols = slice(half * HALF, (half + 1) * HALF)
+            rcols = slice(t * P, (t + 1) * P)
+            d = psum.tile([P, HALF], F32, name="d")
+            nc.tensor.matmul_mx(
+                out=d[:],
+                lhsT=w2_w[a][:, rcols].bitcast(E4M3),
+                lhsT_scale=w2_s[a][:, rcols],
+                rhs=v_w[:, cols].bitcast(E5M2),
+                rhs_scale=v_s[:, cols],
+                start=True,
+                stop=True,
+            )
+            if t == 0:
+                h_rows[a, half] = ring.tile([P, PACK, HALF], BF16, name="h_rows")
+            nc.vector.scalar_tensor_tensor(
+                h_rows[a, half][:, t, :], squares[a, t, half], 1.0, d[:], ALU.subtract, ALU.mult
+            )
+
+        def interleave_h(a, half):
+            h_words[a, half] = ring.tile([P, HALF * PACK], BF16, name="h_words", align_bytes=64, tag="grouped")
+            nc.scalar.copy(
+                h_words[a, half][:].rearrange("p (c i t) -> p c t i", i=4, t=PACK),
+                h_rows[a, half][:].rearrange("p t (c i) -> p c t i", i=4),
+            )
+
+        def quantize_h(a, half):
+            h_w[a, half] = keep.tile([P, HALF], U32, name="h_w%d%d" % (a, half), align_bytes=64)
+            h_s[a, half] = keep.tile([P, HALF], U8, name="h_s%d%d" % (a, half), align_bytes=64)
+            nc.vector.quantize_mx(
+                out=h_w[a, half][:].bitcast(E4M3), scales=h_s[a, half][:], in_=h_words[a, half][:]
+            )
+
+        y_sb = {}
+
+        def product(n, half):
+            ncols = slice(n * P, (n + 1) * P)
+            y = psum.tile([P, HALF], F32, name="y")
+            for a in range(PASSES):
+                nc.tensor.matmul_mx(
+                    out=y[:],
+                    lhsT=w1_w[:, a, ncols].bitcast(E4M3),
+                    lhsT_scale=w1_s[4 * a :, ncols],
+                    rhs=h_w[a, half][:].bitcast(E4M3),
+                    rhs_scale=h_s[a, half][:],
+                    start=(a == 0),
+                    stop=(a == PASSES - 1),
+                )
+            if half == 0:
+                y_sb[n] = ring.tile([P, S], F32, name="y_sb")
+            nc.scalar.activation(y_sb[n][:, half * HALF : (half + 1) * HALF], y[:], ACT.Copy, scale=-1.0)
+
+        def place(n, cols):
+            frame = frames[n % len(frames)]
+            nc.vector.tensor_tensor(frame[:].indirect(listed(idx2, cols)), y_sb[n][:, cols], wgo_sb[:, cols], ALU.mult)
+
+        def store(n):
+            nc.sync.dma_start(out[n * P : (n + 1) * P, :], frames[n % len(frames)][:])
+
+        whole = slice(0, S)
+        halves = [slice(h * HALF, (h + 1) * HALF) for h in range(HALVES)]
+
+        nc.vector.tensor_copy(v_s[:], tab_s[:].indirect(idx[:]))
+        nc.vector.tensor_copy(v_w[:], tab_w[:].bitcast(U32).indirect(idx[:]))
+        round_w2(0)
+        gather_s(0, 0, whole)
+        quantize_w2(0)
+
+        last = PASSES - 1
+        for i in range(1, last * PACK + 1):
+            a, t = divmod(i, PACK)
+            pa, pt = divmod(i - 1, PACK)
+            if t == 1:
+                round_w2(a + 1)
+            if a < last:
+                gather_s(a, t, whole)
+            else:
+                gather_s(a, t, halves[0])
+            if t == 2:
+                quantize_w2(a + 1)
+                if a > 0:
+                    for half in range(HALVES):
+                        quantize_h(a - 1, half)
+            for half in range(HALVES):
+                derivative(pa, pt, half)
+            if pt == PACK - 1:
+                for half in range(HALVES):
+                    interleave_h(pa, half)
+
+        for t in range(1, PACK):
+            gather_s(last, t, halves[0])
+            derivative(last, t - 1, 0)
+            if t == 2:
+                for half in range(HALVES):
+                    quantize_h(last - 1, half)
+        gather_s(last, 0, halves[1])
+        derivative(last, PACK - 1, 0)
+        interleave_h(last, 0)
+        for t in range(1, PACK):
+            gather_s(last, t, halves[1])
+            derivative(last, t - 1, 1)
+            if t == 2:
+                quantize_h(last, 0)
+                for n in range(SPLIT_BLOCKS):
+                    product(n, 0)
+        derivative(last, PACK - 1, 1)
+        interleave_h(last, 1)
+        place(0, halves[0])
+        quantize_h(last, 1)
+        for n in range(SPLIT_BLOCKS):
+            product(n, 1)
+        for n in range(1, SPLIT_BLOCKS):
+            place(n, halves[0])
+        for n in range(SPLIT_BLOCKS):
+            place(n, halves[1])
+            store(n)
+        for n in range(SPLIT_BLOCKS, BLOCKS):
+            for half in range(HALVES):
+                product(n, half)
+            place(n, whole)
+            store(n)

@@ -33,39 +33,39 @@ def tile_list_fibre_equaliser_backward_kernel(
     nc = tc.nc
     with ExitStack() as ctx:
         keep = ctx.enter_context(tc.tile_pool(name="keep", bufs=1))
-        rows = ctx.enter_context(tc.tile_pool(name="rows", bufs=9))
         ring = ctx.enter_context(tc.tile_pool(name="ring", bufs=3))
         psum = ctx.enter_context(tc.psum_pool(name="psum", bufs=4))
 
         idx = keep.tile([P, S // PER_COLUMN], U16, name="idx")
         idx2 = keep.tile([P, S // PER_COLUMN], U16, name="idx2")
-        tab_w = keep.tile([P, T], I32, name="tab_w")
+        tab_w = keep.tile([P, T], I32, name="tab_w", tag="turn")
         tab_s = keep.tile([P, T], U8, name="tab_s")
         v_w = keep.tile([P, S], U32, name="v_w", align_bytes=64)
         v_s = keep.tile([P, S], U8, name="v_s", align_bytes=64)
         w1_w = keep.tile([P, PASSES, N], I32, name="w1_w", align_bytes=64)
         w1_s = keep.tile([P, N], U8, name="w1_s", align_bytes=64)
         wgo_sb = keep.tile([P, S], F32, name="wgo_sb")
-        frames = [keep.tile([P, T2], F32, name="frame%d" % f) for f in range(2)]
+        frames = [keep.tile([P, T2], F32, name="frame0")]
 
         def listed(tile, cols):
             return tile[:, cols.start // PER_COLUMN : cols.stop // PER_COLUMN]
 
-        nc.vector.memset(tab_s[:].bitcast(I32), 0)
-        nc.vector.memset(w1_s[:].bitcast(I32), 0)
-        for frame in frames:
-            nc.vector.memset(frame[:], 0.0)
+        nc.gpsimd.memset(tab_s[:].bitcast(I32), 0)
+        nc.gpsimd.memset(w1_s[:].bitcast(I32), 0)
+        nc.vector.memset(frames[0][:], 0.0)
 
-        s_rows = sT.rearrange("(a p t) c -> a t p c", p=P, t=PACK)
+        s_rows = sT.rearrange("(a p t) c -> a p t c", p=P, t=PACK)
         s_sb = {}
         w2_raw = {}
 
-        def load_s(a, t):
-            s_sb[a, t] = rows.tile([P, T], F32, name="s_sb", tag="row")
-            nc.sync.dma_start(s_sb[a, t][:], s_rows[a, t])
+        def load_s(a, first, count, tag):
+            tile = keep.tile([P, count, T], F32, name="s_sb", tag=tag)
+            nc.sync.dma_start(tile[:], s_rows[a][:, first : first + count, :])
+            for t in range(count):
+                s_sb[a, first + t] = tile[:, t, :]
 
         def load_w2(a):
-            w2_raw[a] = ring.tile([P, PACK, PASS], F32, name="w2_raw")
+            w2_raw[a] = keep.tile([P, PACK, PASS], F32, name="w2_raw", tag="s_last" if a == 0 else "w2_raw%d" % a)
             nc.sync.dma_start(
                 w2_raw[a][:], w2[:, a * PASS : (a + 1) * PASS].rearrange("(p j) c -> p j c", j=PACK)
             )
@@ -73,51 +73,46 @@ def tile_list_fibre_equaliser_backward_kernel(
         nc.sync.dma_start(idx[:], offs)
         nc.sync.dma_start(tab_w[:], tab_words[0].rearrange("p t i -> p (t i)").bitcast(I32))
         for q in range(4):
-            nc.scalar.dma_start(
+            nc.sync.dma_start(
                 tab_s[32 * q : 32 * q + 4, :].bitcast(I32), tab_scales[0, 4 * q : 4 * q + 4, :].bitcast(I32)
             )
-        for a in range(PASSES):
-            load_s(a, 0)
-            load_w2(a)
-            for t in range(1, PACK):
-                load_s(a, t)
-        for q in range(4):
-            nc.sync.dma_start(
-                w1_s[32 * q : 32 * q + 4 * PASSES, :].bitcast(I32),
-                w1_scales[:, 4 * q : 4 * q + 4, :].bitcast(I32),
-            )
-        nc.sync.dma_start(w1_w[:], w1_words.rearrange("a p n i -> p a (n i)").bitcast(I32))
-        nc.sync.dma_start(idx2[:], offs2)
-        nc.sync.dma_start(wgo_sb[:], wgo)
-
-        last_frame = rows.tile([P, T2], F32, name="last_frame", tag="row")
-        nc.gpsimd.memset(last_frame[:], 0.0)
-        frames.append(last_frame)
+        load_w2(0)
+        last = PASSES - 1
+        pairs = [(a, t) for a in range(last) for t in range(0, PACK, 2)]
+        for i, (a, t) in enumerate(pairs):
+            if i == 0:
+                load_s(a, t, 1, "frame1")
+                load_s(a, t + 1, 1, "frame2")
+            else:
+                load_s(a, t, 2, "s_pair%d" % i)
+            if 0 < i < PASSES:
+                load_w2(i)
 
         w2_w, w2_s, h_w, h_s, h_rows, h_words = {}, {}, {}, {}, {}, {}
         w2_grouped, squares = {}, {}
 
         def round_w2(a):
             w2_grouped[a] = ring.tile([P, PASS * PACK], BF16, name="w2_grouped", align_bytes=64, tag="grouped")
-            nc.scalar.copy(
-                w2_grouped[a][:].rearrange("p (t m j) -> p m j t", t=PACK, j=PACK),
-                w2_raw[a][:].rearrange("p j (m t) -> p m j t", t=PACK),
-            )
+            dst = w2_grouped[a][:].rearrange("p (t m j) -> p m j t", t=PACK, j=PACK)
+            src = w2_raw[a][:].rearrange("p j (m t) -> p m j t", t=PACK)
+            nc.scalar.copy(dst, src)
 
         def quantize_w2(a):
             w2_w[a] = keep.tile([P, PASS], U32, name="w2_w%d" % a, align_bytes=64)
             w2_s[a] = keep.tile([P, PASS], U8, name="w2_s%d" % a, align_bytes=64)
             nc.vector.quantize_mx(out=w2_w[a][:].bitcast(E4M3), scales=w2_s[a][:], in_=w2_grouped[a][:])
 
-        def gather_s(a, t, cols):
-            width = cols.stop - cols.start
-            picked = ring.tile([P, width], F32, name="picked", tag="picked")
-            nc.vector.tensor_copy(picked[:], s_sb[a, t][:].indirect(listed(idx, cols)))
-            square = ring.tile([P, width], F32, name="square", tag="square")
-            nc.scalar.activation(square[:], picked[:], ACT.Square)
+        def gather_s(a, t, cols, picked, square):
+            nc.vector.tensor_copy(picked, s_sb[a, t].indirect(listed(idx, cols)))
+            nc.scalar.activation(square, picked, ACT.Square)
             for half in range(cols.start // HALF, cols.stop // HALF):
                 lo = half * HALF - cols.start
                 squares[a, t, half] = square[:, lo : lo + HALF]
+
+        def gather_whole(a, t):
+            picked = ring.tile([P, S], F32, name="picked")
+            square = ring.tile([P, S], F32, name="square")
+            gather_s(a, t, slice(0, S), picked[:], square[:])
 
         def derivative(a, t, half):
             cols = slice(half * HALF, (half + 1) * HALF)
@@ -132,11 +127,21 @@ def tile_list_fibre_equaliser_backward_kernel(
                 start=True,
                 stop=True,
             )
-            if t == 0:
+            if t == 0 and (a, half) == (last, 1):
+                h_rows[a, half] = keep.tile([P, PACK, HALF], BF16, name="last_rows")
+            elif t == 0 and (a, half) == (last, 0):
+                h_rows[a, half] = keep.tile([P, PACK, HALF], BF16, name="h_rows", tag="rows%d" % a, align_bytes=64)
+            elif t == 0:
                 h_rows[a, half] = ring.tile([P, PACK, HALF], BF16, name="h_rows")
-            nc.vector.scalar_tensor_tensor(
-                h_rows[a, half][:, t, :], squares[a, t, half], 1.0, d[:], ALU.subtract, ALU.mult
-            )
+            if half == 1 and a < last:
+                d_sb = ring.tile([P, HALF], F32, name="d_sb", bufs=2)
+                nc.scalar.copy(d_sb[:], d[:])
+                nc.gpsimd.tensor_scalar(squares[a, t, half], squares[a, t, half], 1.0, -1.0, ALU.mult, ALU.add)
+                nc.gpsimd.tensor_tensor(h_rows[a, half][:, t, :], squares[a, t, half], d_sb[:], ALU.mult)
+            else:
+                nc.vector.scalar_tensor_tensor(
+                    h_rows[a, half][:, t, :], squares[a, t, half], 1.0, d[:], ALU.subtract, ALU.mult
+                )
 
         def interleave_h(a, half):
             h_words[a, half] = ring.tile([P, HALF * PACK], BF16, name="h_words", align_bytes=64, tag="grouped")
@@ -146,7 +151,14 @@ def tile_list_fibre_equaliser_backward_kernel(
             )
 
         def quantize_h(a, half):
-            h_w[a, half] = keep.tile([P, HALF], U32, name="h_w%d%d" % (a, half), align_bytes=64)
+            tag = "h_w%d%d" % (a, half)
+            if (a, half) == (last - 1, 0):
+                tag = "first_picked0"
+            if (a, half) == (last - 2, 1):
+                tag = "first_picked1"
+            if (a, half) == (last - 1, 1):
+                tag = "rows%d" % last
+            h_w[a, half] = keep.tile([P, HALF], U32, name="h_w", tag=tag, align_bytes=64)
             h_s[a, half] = keep.tile([P, HALF], U8, name="h_s%d%d" % (a, half), align_bytes=64)
             nc.vector.quantize_mx(
                 out=h_w[a, half][:].bitcast(E4M3), scales=h_s[a, half][:], in_=h_words[a, half][:]
@@ -167,8 +179,10 @@ def tile_list_fibre_equaliser_backward_kernel(
                     start=(a == 0),
                     stop=(a == PASSES - 1),
                 )
-            if half == 0:
-                y_sb[n] = ring.tile([P, S], F32, name="y_sb")
+            if half == 0 and n < SPLIT_BLOCKS:
+                y_sb[n] = keep.tile([P, S], F32, name="y_sb", tag=("turn", "last_rows")[n])
+            elif half == 0:
+                y_sb[n] = ring.tile([P, S], F32, name="y_sb", tag="picked")
             nc.scalar.activation(y_sb[n][:, half * HALF : (half + 1) * HALF], y[:], ACT.Copy, scale=-1.0)
 
         def place(n, cols):
@@ -184,48 +198,61 @@ def tile_list_fibre_equaliser_backward_kernel(
         nc.vector.tensor_copy(v_s[:], tab_s[:].indirect(idx[:]))
         nc.vector.tensor_copy(v_w[:], tab_w[:].bitcast(U32).indirect(idx[:]))
         round_w2(0)
-        gather_s(0, 0, whole)
-        quantize_w2(0)
-
-        last = PASSES - 1
-        for i in range(1, last * PACK + 1):
-            a, t = divmod(i, PACK)
-            pa, pt = divmod(i - 1, PACK)
-            if t == 1:
-                round_w2(a + 1)
-            if a < last:
-                gather_s(a, t, whole)
-            else:
-                gather_s(a, t, halves[0])
-            if t == 2:
-                quantize_w2(a + 1)
+        load_s(last, 0, PACK, "s_last")
+        for q in range(4):
+            nc.sync.dma_start(
+                w1_s[32 * q : 32 * q + 4 * PASSES, :].bitcast(I32),
+                w1_scales[:, 4 * q : 4 * q + 4, :].bitcast(I32),
+            )
+        nc.sync.dma_start(w1_w[:], w1_words.rearrange("a p n i -> p a (n i)").bitcast(I32))
+        nc.sync.dma_start(idx2[:], offs2)
+        nc.sync.dma_start(wgo_sb[:], wgo)
+        for i, (a, t) in enumerate(pairs):
+            gather_whole(a, t)
+            gather_whole(a, t + 1)
+            if i == 0:
+                for f in (1, 2):
+                    frames.append(keep.tile([P, T2], F32, name="frame", tag="frame%d" % f))
+                    nc.gpsimd.memset(frames[f][:], 0.0)
+            if t == 0:
+                quantize_w2(a)
                 if a > 0:
                     for half in range(HALVES):
-                        quantize_h(a - 1, half)
-            for half in range(HALVES):
-                derivative(pa, pt, half)
-            if pt == PACK - 1:
+                        interleave_h(a - 1, half)
+            elif a > 0:
+                quantize_h(a - 1, 0)
+            for u in (t, t + 1):
                 for half in range(HALVES):
-                    interleave_h(pa, half)
+                    derivative(a, u, half)
+            if t == 0:
+                round_w2(a + 1)
 
-        for t in range(1, PACK):
-            gather_s(last, t, halves[0])
-            derivative(last, t - 1, 0)
-            if t == 2:
-                for half in range(HALVES):
-                    quantize_h(last - 1, half)
-        gather_s(last, 0, halves[1])
-        derivative(last, PACK - 1, 0)
+        quantize_w2(last)
+        for half in range(HALVES):
+            interleave_h(last - 1, half)
+
+        first_squares = keep.tile([P, PACK, HALF], F32, name="first_squares", tag="turn")
+        for t in range(PACK):
+            picked = keep.tile([P, HALF], F32, name="first_picked", tag="first_picked%d" % t, align_bytes=64)
+            gather_s(last, t, halves[0], picked[:], first_squares[:, t, :])
+        quantize_h(last - 2, 1)
+        quantize_h(last - 1, 0)
+        for t in range(PACK):
+            derivative(last, t, 0)
         interleave_h(last, 0)
-        for t in range(1, PACK):
-            gather_s(last, t, halves[1])
-            derivative(last, t - 1, 1)
-            if t == 2:
+        second_picked = keep.tile([P, PACK, HALF], F32, name="second_picked", tag="turn")
+        for t in range(PACK):
+            square = ring.tile([P, HALF], F32, name="square")
+            gather_s(last, t, halves[1], second_picked[:, t, :], square[:])
+            if t == PACK - 2:
                 quantize_h(last, 0)
-                for n in range(SPLIT_BLOCKS):
-                    product(n, 0)
+                quantize_h(last - 1, 1)
+            if t > 0:
+                derivative(last, t - 1, 1)
         derivative(last, PACK - 1, 1)
+        product(0, 0)
         interleave_h(last, 1)
+        product(1, 0)
         place(0, halves[0])
         quantize_h(last, 1)
         for n in range(SPLIT_BLOCKS):

@@ -25,6 +25,7 @@ HALVES = S // HALF
 BLOCKS = N // P
 PER_COLUMN = 16
 SPLIT_BLOCKS = 2
+SPARE = ("tab_w", "w2_raw1", "w2_raw2", "w2_w0")
 
 
 def tile_list_fibre_equaliser_backward_kernel(
@@ -34,38 +35,40 @@ def tile_list_fibre_equaliser_backward_kernel(
     with ExitStack() as ctx:
         keep = ctx.enter_context(tc.tile_pool(name="keep", bufs=1))
         ring = ctx.enter_context(tc.tile_pool(name="ring", bufs=3))
-        psum = ctx.enter_context(tc.psum_pool(name="psum", bufs=4))
+        psum = ctx.enter_context(tc.psum_pool(name="psum", bufs=8))
 
         idx = keep.tile([P, S // PER_COLUMN], U16, name="idx")
         idx2 = keep.tile([P, S // PER_COLUMN], U16, name="idx2")
-        tab_w = keep.tile([P, T], I32, name="tab_w", tag="turn")
+        tab_w = keep.tile([P, T], I32, name="tab_w", tag="tab_w", align_bytes=64)
         tab_s = keep.tile([P, T], U8, name="tab_s")
         v_w = keep.tile([P, S], U32, name="v_w", align_bytes=64)
         v_s = keep.tile([P, S], U8, name="v_s", align_bytes=64)
         w1_w = keep.tile([P, PASSES, N], I32, name="w1_w", align_bytes=64)
         w1_s = keep.tile([P, N], U8, name="w1_s", align_bytes=64)
         wgo_sb = keep.tile([P, S], F32, name="wgo_sb")
-        frames = [keep.tile([P, T2], F32, name="frame0")]
+        frames = [keep.tile([P, T2], F32, name="frame%d" % f) for f in range(3)]
 
         def listed(tile, cols):
             return tile[:, cols.start // PER_COLUMN : cols.stop // PER_COLUMN]
 
         nc.gpsimd.memset(tab_s[:].bitcast(I32), 0)
         nc.gpsimd.memset(w1_s[:].bitcast(I32), 0)
-        nc.vector.memset(frames[0][:], 0.0)
+        for frame in frames:
+            nc.gpsimd.memset(frame[:], 0.0)
 
         s_rows = sT.rearrange("(a p t) c -> a p t c", p=P, t=PACK)
         s_sb = {}
         w2_raw = {}
 
-        def load_s(a, first, count, tag):
-            tile = keep.tile([P, count, T], F32, name="s_sb", tag=tag)
-            nc.sync.dma_start(tile[:], s_rows[a][:, first : first + count, :])
-            for t in range(count):
-                s_sb[a, first + t] = tile[:, t, :]
+        def load_s(first, count, tag):
+            tile = keep.tile([P, count, T], F32, name="s_sb", tag=tag, align_bytes=64)
+            a, t = divmod(first, PACK)
+            nc.sync.dma_start(tile[:], s_rows[a][:, t : t + count, :])
+            for u in range(count):
+                s_sb[first + u] = tile[:, u, :]
 
         def load_w2(a):
-            w2_raw[a] = keep.tile([P, PACK, PASS], F32, name="w2_raw", tag="s_last" if a == 0 else "w2_raw%d" % a)
+            w2_raw[a] = keep.tile([P, PACK, PASS], F32, name="w2_raw", tag="w2_raw%d" % a, align_bytes=64)
             nc.sync.dma_start(
                 w2_raw[a][:], w2[:, a * PASS : (a + 1) * PASS].rearrange("(p j) c -> p j c", j=PACK)
             )
@@ -76,48 +79,47 @@ def tile_list_fibre_equaliser_backward_kernel(
             nc.sync.dma_start(
                 tab_s[32 * q : 32 * q + 4, :].bitcast(I32), tab_scales[0, 4 * q : 4 * q + 4, :].bitcast(I32)
             )
-        load_w2(0)
         last = PASSES - 1
-        pairs = [(a, t) for a in range(last) for t in range(0, PACK, 2)]
-        for i, (a, t) in enumerate(pairs):
-            if i == 0:
-                load_s(a, t, 1, "frame1")
-                load_s(a, t + 1, 1, "frame2")
-            else:
-                load_s(a, t, 2, "s_pair%d" % i)
-            if 0 < i < PASSES:
-                load_w2(i)
+        for pair in range(2 * last):
+            load_s(2 * pair, 2, "pair%d" % pair)
+            if pair < PASSES:
+                load_w2(pair)
+        load_s(last * PACK, PACK, "s_last")
+        for q in range(4):
+            nc.sync.dma_start(
+                w1_s[32 * q : 32 * q + 4 * PASSES, :].bitcast(I32),
+                w1_scales[:, 4 * q : 4 * q + 4, :].bitcast(I32),
+            )
+        nc.sync.dma_start(w1_w[:], w1_words.rearrange("a p n i -> p a (n i)").bitcast(I32))
+        nc.sync.dma_start(idx2[:], offs2)
+        nc.sync.dma_start(wgo_sb[:], wgo)
 
         w2_w, w2_s, h_w, h_s, h_rows, h_words = {}, {}, {}, {}, {}, {}
-        w2_grouped, squares = {}, {}
+        w2_grouped, squares, spare_d = {}, {}, {}
 
         def round_w2(a):
-            w2_grouped[a] = ring.tile([P, PASS * PACK], BF16, name="w2_grouped", align_bytes=64, tag="grouped")
-            dst = w2_grouped[a][:].rearrange("p (t m j) -> p m j t", t=PACK, j=PACK)
-            src = w2_raw[a][:].rearrange("p j (m t) -> p m j t", t=PACK)
-            nc.scalar.copy(dst, src)
+            w2_grouped[a] = keep.tile([P, PASS * PACK], BF16, name="w2_grouped", align_bytes=64)
+            nc.scalar.copy(
+                w2_grouped[a][:].rearrange("p (t m j) -> p m j t", t=PACK, j=PACK),
+                w2_raw[a][:].rearrange("p j (m t) -> p m j t", t=PACK),
+            )
 
-        def quantize_w2(a):
-            w2_w[a] = keep.tile([P, PASS], U32, name="w2_w%d" % a, align_bytes=64)
+        def quantize_w2(a, codes):
+            w2_w[a] = codes
             w2_s[a] = keep.tile([P, PASS], U8, name="w2_s%d" % a, align_bytes=64)
-            nc.vector.quantize_mx(out=w2_w[a][:].bitcast(E4M3), scales=w2_s[a][:], in_=w2_grouped[a][:])
+            nc.vector.quantize_mx(out=codes.bitcast(E4M3), scales=w2_s[a][:], in_=w2_grouped[a][:])
 
         def gather_s(a, t, cols, picked, square):
-            nc.vector.tensor_copy(picked, s_sb[a, t].indirect(listed(idx, cols)))
-            nc.scalar.activation(square, picked, ACT.Square)
+            nc.vector.tensor_copy(picked, s_sb[a * PACK + t].indirect(listed(idx, cols)))
             for half in range(cols.start // HALF, cols.stop // HALF):
                 lo = half * HALF - cols.start
                 squares[a, t, half] = square[:, lo : lo + HALF]
-
-        def gather_whole(a, t):
-            picked = ring.tile([P, S], F32, name="picked")
-            square = ring.tile([P, S], F32, name="square")
-            gather_s(a, t, slice(0, S), picked[:], square[:])
+                nc.scalar.activation(squares[a, t, half], picked[:, lo : lo + HALF], ACT.Square)
 
         def derivative(a, t, half):
             cols = slice(half * HALF, (half + 1) * HALF)
             rcols = slice(t * P, (t + 1) * P)
-            d = psum.tile([P, HALF], F32, name="d")
+            d = psum.tile([P, HALF], F32, name="d", tag="bank")
             nc.tensor.matmul_mx(
                 out=d[:],
                 lhsT=w2_w[a][:, rcols].bitcast(E4M3),
@@ -127,62 +129,52 @@ def tile_list_fibre_equaliser_backward_kernel(
                 start=True,
                 stop=True,
             )
-            if t == 0 and (a, half) == (last, 1):
-                h_rows[a, half] = keep.tile([P, PACK, HALF], BF16, name="last_rows")
-            elif t == 0 and (a, half) == (last, 0):
-                h_rows[a, half] = keep.tile([P, PACK, HALF], BF16, name="h_rows", tag="rows%d" % a, align_bytes=64)
-            elif t == 0:
-                h_rows[a, half] = ring.tile([P, PACK, HALF], BF16, name="h_rows")
-            if half == 1 and a < last:
-                d_sb = ring.tile([P, HALF], F32, name="d_sb", bufs=2)
-                nc.scalar.copy(d_sb[:], d[:])
+            if t == 0:
+                h_rows[a, half] = keep.tile(
+                    [P, PACK, HALF], BF16, name="h_rows", tag="h_rows%d%d" % (a, half), align_bytes=64
+                )
+            if half == 1 and a * PACK + t < 9:
+                d_sb = spare_d[a, t]
+                nc.scalar.copy(d_sb, d[:])
                 nc.gpsimd.tensor_scalar(squares[a, t, half], squares[a, t, half], 1.0, -1.0, ALU.mult, ALU.add)
-                nc.gpsimd.tensor_tensor(h_rows[a, half][:, t, :], squares[a, t, half], d_sb[:], ALU.mult)
+                nc.gpsimd.tensor_tensor(h_rows[a, half][:, t, :], squares[a, t, half], d_sb, ALU.mult)
             else:
                 nc.vector.scalar_tensor_tensor(
                     h_rows[a, half][:, t, :], squares[a, t, half], 1.0, d[:], ALU.subtract, ALU.mult
                 )
 
         def interleave_h(a, half):
-            h_words[a, half] = ring.tile([P, HALF * PACK], BF16, name="h_words", align_bytes=64, tag="grouped")
+            h_words[a, half] = ring.tile([P, HALF * PACK], BF16, name="h_words", align_bytes=64, bufs=2)
             nc.scalar.copy(
                 h_words[a, half][:].rearrange("p (c i t) -> p c t i", i=4, t=PACK),
                 h_rows[a, half][:].rearrange("p t (c i) -> p c t i", i=4),
             )
 
-        def quantize_h(a, half):
-            tag = "h_w%d%d" % (a, half)
-            if (a, half) == (last - 1, 0):
-                tag = "first_picked0"
-            if (a, half) == (last - 2, 1):
-                tag = "first_picked1"
-            if (a, half) == (last - 1, 1):
-                tag = "rows%d" % last
-            h_w[a, half] = keep.tile([P, HALF], U32, name="h_w", tag=tag, align_bytes=64)
+        def quantize_h(a, half, codes):
+            h_w[a, half] = codes
             h_s[a, half] = keep.tile([P, HALF], U8, name="h_s%d%d" % (a, half), align_bytes=64)
-            nc.vector.quantize_mx(
-                out=h_w[a, half][:].bitcast(E4M3), scales=h_s[a, half][:], in_=h_words[a, half][:]
-            )
+            nc.vector.quantize_mx(out=codes.bitcast(E4M3), scales=h_s[a, half][:], in_=h_words[a, half][:])
+
+        def words(tag, width):
+            return keep.tile([P, width], U32, name="codes", tag=tag, align_bytes=64)
 
         y_sb = {}
 
         def product(n, half):
             ncols = slice(n * P, (n + 1) * P)
-            y = psum.tile([P, HALF], F32, name="y")
+            y = psum.tile([P, HALF], F32, name="y", tag="bank")
             for a in range(PASSES):
                 nc.tensor.matmul_mx(
                     out=y[:],
                     lhsT=w1_w[:, a, ncols].bitcast(E4M3),
                     lhsT_scale=w1_s[4 * a :, ncols],
-                    rhs=h_w[a, half][:].bitcast(E4M3),
+                    rhs=h_w[a, half].bitcast(E4M3),
                     rhs_scale=h_s[a, half][:],
                     start=(a == 0),
                     stop=(a == PASSES - 1),
                 )
-            if half == 0 and n < SPLIT_BLOCKS:
-                y_sb[n] = keep.tile([P, S], F32, name="y_sb", tag=("turn", "last_rows")[n])
-            elif half == 0:
-                y_sb[n] = ring.tile([P, S], F32, name="y_sb", tag="picked")
+            if half == 0:
+                y_sb[n] = keep.tile([P, S], F32, name="y_sb", tag=("pair0", "h_rows21", "pair1")[n % 3], align_bytes=64)
             nc.scalar.activation(y_sb[n][:, half * HALF : (half + 1) * HALF], y[:], ACT.Copy, scale=-1.0)
 
         def place(n, cols):
@@ -198,63 +190,52 @@ def tile_list_fibre_equaliser_backward_kernel(
         nc.vector.tensor_copy(v_s[:], tab_s[:].indirect(idx[:]))
         nc.vector.tensor_copy(v_w[:], tab_w[:].bitcast(U32).indirect(idx[:]))
         round_w2(0)
-        load_s(last, 0, PACK, "s_last")
-        for q in range(4):
-            nc.sync.dma_start(
-                w1_s[32 * q : 32 * q + 4 * PASSES, :].bitcast(I32),
-                w1_scales[:, 4 * q : 4 * q + 4, :].bitcast(I32),
-            )
-        nc.sync.dma_start(w1_w[:], w1_words.rearrange("a p n i -> p a (n i)").bitcast(I32))
-        nc.sync.dma_start(idx2[:], offs2)
-        nc.sync.dma_start(wgo_sb[:], wgo)
-        for i, (a, t) in enumerate(pairs):
-            gather_whole(a, t)
-            gather_whole(a, t + 1)
-            if i == 0:
-                for f in (1, 2):
-                    frames.append(keep.tile([P, T2], F32, name="frame", tag="frame%d" % f))
-                    nc.gpsimd.memset(frames[f][:], 0.0)
-            if t == 0:
-                quantize_w2(a)
-                if a > 0:
-                    for half in range(HALVES):
-                        interleave_h(a - 1, half)
-            elif a > 0:
-                quantize_h(a - 1, 0)
-            for u in (t, t + 1):
+        for pair in range(2 * last):
+            a, t0 = divmod(2 * pair, PACK)
+            both = keep.tile([P, 2, S + HALF], F32, name="work", tag=("w2_raw0", "pair0", "pair1", "w2_raw0")[pair], align_bytes=64)
+            for u in range(2):
+                spare_d[a, t0 + u] = both[:, u, S:]
+                picked = ring.tile([P, S], F32, name="picked", bufs=2)
+                gather_s(a, t0 + u, whole, picked[:], both[:, u, :S])
+            if pair == 0:
+                quantize_w2(0, words("w2_w0", PASS)[:])
+            if pair >= 2:
+                codes = words("pair%d" % pair, PASS + HALF)
+                quantize_w2(pair - 1, codes[:, :PASS])
+                quantize_h(0, pair - 2, codes[:, PASS:])
+            for u in range(2):
                 for half in range(HALVES):
-                    derivative(a, u, half)
-            if t == 0:
-                round_w2(a + 1)
+                    derivative(a, t0 + u, half)
+            if pair in (1, 2):
+                interleave_h(0, pair - 1)
+                round_w2(pair)
+        interleave_h(last - 1, 0)
 
-        quantize_w2(last)
-        for half in range(HALVES):
-            interleave_h(last - 1, half)
-
-        first_squares = keep.tile([P, PACK, HALF], F32, name="first_squares", tag="turn")
+        first_squares = keep.tile([P, PACK, HALF], F32, name="first_squares", tag="pair0", align_bytes=64)
         for t in range(PACK):
-            picked = keep.tile([P, HALF], F32, name="first_picked", tag="first_picked%d" % t, align_bytes=64)
+            picked = keep.tile([P, HALF], F32, name="first_picked", tag=SPARE[t], align_bytes=64)
             gather_s(last, t, halves[0], picked[:], first_squares[:, t, :])
-        quantize_h(last - 2, 1)
-        quantize_h(last - 1, 0)
+        quantize_h(last - 1, 0, words(SPARE[0], HALF)[:])
         for t in range(PACK):
             derivative(last, t, 0)
         interleave_h(last, 0)
-        second_picked = keep.tile([P, PACK, HALF], F32, name="second_picked", tag="turn")
+        interleave_h(last - 1, 1)
+        second_picked = keep.tile([P, PACK, HALF], F32, name="second_picked", tag="pair0", align_bytes=64)
+        second_squares = keep.tile([P, PACK, HALF], F32, name="second_squares", tag="pair1", align_bytes=64)
+        last_d = keep.tile([P, 1, HALF], F32, name="last_d", tag="w2_raw0", align_bytes=64)
+        for t in range(1):
+            spare_d[last, t] = last_d[:, t, :]
         for t in range(PACK):
-            square = ring.tile([P, HALF], F32, name="square")
-            gather_s(last, t, halves[1], second_picked[:, t, :], square[:])
-            if t == PACK - 2:
-                quantize_h(last, 0)
-                quantize_h(last - 1, 1)
-            if t > 0:
-                derivative(last, t - 1, 1)
-        derivative(last, PACK - 1, 1)
+            gather_s(last, t, halves[1], second_picked[:, t, :], second_squares[:, t, :])
+        quantize_h(last, 0, words(SPARE[1], HALF)[:])
+        quantize_h(last - 1, 1, words("h_rows20", HALF)[:])
+        for t in range(PACK):
+            derivative(last, t, 1)
         product(0, 0)
         interleave_h(last, 1)
         product(1, 0)
         place(0, halves[0])
-        quantize_h(last, 1)
+        quantize_h(last, 1, words(SPARE[2], HALF)[:])
         for n in range(SPLIT_BLOCKS):
             product(n, 1)
         for n in range(1, SPLIT_BLOCKS):

@@ -20,12 +20,32 @@ P = 128
 PACK = 4
 PASS = P * PACK
 PASSES = H // PASS
+SLICES = PASSES * PACK
 HALF = 512
 HALVES = S // HALF
 BLOCKS = N // P
 PER_COLUMN = 16
-SPLIT_BLOCKS = 2
-SPARE = ("tab_w", "w2_raw1", "w2_raw2", "w2_w0")
+SPLIT_BLOCKS = 4
+FRAMES = 4
+KB = 1024
+LAG = 1
+
+AT_S = 0
+AT_W2 = 96
+AT_TAB = 120
+AT_FRAME = 128
+AT_W1 = 160
+AT_WGO = 172
+AT_TAB_S = 176
+AT_V_W = 178
+AT_V_S = 182
+AT_W1_S = 183
+AT_PICKED = 184
+AT_D = 208
+AT_W2_BF = 224
+AT_W2_CODES = 228
+AT_SQUARE = 232
+D_PLACES = [AT_D + 2 * i for i in range(8)] + [AT_TAB + 2 * i for i in range(4)] + [AT_W2 + 4, AT_W2 + 6, AT_W2 + 12]
 
 
 def tile_list_fibre_equaliser_backward_kernel(
@@ -33,20 +53,39 @@ def tile_list_fibre_equaliser_backward_kernel(
 ):
     nc = tc.nc
     with ExitStack() as ctx:
-        keep = ctx.enter_context(tc.tile_pool(name="keep", bufs=1))
-        ring = ctx.enter_context(tc.tile_pool(name="ring", bufs=3))
+        lists = ctx.enter_context(tc.tile_pool(name="lists", bufs=1))
+        arena = ctx.enter_context(tc.tile_pool(name="arena", bufs=1))
         psum = ctx.enter_context(tc.psum_pool(name="psum", bufs=8))
 
-        idx = keep.tile([P, S // PER_COLUMN], U16, name="idx")
-        idx2 = keep.tile([P, S // PER_COLUMN], U16, name="idx2")
-        tab_w = keep.tile([P, T], I32, name="tab_w", tag="tab_w", align_bytes=64)
-        tab_s = keep.tile([P, T], U8, name="tab_s")
-        v_w = keep.tile([P, S], U32, name="v_w", align_bytes=64)
-        v_s = keep.tile([P, S], U8, name="v_s", align_bytes=64)
-        w1_w = keep.tile([P, PASSES, N], I32, name="w1_w", align_bytes=64)
-        w1_s = keep.tile([P, N], U8, name="w1_s", align_bytes=64)
-        wgo_sb = keep.tile([P, S], F32, name="wgo_sb")
-        frames = [keep.tile([P, T2], F32, name="frame%d" % f) for f in range(3)]
+        def place_tile(name, shape, dtype, kib):
+            return arena.tile(shape, dtype, name=name, tag=name, align_bytes=64, offset=int(kib * KB))
+
+        def at_s(k):
+            return AT_S + 8 * k
+
+        def at_w2(a):
+            return AT_W2 + 8 * a
+
+        def at_rows(a, half):
+            return at_w2(0) if (a, half) == (0, 0) else at_s(PACK * a + 1) + 4 * half
+
+        def at_picked(k):
+            if k < 6:
+                return AT_PICKED + 4 * k
+            return at_s(0) + 4 * (k - 6) if k < 8 else at_s(2) + 4 * (k - 8)
+
+        idx = lists.tile([P, S // PER_COLUMN], U16, name="idx")
+        idx2 = lists.tile([P, S // PER_COLUMN], U16, name="idx2")
+        tab_w = place_tile("tab_w", [P, T], I32, AT_TAB)
+        tab_s = place_tile("tab_s", [P, T], U8, AT_TAB_S)
+        v_w = place_tile("v_w", [P, S], U32, AT_V_W)
+        v_s = place_tile("v_s", [P, S], U8, AT_V_S)
+        first_cols = SPLIT_BLOCKS * P
+        w1_first = place_tile("w1_first", [P, PASSES, first_cols], I32, AT_W1)
+        w1_rest = place_tile("w1_rest", [P, PASSES, N - first_cols], I32, AT_W1 + PASSES * first_cols * 4 / KB)
+        w1_s = place_tile("w1_s", [P, N], U8, AT_W1_S)
+        wgo_sb = place_tile("wgo_sb", [P, S], F32, AT_WGO)
+        frames = [place_tile("frame%d" % f, [P, T2], F32, AT_FRAME + 8 * f) for f in range(FRAMES)]
 
         def listed(tile, cols):
             return tile[:, cols.start // PER_COLUMN : cols.stop // PER_COLUMN]
@@ -57,18 +96,23 @@ def tile_list_fibre_equaliser_backward_kernel(
             nc.gpsimd.memset(frame[:], 0.0)
 
         s_rows = sT.rearrange("(a p t) c -> a p t c", p=P, t=PACK)
-        s_sb = {}
-        w2_raw = {}
+        w1_rows = w1_words.rearrange("a p n i -> p a (n i)").bitcast(I32)
+        s_sb, w2_raw = {}, {}
 
-        def load_s(first, count, tag):
-            tile = keep.tile([P, count, T], F32, name="s_sb", tag=tag, align_bytes=64)
-            a, t = divmod(first, PACK)
-            nc.sync.dma_start(tile[:], s_rows[a][:, t : t + count, :])
-            for u in range(count):
-                s_sb[first + u] = tile[:, u, :]
+        def load_s(k):
+            a, t = divmod(k, PACK)
+            s_sb[k] = place_tile("s%d" % k, [P, T], F32, at_s(k))[:]
+            nc.sync.dma_start(s_sb[k], s_rows[a][:, t, :])
+
+        def load_s_pair(k):
+            a, t = divmod(k, PACK)
+            both = place_tile("s%d" % k, [P, 2, T], F32, at_s(k))
+            nc.sync.dma_start(both[:], s_rows[a][:, t : t + 2, :])
+            for u in range(2):
+                s_sb[k + u] = both[:, u, :]
 
         def load_w2(a):
-            w2_raw[a] = keep.tile([P, PACK, PASS], F32, name="w2_raw", tag="w2_raw%d" % a, align_bytes=64)
+            w2_raw[a] = place_tile("w2_raw%d" % a, [P, PACK, PASS], F32, at_w2(a))
             nc.sync.dma_start(
                 w2_raw[a][:], w2[:, a * PASS : (a + 1) * PASS].rearrange("(p j) c -> p j c", j=PACK)
             )
@@ -79,168 +123,174 @@ def tile_list_fibre_equaliser_backward_kernel(
             nc.sync.dma_start(
                 tab_s[32 * q : 32 * q + 4, :].bitcast(I32), tab_scales[0, 4 * q : 4 * q + 4, :].bitcast(I32)
             )
-        last = PASSES - 1
-        for pair in range(2 * last):
-            load_s(2 * pair, 2, "pair%d" % pair)
-            if pair < PASSES:
-                load_w2(pair)
-        load_s(last * PACK, PACK, "s_last")
-        for q in range(4):
-            nc.sync.dma_start(
-                w1_s[32 * q : 32 * q + 4 * PASSES, :].bitcast(I32),
-                w1_scales[:, 4 * q : 4 * q + 4, :].bitcast(I32),
-            )
-        nc.sync.dma_start(w1_w[:], w1_words.rearrange("a p n i -> p a (n i)").bitcast(I32))
-        nc.sync.dma_start(idx2[:], offs2)
+        for k in range(SLICES - 1):
+            if k in (0, 2, 7):
+                load_w2((k + 2) // PACK)
+            if k == SLICES - 2:
+                nc.sync.dma_start(idx2[:], offs2)
+                for q in range(4):
+                    nc.sync.dma_start(
+                        w1_s[32 * q : 32 * q + 4 * PASSES, :].bitcast(I32),
+                        w1_scales[:, 4 * q : 4 * q + 4, :].bitcast(I32),
+                    )
+            if k == SLICES - 2:
+                load_s_pair(k)
+            else:
+                load_s(k)
+        nc.sync.dma_start(w1_first[:], w1_rows[:, :, :first_cols])
         nc.sync.dma_start(wgo_sb[:], wgo)
+        nc.sync.dma_start(w1_rest[:], w1_rows[:, :, first_cols:])
 
-        w2_w, w2_s, h_w, h_s, h_rows, h_words = {}, {}, {}, {}, {}, {}
-        w2_grouped, squares, spare_d = {}, {}, {}
+        w2_bf, w2_w, w2_s, h_rows, h_words, h_w, h_s, squares, y_sb = {}, {}, {}, {}, {}, {}, {}, {}, {}
+        whole = slice(0, S)
+        halves = [slice(h * HALF, (h + 1) * HALF) for h in range(HALVES)]
+        evacuated = []
 
-        def round_w2(a):
-            w2_grouped[a] = keep.tile([P, PASS * PACK], BF16, name="w2_grouped", align_bytes=64)
+        def round_w2(a, kib):
+            w2_bf[a] = place_tile("w2_bf%d" % a, [P, PASS * PACK], BF16, kib)
             nc.scalar.copy(
-                w2_grouped[a][:].rearrange("p (t m j) -> p m j t", t=PACK, j=PACK),
+                w2_bf[a][:].rearrange("p (t m j) -> p m j t", t=PACK, j=PACK),
                 w2_raw[a][:].rearrange("p j (m t) -> p m j t", t=PACK),
             )
 
-        def quantize_w2(a, codes):
-            w2_w[a] = codes
-            w2_s[a] = keep.tile([P, PASS], U8, name="w2_s%d" % a, align_bytes=64)
-            nc.vector.quantize_mx(out=codes.bitcast(E4M3), scales=w2_s[a][:], in_=w2_grouped[a][:])
+        def quantize_w2(a, kib):
+            w2_w[a] = place_tile("w2_w%d" % a, [P, PASS], U32, kib)
+            w2_s[a] = place_tile("w2_s%d" % a, [P, PASS], U8, kib + 2)
+            nc.vector.quantize_mx(out=w2_w[a][:].bitcast(E4M3), scales=w2_s[a][:], in_=w2_bf[a][:])
 
-        def gather_s(a, t, cols, picked, square):
-            nc.vector.tensor_copy(picked, s_sb[a * PACK + t].indirect(listed(idx, cols)))
+        def gather_s(k, cols, picked_kib):
+            picked = place_tile("picked%d_%d" % (k, cols.start), [P, cols.stop - cols.start], F32, picked_kib)
+            nc.vector.tensor_copy(picked[:], s_sb[k].indirect(listed(idx, cols)))
+            return picked
+
+        def square_s(k, cols, picked, kib):
+            square = place_tile("square%d_%d" % (k, cols.start), [P, cols.stop - cols.start], F32, kib)
+            nc.scalar.activation(square[:], picked[:], ACT.Square)
             for half in range(cols.start // HALF, cols.stop // HALF):
                 lo = half * HALF - cols.start
-                squares[a, t, half] = square[:, lo : lo + HALF]
-                nc.scalar.activation(squares[a, t, half], picked[:, lo : lo + HALF], ACT.Square)
+                squares[k, half] = square[:, lo : lo + HALF]
 
-        def derivative(a, t, half):
-            cols = slice(half * HALF, (half + 1) * HALF)
+        def first_product(k, half):
+            a, t = divmod(k, PACK)
             rcols = slice(t * P, (t + 1) * P)
             d = psum.tile([P, HALF], F32, name="d", tag="bank")
             nc.tensor.matmul_mx(
                 out=d[:],
                 lhsT=w2_w[a][:, rcols].bitcast(E4M3),
                 lhsT_scale=w2_s[a][:, rcols],
-                rhs=v_w[:, cols].bitcast(E5M2),
-                rhs_scale=v_s[:, cols],
+                rhs=v_w[:, halves[half]].bitcast(E5M2),
+                rhs_scale=v_s[:, halves[half]],
                 start=True,
                 stop=True,
             )
             if t == 0:
-                h_rows[a, half] = keep.tile(
-                    [P, PACK, HALF], BF16, name="h_rows", tag="h_rows%d%d" % (a, half), align_bytes=64
-                )
-            if half == 1 and a * PACK + t < 9:
-                d_sb = spare_d[a, t]
-                nc.scalar.copy(d_sb, d[:])
-                nc.gpsimd.tensor_scalar(squares[a, t, half], squares[a, t, half], 1.0, -1.0, ALU.mult, ALU.add)
-                nc.gpsimd.tensor_tensor(h_rows[a, half][:, t, :], squares[a, t, half], d_sb, ALU.mult)
-            else:
-                nc.vector.scalar_tensor_tensor(
-                    h_rows[a, half][:, t, :], squares[a, t, half], 1.0, d[:], ALU.subtract, ALU.mult
-                )
+                h_rows[a, half] = place_tile("h_rows%d%d" % (a, half), [P, PACK, HALF], BF16, at_rows(a, half))
+            return d, h_rows[a, half][:, t, :]
 
-        def interleave_h(a, half):
-            h_words[a, half] = ring.tile([P, HALF * PACK], BF16, name="h_words", align_bytes=64, bufs=2)
+        def derivative_vector(k, half):
+            d, h = first_product(k, half)
+            nc.vector.scalar_tensor_tensor(h, squares[k, half], 1.0, d[:], ALU.subtract, ALU.mult)
+
+        def derivative_gpsimd(k, half):
+            d, h = first_product(k, half)
+            d_sb = place_tile("d_sb%d_%d" % (k, half), [P, HALF], F32, D_PLACES[len(evacuated) % len(D_PLACES)])
+            evacuated.append((k, half))
+            nc.scalar.copy(d_sb[:], d[:])
+            nc.gpsimd.tensor_scalar(squares[k, half], squares[k, half], 1.0, -1.0, ALU.mult, ALU.add)
+            nc.gpsimd.tensor_tensor(h, squares[k, half], d_sb[:], ALU.mult)
+
+        def interleave_h(a, half, kib):
+            h_words[a, half] = place_tile("h_words%d%d" % (a, half), [P, HALF * PACK], BF16, kib)
             nc.scalar.copy(
                 h_words[a, half][:].rearrange("p (c i t) -> p c t i", i=4, t=PACK),
                 h_rows[a, half][:].rearrange("p t (c i) -> p c t i", i=4),
             )
 
-        def quantize_h(a, half, codes):
-            h_w[a, half] = codes
-            h_s[a, half] = keep.tile([P, HALF], U8, name="h_s%d%d" % (a, half), align_bytes=64)
-            nc.vector.quantize_mx(out=codes.bitcast(E4M3), scales=h_s[a, half][:], in_=h_words[a, half][:])
-
-        def words(tag, width):
-            return keep.tile([P, width], U32, name="codes", tag=tag, align_bytes=64)
-
-        y_sb = {}
+        def quantize_h(a, half, codes_kib, scales_kib):
+            h_w[a, half] = place_tile("h_w%d%d" % (a, half), [P, HALF], U32, codes_kib)
+            h_s[a, half] = place_tile("h_s%d%d" % (a, half), [P, HALF], U8, scales_kib)
+            nc.vector.quantize_mx(out=h_w[a, half][:].bitcast(E4M3), scales=h_s[a, half][:], in_=h_words[a, half][:])
 
         def product(n, half):
             ncols = slice(n * P, (n + 1) * P)
+            w1_w = w1_first[:, :, ncols] if n < SPLIT_BLOCKS else w1_rest[:, :, n * P - first_cols : (n + 1) * P - first_cols]
             y = psum.tile([P, HALF], F32, name="y", tag="bank")
             for a in range(PASSES):
                 nc.tensor.matmul_mx(
                     out=y[:],
-                    lhsT=w1_w[:, a, ncols].bitcast(E4M3),
+                    lhsT=w1_w[:, a, :].bitcast(E4M3),
                     lhsT_scale=w1_s[4 * a :, ncols],
-                    rhs=h_w[a, half].bitcast(E4M3),
+                    rhs=h_w[a, half][:].bitcast(E4M3),
                     rhs_scale=h_s[a, half][:],
                     start=(a == 0),
                     stop=(a == PASSES - 1),
                 )
             if half == 0:
-                y_sb[n] = keep.tile([P, S], F32, name="y_sb", tag=("pair0", "h_rows21", "pair1")[n % 3], align_bytes=64)
-            nc.scalar.activation(y_sb[n][:, half * HALF : (half + 1) * HALF], y[:], ACT.Copy, scale=-1.0)
+                y_sb[n] = place_tile("y_sb%d" % n, [P, S], F32, AT_PICKED + 4 * (n % FRAMES))
+            if (n, half) == (0, 0):
+                nc.vector.tensor_scalar_mul(y_sb[n][:, halves[half]], y[:], -1.0)
+            else:
+                nc.scalar.activation(y_sb[n][:, halves[half]], y[:], ACT.Copy, scale=-1.0)
 
         def place(n, cols):
-            frame = frames[n % len(frames)]
+            frame = frames[n % FRAMES]
             nc.vector.tensor_tensor(frame[:].indirect(listed(idx2, cols)), y_sb[n][:, cols], wgo_sb[:, cols], ALU.mult)
 
         def store(n):
-            nc.sync.dma_start(out[n * P : (n + 1) * P, :], frames[n % len(frames)][:])
+            nc.sync.dma_start(out[n * P : (n + 1) * P, :], frames[n % FRAMES][:])
 
-        whole = slice(0, S)
-        halves = [slice(h * HALF, (h + 1) * HALF) for h in range(HALVES)]
-
-        nc.vector.tensor_copy(v_s[:], tab_s[:].indirect(idx[:]))
         nc.vector.tensor_copy(v_w[:], tab_w[:].bitcast(U32).indirect(idx[:]))
-        round_w2(0)
-        for pair in range(2 * last):
-            a, t0 = divmod(2 * pair, PACK)
-            both = keep.tile([P, 2, S + HALF], F32, name="work", tag=("w2_raw0", "pair0", "pair1", "w2_raw0")[pair], align_bytes=64)
-            for u in range(2):
-                spare_d[a, t0 + u] = both[:, u, S:]
-                picked = ring.tile([P, S], F32, name="picked", bufs=2)
-                gather_s(a, t0 + u, whole, picked[:], both[:, u, :S])
-            if pair == 0:
-                quantize_w2(0, words("w2_w0", PASS)[:])
-            if pair >= 2:
-                codes = words("pair%d" % pair, PASS + HALF)
-                quantize_w2(pair - 1, codes[:, :PASS])
-                quantize_h(0, pair - 2, codes[:, PASS:])
-            for u in range(2):
+        nc.vector.tensor_copy(v_s[:], tab_s[:].indirect(idx[:]))
+        round_w2(0, AT_W2_BF)
+        quantize_w2(0, AT_W2_CODES)
+        last = SLICES - 1
+        square_places = {0: AT_SQUARE, 2: at_w2(1), 6: at_rows(0, 0), 7: at_w2(2), 10: at_rows(1, 0)}
+        lagging = []
+        for k in range(last):
+            a, t = divmod(k, PACK)
+            picked = gather_s(k, whole, at_picked(k))
+            if k in (2, 7):
+                round_w2((k + 2) // PACK, at_picked(k - 1))
+            if k in (6, 10):
+                interleave_h(a - 1, 0, at_picked(k - 1))
+            square_s(k, whole, picked, square_places.get(k, at_picked(k - 1)))
+            if t == 1:
                 for half in range(HALVES):
-                    derivative(a, t0 + u, half)
-            if pair in (1, 2):
-                interleave_h(0, pair - 1)
-                round_w2(pair)
-        interleave_h(last - 1, 0)
+                    if (k - 1, half) != (0, 0):
+                        derivative_vector(k - 1, half)
+            if k == 0:
+                derivative_gpsimd(k, 0)
+            if t >= 1 and k < last - 1:
+                derivative_gpsimd(k, 0)
+                lagging.append(k)
+                if len(lagging) > LAG:
+                    derivative_gpsimd(lagging.pop(0), 1)
+            if k in (4, 8):
+                quantize_w2(a, at_s(k))
+        for k in lagging:
+            derivative_gpsimd(k, 1)
 
-        first_squares = keep.tile([P, PACK, HALF], F32, name="first_squares", tag="pair0", align_bytes=64)
-        for t in range(PACK):
-            picked = keep.tile([P, HALF], F32, name="first_picked", tag=SPARE[t], align_bytes=64)
-            gather_s(last, t, halves[0], picked[:], first_squares[:, t, :])
-        quantize_h(last - 1, 0, words(SPARE[0], HALF)[:])
-        for t in range(PACK):
-            derivative(last, t, 0)
-        interleave_h(last, 0)
-        interleave_h(last - 1, 1)
-        second_picked = keep.tile([P, PACK, HALF], F32, name="second_picked", tag="pair0", align_bytes=64)
-        second_squares = keep.tile([P, PACK, HALF], F32, name="second_squares", tag="pair1", align_bytes=64)
-        last_d = keep.tile([P, 1, HALF], F32, name="last_d", tag="w2_raw0", align_bytes=64)
-        for t in range(1):
-            spare_d[last, t] = last_d[:, t, :]
-        for t in range(PACK):
-            gather_s(last, t, halves[1], second_picked[:, t, :], second_squares[:, t, :])
-        quantize_h(last, 0, words(SPARE[1], HALF)[:])
-        quantize_h(last - 1, 1, words("h_rows20", HALF)[:])
-        for t in range(PACK):
-            derivative(last, t, 1)
+        picked = [gather_s(last, halves[half], at_picked(last) + 2 * half) for half in range(HALVES)]
+        square_s(last, halves[0], picked[0], at_picked(last - 1))
+        square_s(last, halves[1], picked[1], at_picked(last))
+        derivative_vector(last - 1, 0)
+        derivative_vector(last, 0)
+        interleave_h(2, 0, at_s(6))
+        quantize_h(1, 0, at_s(7) + 4, at_picked(last - 1))
+        quantize_h(0, 0, at_s(7) + 6, at_picked(last - 1) + 0.5)
+        derivative_vector(last - 1, 1)
+        derivative_vector(last, 1)
+        quantize_h(2, 0, at_s(4) + 4, at_s(7) + 2.5)
         product(0, 0)
-        interleave_h(last, 1)
-        product(1, 0)
         place(0, halves[0])
-        quantize_h(last, 1, words(SPARE[2], HALF)[:])
+        words_places = [at_rows(2, 0), at_rows(0, 1), at_rows(1, 1)]
+        for a in range(PASSES):
+            interleave_h(a, 1, words_places[a])
+            quantize_h(a, 1, at_s(8) + 4 + 2 * a if a < 2 else at_s(4) + 6, at_s(7) + 3 - a)
+            product(a + 1, 0)
+            place(a + 1, halves[0])
         for n in range(SPLIT_BLOCKS):
             product(n, 1)
-        for n in range(1, SPLIT_BLOCKS):
-            place(n, halves[0])
-        for n in range(SPLIT_BLOCKS):
             place(n, halves[1])
             store(n)
         for n in range(SPLIT_BLOCKS, BLOCKS):

@@ -28,7 +28,6 @@ PER_COLUMN = 16
 SPLIT_BLOCKS = 4
 FRAMES = 4
 KB = 1024
-LAG = 1
 
 AT_S = 0
 AT_W2 = 96
@@ -40,12 +39,13 @@ AT_TAB_S = 176
 AT_V_W = 178
 AT_V_S = 182
 AT_W1_S = 183
-AT_PICKED = 184
-AT_D = 208
+AT_SQUARES = 184
+AT_D = 200
+AT_PICKED = 208
 AT_W2_BF = 224
 AT_W2_CODES = 228
-AT_SQUARE = 232
-D_PLACES = [AT_D + 2 * i for i in range(8)] + [AT_TAB + 2 * i for i in range(4)] + [AT_W2 + 4, AT_W2 + 6, AT_W2 + 12]
+AT_SPARE = 231
+CHUNK = 128
 
 
 def tile_list_fibre_equaliser_backward_kernel(
@@ -65,14 +65,6 @@ def tile_list_fibre_equaliser_backward_kernel(
 
         def at_w2(a):
             return AT_W2 + 8 * a
-
-        def at_rows(a, half):
-            return at_w2(0) if (a, half) == (0, 0) else at_s(PACK * a + 1) + 4 * half
-
-        def at_picked(k):
-            if k < 6:
-                return AT_PICKED + 4 * k
-            return at_s(0) + 4 * (k - 6) if k < 8 else at_s(2) + 4 * (k - 8)
 
         idx = lists.tile([P, S // PER_COLUMN], U16, name="idx")
         idx2 = lists.tile([P, S // PER_COLUMN], U16, name="idx2")
@@ -104,13 +96,6 @@ def tile_list_fibre_equaliser_backward_kernel(
             s_sb[k] = place_tile("s%d" % k, [P, T], F32, at_s(k))[:]
             nc.sync.dma_start(s_sb[k], s_rows[a][:, t, :])
 
-        def load_s_pair(k):
-            a, t = divmod(k, PACK)
-            both = place_tile("s%d" % k, [P, 2, T], F32, at_s(k))
-            nc.sync.dma_start(both[:], s_rows[a][:, t : t + 2, :])
-            for u in range(2):
-                s_sb[k + u] = both[:, u, :]
-
         def load_w2(a):
             w2_raw[a] = place_tile("w2_raw%d" % a, [P, PACK, PASS], F32, at_w2(a))
             nc.sync.dma_start(
@@ -123,8 +108,8 @@ def tile_list_fibre_equaliser_backward_kernel(
             nc.sync.dma_start(
                 tab_s[32 * q : 32 * q + 4, :].bitcast(I32), tab_scales[0, 4 * q : 4 * q + 4, :].bitcast(I32)
             )
-        for k in range(SLICES - 1):
-            if k in (0, 2, 7):
+        for k in range(SLICES):
+            if k in (0, 2, 9):
                 load_w2((k + 2) // PACK)
             if k == SLICES - 2:
                 nc.sync.dma_start(idx2[:], offs2)
@@ -133,10 +118,7 @@ def tile_list_fibre_equaliser_backward_kernel(
                         w1_s[32 * q : 32 * q + 4 * PASSES, :].bitcast(I32),
                         w1_scales[:, 4 * q : 4 * q + 4, :].bitcast(I32),
                     )
-            if k == SLICES - 2:
-                load_s_pair(k)
-            else:
-                load_s(k)
+            load_s(k)
         nc.sync.dma_start(w1_first[:], w1_rows[:, :, :first_cols])
         nc.sync.dma_start(wgo_sb[:], wgo)
         nc.sync.dma_start(w1_rest[:], w1_rows[:, :, first_cols:])
@@ -144,7 +126,6 @@ def tile_list_fibre_equaliser_backward_kernel(
         w2_bf, w2_w, w2_s, h_rows, h_words, h_w, h_s, squares, y_sb = {}, {}, {}, {}, {}, {}, {}, {}, {}
         whole = slice(0, S)
         halves = [slice(h * HALF, (h + 1) * HALF) for h in range(HALVES)]
-        evacuated = []
 
         def round_w2(a, kib):
             w2_bf[a] = place_tile("w2_bf%d" % a, [P, PASS * PACK], BF16, kib)
@@ -183,21 +164,25 @@ def tile_list_fibre_equaliser_backward_kernel(
                 start=True,
                 stop=True,
             )
-            if t == 0:
-                h_rows[a, half] = place_tile("h_rows%d%d" % (a, half), [P, PACK, HALF], BF16, at_rows(a, half))
-            return d, h_rows[a, half][:, t, :]
+            return d
 
         def derivative_vector(k, half):
-            d, h = first_product(k, half)
-            nc.vector.scalar_tensor_tensor(h, squares[k, half], 1.0, d[:], ALU.subtract, ALU.mult)
+            a, t = divmod(k, PACK)
+            d = first_product(k, half)
+            nc.vector.scalar_tensor_tensor(h_rows[a, half][:, t, :], squares[k, half], 1.0, d[:], ALU.subtract, ALU.mult)
 
-        def derivative_gpsimd(k, half):
-            d, h = first_product(k, half)
-            d_sb = place_tile("d_sb%d_%d" % (k, half), [P, HALF], F32, D_PLACES[len(evacuated) % len(D_PLACES)])
-            evacuated.append((k, half))
-            nc.scalar.copy(d_sb[:], d[:])
-            nc.gpsimd.tensor_scalar(squares[k, half], squares[k, half], 1.0, -1.0, ALU.mult, ALU.add)
-            nc.gpsimd.tensor_tensor(h, squares[k, half], d_sb[:], ALU.mult)
+        def derivative_gpsimd(a, half, factors, d_kib, words_kib):
+            d_sb = place_tile("d_sb%d%d" % (a, half), [P, PACK, HALF], F32, d_kib)
+            for t in range(PACK):
+                nc.scalar.copy(d_sb[:, t, :], first_product(PACK * a + t, half)[:])
+            h_words[a, half] = place_tile("h_words%d%d" % (a, half), [P, HALF * PACK], BF16, words_kib)
+            for c in range(0, HALF, CHUNK):
+                nc.gpsimd.tensor_tensor(
+                    h_words[a, half][:, PACK * c : PACK * (c + CHUNK)].rearrange("p (c i t) -> p c t i", i=4, t=PACK),
+                    factors[:, half, :, c : c + CHUNK].rearrange("p t (c i) -> p c t i", i=4),
+                    d_sb[:, :, c : c + CHUNK].rearrange("p t (c i) -> p c t i", i=4),
+                    ALU.mult,
+                )
 
         def interleave_h(a, half, kib):
             h_words[a, half] = place_tile("h_words%d%d" % (a, half), [P, HALF * PACK], BF16, kib)
@@ -225,16 +210,21 @@ def tile_list_fibre_equaliser_backward_kernel(
                     start=(a == 0),
                     stop=(a == PASSES - 1),
                 )
-            if half == 0:
-                y_sb[n] = place_tile("y_sb%d" % n, [P, S], F32, AT_PICKED + 4 * (n % FRAMES))
-            if (n, half) == (0, 0):
-                nc.vector.tensor_scalar_mul(y_sb[n][:, halves[half]], y[:], -1.0)
+            if n < SPLIT_BLOCKS:
+                y_sb[n] = place_tile("y_sb%d%d" % (n, half), [P, HALF], F32, at_s(11) + 2 * n if half == 0 else at_s(2) + 2 * n)[:]
+                target = y_sb[n]
             else:
-                nc.scalar.activation(y_sb[n][:, halves[half]], y[:], ACT.Copy, scale=-1.0)
+                if half == 0:
+                    y_sb[n] = place_tile("y_sb%d" % n, [P, S], F32, AT_SQUARES + 4 * (n % FRAMES))[:]
+                target = y_sb[n][:, halves[half]]
+            if (n, half) == (0, 0):
+                nc.vector.tensor_scalar_mul(target, y[:], -1.0)
+            else:
+                nc.scalar.activation(target, y[:], ACT.Copy, scale=-1.0)
 
         def place(n, cols):
             frame = frames[n % FRAMES]
-            nc.vector.tensor_tensor(frame[:].indirect(listed(idx2, cols)), y_sb[n][:, cols], wgo_sb[:, cols], ALU.mult)
+            nc.vector.tensor_tensor(frame[:].indirect(listed(idx2, cols)), y_sb[n], wgo_sb[:, cols], ALU.mult)
 
         def store(n):
             nc.sync.dma_start(out[n * P : (n + 1) * P, :], frames[n % FRAMES][:])
@@ -243,52 +233,51 @@ def tile_list_fibre_equaliser_backward_kernel(
         nc.vector.tensor_copy(v_s[:], tab_s[:].indirect(idx[:]))
         round_w2(0, AT_W2_BF)
         quantize_w2(0, AT_W2_CODES)
-        last = SLICES - 1
-        square_places = {0: AT_SQUARE, 2: at_w2(1), 6: at_rows(0, 0), 7: at_w2(2), 10: at_rows(1, 0)}
-        lagging = []
-        for k in range(last):
-            a, t = divmod(k, PACK)
-            picked = gather_s(k, whole, at_picked(k))
-            if k in (2, 7):
-                round_w2((k + 2) // PACK, at_picked(k - 1))
-            if k in (6, 10):
-                interleave_h(a - 1, 0, at_picked(k - 1))
-            square_s(k, whole, picked, square_places.get(k, at_picked(k - 1)))
-            if t == 1:
-                for half in range(HALVES):
-                    if (k - 1, half) != (0, 0):
-                        derivative_vector(k - 1, half)
-            if k == 0:
-                derivative_gpsimd(k, 0)
-            if t >= 1 and k < last - 1:
-                derivative_gpsimd(k, 0)
-                lagging.append(k)
-                if len(lagging) > LAG:
-                    derivative_gpsimd(lagging.pop(0), 1)
-            if k in (4, 8):
-                quantize_w2(a, at_s(k))
-        for k in lagging:
-            derivative_gpsimd(k, 1)
+        picked_places = [AT_PICKED, AT_PICKED + 4, AT_PICKED + 8, AT_PICKED + 12, AT_TAB, AT_TAB + 4, AT_PICKED, AT_PICKED + 4]
+        for a in range(PASSES - 1):
+            factors = place_tile("factors%d" % a, [P, HALVES, PACK, HALF], F32, (AT_SQUARES, at_s(0))[a])
+            for t in range(PACK):
+                k = PACK * a + t
+                picked = gather_s(k, whole, picked_places[k])
+                if k == 2:
+                    round_w2(1, AT_W2_BF)
+                nc.scalar.activation(factors[:, :, t, :], picked[:].rearrange("p (h c) -> p h c", h=HALVES), ACT.Square)
+                nc.gpsimd.tensor_scalar(factors[:, :, t, :], factors[:, :, t, :], 1.0, -1.0, ALU.mult, ALU.add)
+                if k == PACK:
+                    quantize_w2(1, at_s(k))
+            derivative_gpsimd(a, 0, factors, (AT_D, at_s(2))[a], at_w2(a))
+            derivative_gpsimd(a, 1, factors, (AT_PICKED + 8, AT_PICKED)[a], at_w2(a) + 4)
 
-        picked = [gather_s(last, halves[half], at_picked(last) + 2 * half) for half in range(HALVES)]
-        square_s(last, halves[0], picked[0], at_picked(last - 1))
-        square_s(last, halves[1], picked[1], at_picked(last))
-        derivative_vector(last - 1, 0)
-        derivative_vector(last, 0)
-        interleave_h(2, 0, at_s(6))
-        quantize_h(1, 0, at_s(7) + 4, at_picked(last - 1))
-        quantize_h(0, 0, at_s(7) + 6, at_picked(last - 1) + 0.5)
-        derivative_vector(last - 1, 1)
-        derivative_vector(last, 1)
-        quantize_h(2, 0, at_s(4) + 4, at_s(7) + 2.5)
+        last = SLICES - 1
+        square_s(8, whole, gather_s(8, whole, AT_TAB), at_s(3))
+        quantize_h(0, 0, at_s(8), at_s(8) + 2)
+        round_w2(2, AT_W2_BF)
+        square_s(9, whole, gather_s(9, whole, AT_TAB + 4), at_w2(2))
+        quantize_w2(2, at_s(9))
+        square_s(10, whole, gather_s(10, whole, AT_SPARE), at_w2(2) + 4)
+        picked = [gather_s(last, halves[half], AT_SPARE + 4 + 2 * half) for half in range(HALVES)]
+        square_s(last, halves[0], picked[0], at_s(3) + 4)
+        square_s(last, halves[1], picked[1], AT_SPARE)
+        h_rows[2, 0] = place_tile("h_rows20", [P, PACK, HALF], BF16, at_s(10))
+        for k in range(8, SLICES):
+            derivative_vector(k, 0)
+        interleave_h(2, 0, at_s(5))
+        h_rows[2, 1] = place_tile("h_rows21", [P, PACK, HALF], BF16, at_s(3) + 4)
+        for k in range(8, SLICES):
+            derivative_vector(k, 1)
+        quantize_h(1, 0, at_s(6), at_s(3))
+        quantize_h(2, 0, at_s(6) + 2, at_s(7))
+        quantize_h(0, 1, at_s(6) + 4, at_s(5))
         product(0, 0)
         place(0, halves[0])
-        words_places = [at_rows(2, 0), at_rows(0, 1), at_rows(1, 1)]
-        for a in range(PASSES):
-            interleave_h(a, 1, words_places[a])
-            quantize_h(a, 1, at_s(8) + 4 + 2 * a if a < 2 else at_s(4) + 6, at_s(7) + 3 - a)
-            product(a + 1, 0)
-            place(a + 1, halves[0])
+        interleave_h(2, 1, at_s(5) + 4)
+        quantize_h(1, 1, at_s(6) + 6, at_s(11))
+        product(1, 0)
+        place(1, halves[0])
+        quantize_h(2, 1, at_s(7) + 2, at_s(11) + 2)
+        for n in range(2, SPLIT_BLOCKS):
+            product(n, 0)
+            place(n, halves[0])
         for n in range(SPLIT_BLOCKS):
             product(n, 1)
             place(n, halves[1])

@@ -28,24 +28,26 @@ PER_COLUMN = 16
 SPLIT_BLOCKS = 4
 FRAMES = 4
 KB = 1024
+BANKS = {"first": (0, 1), "second": (2, 3, 4, 5), "turn": (6, 7)}
+PAIRED = ()
 
 AT_S = 0
 AT_W2 = 96
 AT_TAB = 120
 AT_FRAME = 128
-AT_W1 = 160
-AT_WGO = 172
-AT_TAB_S = 176
-AT_V_W = 178
-AT_V_S = 182
-AT_W1_S = 183
-AT_SQUARES = 184
-AT_D = 200
-AT_PICKED = 208
-AT_W2_BF = 224
-AT_W2_CODES = 228
-AT_SPARE = 231
-CHUNK = 128
+AT_W1 = 168
+AT_WGO = 180
+AT_TAB_S = 184
+AT_V_W = 186
+AT_V_S = 190
+AT_W1_S = 191
+AT_W2_BF = 192
+AT_PICKED_MORE = 196
+AT_LATE = 228
+AT_PICKED = 200
+AT_SQUARE = 216
+AT_D = 220
+AT_SMALL = 160
 
 
 def tile_list_fibre_equaliser_backward_kernel(
@@ -55,10 +57,18 @@ def tile_list_fibre_equaliser_backward_kernel(
     with ExitStack() as ctx:
         lists = ctx.enter_context(tc.tile_pool(name="lists", bufs=1))
         arena = ctx.enter_context(tc.tile_pool(name="arena", bufs=1))
-        psum = ctx.enter_context(tc.psum_pool(name="psum", bufs=8))
+        psum = ctx.enter_context(tc.psum_pool(name="psum", bufs=1))
 
         def place_tile(name, shape, dtype, kib):
             return arena.tile(shape, dtype, name=name, tag=name, align_bytes=64, offset=int(kib * KB))
+
+        taken = {kind: [] for kind in BANKS}
+
+        def bank(kind):
+            number = BANKS[kind][len(taken[kind]) % len(BANKS[kind])]
+            taken[kind].append(number)
+            name = "%s%d" % (kind, len(taken[kind]))
+            return psum.tile([P, HALF], F32, name=name, tag=name, offset=number * 2 * KB)
 
         def at_s(k):
             return AT_S + 8 * k
@@ -109,21 +119,20 @@ def tile_list_fibre_equaliser_backward_kernel(
                 tab_s[32 * q : 32 * q + 4, :].bitcast(I32), tab_scales[0, 4 * q : 4 * q + 4, :].bitcast(I32)
             )
         for k in range(SLICES):
-            if k in (0, 2, 9):
-                load_w2((k + 2) // PACK)
-            if k == SLICES - 2:
-                nc.sync.dma_start(idx2[:], offs2)
-                for q in range(4):
-                    nc.sync.dma_start(
-                        w1_s[32 * q : 32 * q + 4 * PASSES, :].bitcast(I32),
-                        w1_scales[:, 4 * q : 4 * q + 4, :].bitcast(I32),
-                    )
+            if k in (0, 3, 7):
+                load_w2((k + 1) // PACK)
             load_s(k)
+        nc.sync.dma_start(idx2[:], offs2)
+        for q in range(4):
+            nc.sync.dma_start(
+                w1_s[32 * q : 32 * q + 4 * PASSES, :].bitcast(I32),
+                w1_scales[:, 4 * q : 4 * q + 4, :].bitcast(I32),
+            )
         nc.sync.dma_start(w1_first[:], w1_rows[:, :, :first_cols])
         nc.sync.dma_start(wgo_sb[:], wgo)
         nc.sync.dma_start(w1_rest[:], w1_rows[:, :, first_cols:])
 
-        w2_bf, w2_w, w2_s, h_rows, h_words, h_w, h_s, squares, y_sb = {}, {}, {}, {}, {}, {}, {}, {}, {}
+        w2_bf, w2_w, w2_s, h_rows, h_words, h_w, h_s, picked, squares, y_sb = {}, {}, {}, {}, {}, {}, {}, {}, {}, {}
         whole = slice(0, S)
         halves = [slice(h * HALF, (h + 1) * HALF) for h in range(HALVES)]
 
@@ -139,22 +148,22 @@ def tile_list_fibre_equaliser_backward_kernel(
             w2_s[a] = place_tile("w2_s%d" % a, [P, PASS], U8, kib + 2)
             nc.vector.quantize_mx(out=w2_w[a][:].bitcast(E4M3), scales=w2_s[a][:], in_=w2_bf[a][:])
 
-        def gather_s(k, cols, picked_kib):
-            picked = place_tile("picked%d_%d" % (k, cols.start), [P, cols.stop - cols.start], F32, picked_kib)
-            nc.vector.tensor_copy(picked[:], s_sb[k].indirect(listed(idx, cols)))
-            return picked
+        def gather_s(k, cols, kib):
+            tile = place_tile("picked%d_%d" % (k, cols.start), [P, cols.stop - cols.start], F32, kib)
+            nc.vector.tensor_copy(tile[:], s_sb[k].indirect(listed(idx, cols)))
+            picked[k, cols.start] = tile
 
-        def square_s(k, cols, picked, kib):
+        def square_s(k, cols, kib):
             square = place_tile("square%d_%d" % (k, cols.start), [P, cols.stop - cols.start], F32, kib)
-            nc.scalar.activation(square[:], picked[:], ACT.Square)
+            nc.scalar.activation(square[:], picked[k, cols.start][:], ACT.Square)
             for half in range(cols.start // HALF, cols.stop // HALF):
                 lo = half * HALF - cols.start
                 squares[k, half] = square[:, lo : lo + HALF]
 
-        def first_product(k, half):
+        def first_product(k, half, kind):
             a, t = divmod(k, PACK)
             rcols = slice(t * P, (t + 1) * P)
-            d = psum.tile([P, HALF], F32, name="d", tag="bank")
+            d = bank(kind)
             nc.tensor.matmul_mx(
                 out=d[:],
                 lhsT=w2_w[a][:, rcols].bitcast(E4M3),
@@ -166,26 +175,42 @@ def tile_list_fibre_equaliser_backward_kernel(
             )
             return d
 
-        def derivative_vector(k, half):
+        def rows_h(a, half, kib):
+            h_rows[a, half] = place_tile("h_rows%d%d" % (a, half), [P, PACK, HALF], BF16, kib)
+
+        def derivative_vector(k, half, kind):
             a, t = divmod(k, PACK)
-            d = first_product(k, half)
+            d = first_product(k, half, kind)
             nc.vector.scalar_tensor_tensor(h_rows[a, half][:, t, :], squares[k, half], 1.0, d[:], ALU.subtract, ALU.mult)
 
-        def derivative_gpsimd(a, half, factors, d_kib, words_kib):
-            d_sb = place_tile("d_sb%d%d" % (a, half), [P, PACK, HALF], F32, d_kib)
-            for t in range(PACK):
-                nc.scalar.copy(d_sb[:, t, :], first_product(PACK * a + t, half)[:])
-            h_words[a, half] = place_tile("h_words%d%d" % (a, half), [P, HALF * PACK], BF16, words_kib)
-            for c in range(0, HALF, CHUNK):
-                nc.gpsimd.tensor_tensor(
-                    h_words[a, half][:, PACK * c : PACK * (c + CHUNK)].rearrange("p (c i t) -> p c t i", i=4, t=PACK),
-                    factors[:, half, :, c : c + CHUNK].rearrange("p t (c i) -> p c t i", i=4),
-                    d_sb[:, :, c : c + CHUNK].rearrange("p t (c i) -> p c t i", i=4),
-                    ALU.mult,
-                )
+        def empty_d(k, half, kind, kib):
+            d = first_product(k, half, kind)
+            d_sb = place_tile("d_sb%d_%d" % (k, half), [P, HALF], F32, kib)
+            nc.scalar.copy(d_sb[:], d[:])
+            return d_sb
+
+        def multiply_gpsimd(k, half, factor, d_sb):
+            a, t = divmod(k, PACK)
+            if (a, half) in PAIRED:
+                pairs = h_rows[a, half][:].rearrange("p (u x) c -> p u (x c)", u=2).rearrange("p u (c e) -> p u c e", e=2)
+                target = pairs[:, t // 2, :, t % 2]
+            else:
+                target = h_rows[a, half][:, t, :]
+            nc.gpsimd.tensor_tensor(target, factor, d_sb[:], ALU.mult)
+
+        def less_one_gpsimd(k, half, kib=None):
+            factor = squares[k, half] if kib is None else place_tile("factor%d" % k, [P, HALF], F32, kib)[:]
+            nc.gpsimd.tensor_scalar(factor, squares[k, half], 1.0, -1.0, ALU.mult, ALU.add)
+            return factor
 
         def interleave_h(a, half, kib):
             h_words[a, half] = place_tile("h_words%d%d" % (a, half), [P, HALF * PACK], BF16, kib)
+            if (a, half) in PAIRED:
+                nc.scalar.copy(
+                    h_words[a, half][:].bitcast(U32).rearrange("p (c u) -> p c u", u=2),
+                    h_rows[a, half][:].rearrange("p t c -> p (t c)").bitcast(U32).rearrange("p (u c) -> p c u", u=2),
+                )
+                return
             nc.scalar.copy(
                 h_words[a, half][:].rearrange("p (c i t) -> p c t i", i=4, t=PACK),
                 h_rows[a, half][:].rearrange("p t (c i) -> p c t i", i=4),
@@ -196,10 +221,10 @@ def tile_list_fibre_equaliser_backward_kernel(
             h_s[a, half] = place_tile("h_s%d%d" % (a, half), [P, HALF], U8, scales_kib)
             nc.vector.quantize_mx(out=h_w[a, half][:].bitcast(E4M3), scales=h_s[a, half][:], in_=h_words[a, half][:])
 
-        def product(n, half):
+        def product(n, half, kib):
             ncols = slice(n * P, (n + 1) * P)
             w1_w = w1_first[:, :, ncols] if n < SPLIT_BLOCKS else w1_rest[:, :, n * P - first_cols : (n + 1) * P - first_cols]
-            y = psum.tile([P, HALF], F32, name="y", tag="bank")
+            y = bank("first" if n < SPLIT_BLOCKS and half == 0 else "second")
             for a in range(PASSES):
                 nc.tensor.matmul_mx(
                     out=y[:],
@@ -211,11 +236,11 @@ def tile_list_fibre_equaliser_backward_kernel(
                     stop=(a == PASSES - 1),
                 )
             if n < SPLIT_BLOCKS:
-                y_sb[n] = place_tile("y_sb%d%d" % (n, half), [P, HALF], F32, at_s(11) + 2 * n if half == 0 else at_s(2) + 2 * n)[:]
+                y_sb[n] = place_tile("y_sb%d%d" % (n, half), [P, HALF], F32, kib)[:]
                 target = y_sb[n]
             else:
                 if half == 0:
-                    y_sb[n] = place_tile("y_sb%d" % n, [P, S], F32, AT_SQUARES + 4 * (n % FRAMES))[:]
+                    y_sb[n] = place_tile("y_sb%d" % n, [P, S], F32, kib)[:]
                 target = y_sb[n][:, halves[half]]
             if (n, half) == (0, 0):
                 nc.vector.tensor_scalar_mul(target, y[:], -1.0)
@@ -223,67 +248,108 @@ def tile_list_fibre_equaliser_backward_kernel(
                 nc.scalar.activation(target, y[:], ACT.Copy, scale=-1.0)
 
         def place(n, cols):
-            frame = frames[n % FRAMES]
-            nc.vector.tensor_tensor(frame[:].indirect(listed(idx2, cols)), y_sb[n], wgo_sb[:, cols], ALU.mult)
+            window = frames[n % FRAMES][:].indirect(listed(idx2, cols))
+            nc.vector.tensor_tensor(window, y_sb[n], wgo_sb[:, cols], ALU.mult)
 
         def store(n):
             nc.sync.dma_start(out[n * P : (n + 1) * P, :], frames[n % FRAMES][:])
 
+        first, second = halves
+        last = SLICES - 1
+
+        def half_gpsimd(k, half, d_kib):
+            d_sb = empty_d(k, half, ("first", "second")[half], d_kib)
+            multiply_gpsimd(k, half, less_one_gpsimd(k, half), d_sb)
+
         nc.vector.tensor_copy(v_w[:], tab_w[:].bitcast(U32).indirect(idx[:]))
         nc.vector.tensor_copy(v_s[:], tab_s[:].indirect(idx[:]))
         round_w2(0, AT_W2_BF)
-        quantize_w2(0, AT_W2_CODES)
-        picked_places = [AT_PICKED, AT_PICKED + 4, AT_PICKED + 8, AT_PICKED + 12, AT_TAB, AT_TAB + 4, AT_PICKED, AT_PICKED + 4]
-        for a in range(PASSES - 1):
-            factors = place_tile("factors%d" % a, [P, HALVES, PACK, HALF], F32, (AT_SQUARES, at_s(0))[a])
-            for t in range(PACK):
-                k = PACK * a + t
-                picked = gather_s(k, whole, picked_places[k])
-                if k == 2:
-                    round_w2(1, AT_W2_BF)
-                nc.scalar.activation(factors[:, :, t, :], picked[:].rearrange("p (h c) -> p h c", h=HALVES), ACT.Square)
-                nc.gpsimd.tensor_scalar(factors[:, :, t, :], factors[:, :, t, :], 1.0, -1.0, ALU.mult, ALU.add)
-                if k == PACK:
-                    quantize_w2(1, at_s(k))
-            derivative_gpsimd(a, 0, factors, (AT_D, at_s(2))[a], at_w2(a))
-            derivative_gpsimd(a, 1, factors, (AT_PICKED + 8, AT_PICKED)[a], at_w2(a) + 4)
+        quantize_w2(0, at_s(0) + 4)
 
-        last = SLICES - 1
-        square_s(8, whole, gather_s(8, whole, AT_TAB), at_s(3))
-        quantize_h(0, 0, at_s(8), at_s(8) + 2)
-        round_w2(2, AT_W2_BF)
-        square_s(9, whole, gather_s(9, whole, AT_TAB + 4), at_w2(2))
-        quantize_w2(2, at_s(9))
-        square_s(10, whole, gather_s(10, whole, AT_SPARE), at_w2(2) + 4)
-        picked = [gather_s(last, halves[half], AT_SPARE + 4 + 2 * half) for half in range(HALVES)]
-        square_s(last, halves[0], picked[0], at_s(3) + 4)
-        square_s(last, halves[1], picked[1], AT_SPARE)
-        h_rows[2, 0] = place_tile("h_rows20", [P, PACK, HALF], BF16, at_s(10))
+        rows_h(0, 0, at_w2(0))
+        rows_h(0, 1, at_s(2))
+        for k in range(4):
+            gather_s(k, whole, AT_PICKED + 4 * k)
+            if k == 3:
+                round_w2(1, AT_W2_BF)
+            square_s(k, whole, (AT_SQUARE, AT_PICKED_MORE, AT_PICKED, at_w2(1))[k])
+            half_gpsimd(k, 0, (AT_D, AT_D + 2, at_w2(0) + 4, AT_PICKED + 4)[k])
+            if k == 2:
+                derivative_vector(0, 1, "second")
+                derivative_vector(1, 1, "second")
+            if k >= 2:
+                half_gpsimd(k, 1, (AT_PICKED + 6, AT_PICKED + 8)[k - 2])
+
+        rows_h(1, 0, at_s(1))
+        rows_h(1, 1, at_s(6))
+        for k in range(4, 8):
+            cols = whole if k < 6 else first
+            gather_s(k, cols, (AT_TAB, AT_TAB + 4, AT_LATE, AT_LATE + 2)[k - 4])
+            if k >= 6:
+                gather_s(k, second, AT_LATE + 4 + 2 * (k - 6))
+            if k == 4:
+                quantize_w2(1, at_s(k) + 4)
+            if k == 6:
+                interleave_h(0, 0, AT_TAB + 4)
+            if k == 7:
+                round_w2(2, AT_W2_BF)
+            square_s(k, cols, (AT_PICKED + 12, at_s(0), at_w2(0), at_w2(2))[k - 4])
+            half_gpsimd(k, 0, (AT_D + 4, AT_D + 6, AT_LATE, AT_LATE + 2)[k - 4])
+            if k == 6:
+                derivative_vector(4, 1, "second")
+                derivative_vector(5, 1, "second")
+
+        rows_h(2, 0, at_s(1) + 4)
+        for k in range(8, last):
+            gather_s(k, first, at_s(5) + 2 * (k - 8))
+            gather_s(k, second, (at_s(4), at_s(4) + 2, at_s(3) + 4)[k - 8])
+            if k == 8:
+                quantize_w2(2, at_s(k))
+            if k == 10:
+                interleave_h(1, 0, at_s(5))
+            square_s(k, first, (AT_SMALL, AT_SMALL + 2, at_s(1))[k - 8])
+            half_gpsimd(k, 0, (AT_D, AT_D + 2, AT_D + 4)[k - 8])
+        square_s(8, second, at_s(5) + 4)
+
+        gather_s(last, first, at_s(5) + 6)
+        gather_s(last, second, at_s(9) + 4)
+        square_s(last, first, AT_SMALL + 6)
+        derivative_vector(last, 0, "first")
+        square_s(9, second, at_s(5) + 6)
+        square_s(10, second, at_s(4) + 2)
+        interleave_h(2, 0, at_s(3) + 4)
+        square_s(11, second, at_s(1) + 4)
+        quantize_h(0, 0, at_s(10) + 6, AT_SMALL + 6)
+        quantize_h(1, 0, at_s(10), AT_SMALL + 6.5)
+        rows_h(2, 1, at_s(5))
         for k in range(8, SLICES):
-            derivative_vector(k, 0)
-        interleave_h(2, 0, at_s(5))
-        h_rows[2, 1] = place_tile("h_rows21", [P, PACK, HALF], BF16, at_s(3) + 4)
-        for k in range(8, SLICES):
-            derivative_vector(k, 1)
-        quantize_h(1, 0, at_s(6), at_s(3))
-        quantize_h(2, 0, at_s(6) + 2, at_s(7))
-        quantize_h(0, 1, at_s(6) + 4, at_s(5))
-        product(0, 0)
-        place(0, halves[0])
-        interleave_h(2, 1, at_s(5) + 4)
-        quantize_h(1, 1, at_s(6) + 6, at_s(11))
-        product(1, 0)
-        place(1, halves[0])
-        quantize_h(2, 1, at_s(7) + 2, at_s(11) + 2)
-        for n in range(2, SPLIT_BLOCKS):
-            product(n, 0)
-            place(n, halves[0])
+            derivative_vector(k, 1, "turn")
+            if k == 10:
+                quantize_h(2, 0, at_s(10) + 2, at_s(7) + 2.5)
+
+        product(0, 0, at_s(11))
+        place(0, first)
+        for k in (6, 7):
+            square_s(k, second, (at_s(9) + 4, AT_LATE + 4)[k - 6])
+            derivative_vector(k, 1, "turn")
+        product(1, 0, at_s(11) + 2)
+        interleave_h(0, 1, AT_LATE + 6)
+        quantize_h(0, 1, at_s(10) + 4, at_s(11))
+        place(1, first)
+        product(2, 0, at_s(11) + 4)
+        interleave_h(2, 1, at_s(2))
+        quantize_h(2, 1, at_s(7) + 4, at_s(11) + 2)
+        place(2, first)
+        interleave_h(1, 1, at_s(5))
+        product(3, 0, at_s(6))
+        quantize_h(1, 1, at_s(7) + 6, at_s(11) + 4)
+        place(3, first)
         for n in range(SPLIT_BLOCKS):
-            product(n, 1)
-            place(n, halves[1])
+            product(n, 1, AT_D + 2 * n)
+            place(n, second)
             store(n)
         for n in range(SPLIT_BLOCKS, BLOCKS):
             for half in range(HALVES):
-                product(n, half)
+                product(n, half, (at_s(5), at_s(9), at_s(3) + 4, at_s(2))[n - SPLIT_BLOCKS])
             place(n, whole)
             store(n)

@@ -121,13 +121,14 @@ def tile_list_fibre_equaliser_backward_kernel(
         for k in range(SLICES):
             if k in (0, 3, 7):
                 load_w2((k + 1) // PACK)
+            if k == SLICES - 2:
+                nc.sync.dma_start(idx2[:], offs2)
+                for q in range(4):
+                    nc.sync.dma_start(
+                        w1_s[32 * q : 32 * q + 4 * PASSES, :].bitcast(I32),
+                        w1_scales[:, 4 * q : 4 * q + 4, :].bitcast(I32),
+                    )
             load_s(k)
-        nc.sync.dma_start(idx2[:], offs2)
-        for q in range(4):
-            nc.sync.dma_start(
-                w1_s[32 * q : 32 * q + 4 * PASSES, :].bitcast(I32),
-                w1_scales[:, 4 * q : 4 * q + 4, :].bitcast(I32),
-            )
         nc.sync.dma_start(w1_first[:], w1_rows[:, :, :first_cols])
         nc.sync.dma_start(wgo_sb[:], wgo)
         nc.sync.dma_start(w1_rest[:], w1_rows[:, :, first_cols:])

@@ -28,7 +28,6 @@ PER_COLUMN = 16
 SPLIT_BLOCKS = 4
 FRAMES = 4
 KB = 1024
-BANKS = {"first": (0, 1), "second": (2, 3, 4, 5), "turn": (6, 7)}
 PAIRED = ()
 
 AT_S = 0
@@ -62,12 +61,7 @@ def tile_list_fibre_equaliser_backward_kernel(
         def place_tile(name, shape, dtype, kib):
             return arena.tile(shape, dtype, name=name, tag=name, align_bytes=64, offset=int(kib * KB))
 
-        taken = {kind: [] for kind in BANKS}
-
-        def bank(kind):
-            number = BANKS[kind][len(taken[kind]) % len(BANKS[kind])]
-            taken[kind].append(number)
-            name = "%s%d" % (kind, len(taken[kind]))
+        def bank(name, number):
             return psum.tile([P, HALF], F32, name=name, tag=name, offset=number * 2 * KB)
 
         def at_s(k):
@@ -134,6 +128,7 @@ def tile_list_fibre_equaliser_backward_kernel(
         nc.sync.dma_start(w1_rest[:], w1_rows[:, :, first_cols:])
 
         w2_bf, w2_w, w2_s, h_rows, h_words, h_w, h_s, picked, squares, y_sb = {}, {}, {}, {}, {}, {}, {}, {}, {}, {}
+        d_bank = {}
         whole = slice(0, S)
         halves = [slice(h * HALF, (h + 1) * HALF) for h in range(HALVES)]
 
@@ -161,10 +156,11 @@ def tile_list_fibre_equaliser_backward_kernel(
                 lo = half * HALF - cols.start
                 squares[k, half] = square[:, lo : lo + HALF]
 
-        def first_product(k, half, kind):
+        def first_product(k, half, number):
             a, t = divmod(k, PACK)
             rcols = slice(t * P, (t + 1) * P)
-            d = bank(kind)
+            d = bank("d%d_%d" % (k, half), number)
+            d_bank[k, half] = d
             nc.tensor.matmul_mx(
                 out=d[:],
                 lhsT=w2_w[a][:, rcols].bitcast(E4M3),
@@ -174,18 +170,17 @@ def tile_list_fibre_equaliser_backward_kernel(
                 start=True,
                 stop=True,
             )
-            return d
 
         def rows_h(a, half, kib):
             h_rows[a, half] = place_tile("h_rows%d%d" % (a, half), [P, PACK, HALF], BF16, kib)
 
-        def derivative_vector(k, half, kind):
+        def derivative_vector(k, half):
             a, t = divmod(k, PACK)
-            d = first_product(k, half, kind)
+            d = d_bank[k, half]
             nc.vector.scalar_tensor_tensor(h_rows[a, half][:, t, :], squares[k, half], 1.0, d[:], ALU.subtract, ALU.mult)
 
-        def empty_d(k, half, kind, kib):
-            d = first_product(k, half, kind)
+        def empty_d(k, half, kib):
+            d = d_bank[k, half]
             d_sb = place_tile("d_sb%d_%d" % (k, half), [P, HALF], F32, kib)
             nc.scalar.copy(d_sb[:], d[:])
             return d_sb
@@ -225,16 +220,21 @@ def tile_list_fibre_equaliser_backward_kernel(
         def product(n, half, kib):
             ncols = slice(n * P, (n + 1) * P)
             w1_w = w1_first[:, :, ncols] if n < SPLIT_BLOCKS else w1_rest[:, :, n * P - first_cols : (n + 1) * P - first_cols]
-            y = bank("first" if n < SPLIT_BLOCKS and half == 0 else "second")
-            for a in range(PASSES):
+            if n < SPLIT_BLOCKS:
+                number = ((2, 2, 0, 2), (3, 4, 6, 7))[half][n]
+            else:
+                number = (3, 4, 6, 7)[(2 * n + half) % 4]
+            y = bank("y%d_%d" % (n, half), number)
+            order = ((0, 1, 2), (0, 2, 1))[half]
+            for a in order:
                 nc.tensor.matmul_mx(
                     out=y[:],
                     lhsT=w1_w[:, a, :].bitcast(E4M3),
                     lhsT_scale=w1_s[4 * a :, ncols],
                     rhs=h_w[a, half][:].bitcast(E4M3),
                     rhs_scale=h_s[a, half][:],
-                    start=(a == 0),
-                    stop=(a == PASSES - 1),
+                    start=(a == order[0]),
+                    stop=(a == order[-1]),
                 )
             if n < SPLIT_BLOCKS:
                 y_sb[n] = place_tile("y_sb%d%d" % (n, half), [P, HALF], F32, kib)[:]
@@ -259,13 +259,17 @@ def tile_list_fibre_equaliser_backward_kernel(
         last = SLICES - 1
 
         def half_gpsimd(k, half, d_kib):
-            d_sb = empty_d(k, half, ("first", "second")[half], d_kib)
+            d_sb = empty_d(k, half, d_kib)
             multiply_gpsimd(k, half, less_one_gpsimd(k, half), d_sb)
 
         nc.vector.tensor_copy(v_w[:], tab_w[:].bitcast(U32).indirect(idx[:]))
         nc.vector.tensor_copy(v_s[:], tab_s[:].indirect(idx[:]))
         round_w2(0, AT_W2_BF)
         quantize_w2(0, at_s(0) + 4)
+        for k in range(4):
+            first_product(k, 0, k)
+        for k in (2, 0, 1, 3):
+            first_product(k, 1, (4, 5, 6, 7)[k])
 
         rows_h(0, 0, at_w2(0))
         rows_h(0, 1, at_s(2))
@@ -276,8 +280,8 @@ def tile_list_fibre_equaliser_backward_kernel(
             square_s(k, whole, (AT_SQUARE, AT_PICKED_MORE, AT_PICKED, at_w2(1))[k])
             half_gpsimd(k, 0, (AT_D, AT_D + 2, at_w2(0) + 4, AT_PICKED + 4)[k])
             if k == 2:
-                derivative_vector(0, 1, "second")
-                derivative_vector(1, 1, "second")
+                derivative_vector(0, 1)
+                derivative_vector(1, 1)
             if k >= 2:
                 half_gpsimd(k, 1, (AT_PICKED + 6, AT_PICKED + 8)[k - 2])
 
@@ -290,6 +294,10 @@ def tile_list_fibre_equaliser_backward_kernel(
                 gather_s(k, second, AT_LATE + 4 + 2 * (k - 6))
             if k == 4:
                 quantize_w2(1, at_s(k) + 4)
+                for j in range(4, 8):
+                    first_product(j, 0, j - 4)
+                for j in (4, 5):
+                    first_product(j, 1, j)
             if k == 6:
                 interleave_h(0, 0, AT_TAB + 4)
             if k == 7:
@@ -297,8 +305,8 @@ def tile_list_fibre_equaliser_backward_kernel(
             square_s(k, cols, (AT_PICKED + 12, at_s(0), at_w2(0), at_w2(2))[k - 4])
             half_gpsimd(k, 0, (AT_D + 4, AT_D + 6, AT_LATE, AT_LATE + 2)[k - 4])
             if k == 6:
-                derivative_vector(4, 1, "second")
-                derivative_vector(5, 1, "second")
+                derivative_vector(4, 1)
+                derivative_vector(5, 1)
 
         rows_h(2, 0, at_s(1) + 4)
         for k in range(8, last):
@@ -306,16 +314,23 @@ def tile_list_fibre_equaliser_backward_kernel(
             gather_s(k, second, (at_s(4), at_s(4) + 2, at_s(3) + 4)[k - 8])
             if k == 8:
                 quantize_w2(2, at_s(k))
+                for j in range(8, SLICES):
+                    first_product(j, 0, j - 8)
+                for j in range(8, SLICES):
+                    first_product(j, 1, (6, 7, 4, 5)[j - 8])
             if k == 10:
                 interleave_h(1, 0, at_s(5))
             square_s(k, first, (AT_SMALL, AT_SMALL + 2, at_s(1))[k - 8])
-            half_gpsimd(k, 0, (AT_D, AT_D + 2, AT_D + 4)[k - 8])
-        square_s(8, second, at_s(5) + 4)
+            half_gpsimd(k, 0, (AT_D, AT_D + 2, at_s(5) + 4)[k - 8])
+            if k == 8:
+                square_s(8, second, AT_D + 4)
+        for k in (6, 7):
+            first_product(k, 1, k - 6)
 
         gather_s(last, first, at_s(5) + 6)
         gather_s(last, second, at_s(9) + 4)
         square_s(last, first, AT_SMALL + 6)
-        derivative_vector(last, 0, "first")
+        derivative_vector(last, 0)
         square_s(9, second, at_s(5) + 6)
         square_s(10, second, at_s(4) + 2)
         interleave_h(2, 0, at_s(3) + 4)
@@ -324,7 +339,7 @@ def tile_list_fibre_equaliser_backward_kernel(
         quantize_h(1, 0, at_s(10), AT_SMALL + 6.5)
         rows_h(2, 1, at_s(5))
         for k in range(8, SLICES):
-            derivative_vector(k, 1, "turn")
+            derivative_vector(k, 1)
             if k == 10:
                 quantize_h(2, 0, at_s(10) + 2, at_s(7) + 2.5)
 
@@ -332,18 +347,18 @@ def tile_list_fibre_equaliser_backward_kernel(
         place(0, first)
         for k in (6, 7):
             square_s(k, second, (at_s(9) + 4, AT_LATE + 4)[k - 6])
-            derivative_vector(k, 1, "turn")
+            derivative_vector(k, 1)
         product(1, 0, at_s(11) + 2)
         interleave_h(0, 1, AT_LATE + 6)
         quantize_h(0, 1, at_s(10) + 4, at_s(11))
         place(1, first)
-        product(2, 0, at_s(11) + 4)
         interleave_h(2, 1, at_s(2))
+        product(2, 0, at_s(5))
         quantize_h(2, 1, at_s(7) + 4, at_s(11) + 2)
         place(2, first)
-        interleave_h(1, 1, at_s(5))
+        interleave_h(1, 1, at_s(5) + 2)
         product(3, 0, at_s(6))
-        quantize_h(1, 1, at_s(7) + 6, at_s(11) + 4)
+        quantize_h(1, 1, at_s(7) + 6, at_s(5))
         place(3, first)
         for n in range(SPLIT_BLOCKS):
             product(n, 1, AT_D + 2 * n)
@@ -351,6 +366,6 @@ def tile_list_fibre_equaliser_backward_kernel(
             store(n)
         for n in range(SPLIT_BLOCKS, BLOCKS):
             for half in range(HALVES):
-                product(n, half, (at_s(5), at_s(9), at_s(3) + 4, at_s(2))[n - SPLIT_BLOCKS])
+                product(n, half, (at_s(5) + 2, at_s(9), at_s(3) + 4, at_s(2))[n - SPLIT_BLOCKS])
             place(n, whole)
             store(n)

@@ -28,7 +28,7 @@ PER_COLUMN = 16
 SPLIT_BLOCKS = 4
 FRAMES = 4
 KB = 1024
-PAIRED = ()
+PAIRED = ((0, 0), (1, 0))
 
 AT_S = 0
 AT_W2 = 96

@@ -42,11 +42,11 @@ AT_V_S = 190
 AT_W1_S = 191
 AT_W2_BF = 192
 AT_PICKED_MORE = 196
-AT_LATE = 228
+AT_LATE = 160
 AT_PICKED = 200
 AT_SQUARE = 216
 AT_D = 220
-AT_SMALL = 160
+AT_SMALL = 228
 
 
 def tile_list_fibre_equaliser_backward_kernel(
@@ -221,7 +221,7 @@ def tile_list_fibre_equaliser_backward_kernel(
             ncols = slice(n * P, (n + 1) * P)
             w1_w = w1_first[:, :, ncols] if n < SPLIT_BLOCKS else w1_rest[:, :, n * P - first_cols : (n + 1) * P - first_cols]
             if n < SPLIT_BLOCKS:
-                number = ((2, 2, 0, 2), (3, 4, 6, 7))[half][n]
+                number = ((2, 2, 5, 2), (3, 4, 6, 7))[half][n]
             else:
                 number = (3, 4, 6, 7)[(2 * n + half) % 4]
             y = bank("y%d_%d" % (n, half), number)
@@ -288,10 +288,7 @@ def tile_list_fibre_equaliser_backward_kernel(
         rows_h(1, 0, at_s(1))
         rows_h(1, 1, at_s(6))
         for k in range(4, 8):
-            cols = whole if k < 6 else first
-            gather_s(k, cols, (AT_TAB, AT_TAB + 4, AT_LATE, AT_LATE + 2)[k - 4])
-            if k >= 6:
-                gather_s(k, second, AT_LATE + 4 + 2 * (k - 6))
+            gather_s(k, whole, (AT_TAB, AT_TAB + 4, AT_LATE, AT_LATE + 4)[k - 4])
             if k == 4:
                 quantize_w2(1, at_s(k) + 4)
                 for j in range(4, 8):
@@ -302,8 +299,8 @@ def tile_list_fibre_equaliser_backward_kernel(
                 interleave_h(0, 0, AT_TAB + 4)
             if k == 7:
                 round_w2(2, AT_W2_BF)
-            square_s(k, cols, (AT_PICKED + 12, at_s(0), at_w2(0), at_w2(2))[k - 4])
-            half_gpsimd(k, 0, (AT_D + 4, AT_D + 6, AT_LATE, AT_LATE + 2)[k - 4])
+            square_s(k, whole, (AT_PICKED + 12, at_s(0), at_w2(0), at_w2(2))[k - 4])
+            half_gpsimd(k, 0, (AT_D + 4, AT_D + 6, AT_LATE, AT_LATE + 4)[k - 4])
             if k == 6:
                 derivative_vector(4, 1)
                 derivative_vector(5, 1)
@@ -321,19 +318,21 @@ def tile_list_fibre_equaliser_backward_kernel(
             if k == 10:
                 interleave_h(1, 0, at_s(5))
             square_s(k, first, (AT_SMALL, AT_SMALL + 2, at_s(1))[k - 8])
-            half_gpsimd(k, 0, (AT_D, AT_D + 2, at_s(5) + 4)[k - 8])
+            half_gpsimd(k, 0, (AT_D, AT_D + 2, AT_LATE + 2)[k - 8])
             if k == 8:
                 square_s(8, second, AT_D + 4)
         for k in (6, 7):
             first_product(k, 1, k - 6)
+        d_late = {6: empty_d(6, 1, at_s(5) + 4)}
 
         gather_s(last, first, at_s(5) + 6)
-        gather_s(last, second, at_s(9) + 4)
+        gather_s(last, second, at_s(9))
         square_s(last, first, AT_SMALL + 6)
         derivative_vector(last, 0)
         square_s(9, second, at_s(5) + 6)
         square_s(10, second, at_s(4) + 2)
         interleave_h(2, 0, at_s(3) + 4)
+        d_late[7] = empty_d(7, 1, at_s(1) + 6)
         square_s(11, second, at_s(1) + 4)
         quantize_h(0, 0, at_s(10) + 6, AT_SMALL + 6)
         quantize_h(1, 0, at_s(10), AT_SMALL + 6.5)
@@ -342,14 +341,13 @@ def tile_list_fibre_equaliser_backward_kernel(
             derivative_vector(k, 1)
             if k == 10:
                 quantize_h(2, 0, at_s(10) + 2, at_s(7) + 2.5)
+        for k in (6, 7):
+            multiply_gpsimd(k, 1, less_one_gpsimd(k, 1, AT_LATE + 2 if k == 6 else at_s(5) + 4), d_late[k])
 
         product(0, 0, at_s(11))
         place(0, first)
-        for k in (6, 7):
-            square_s(k, second, (at_s(9) + 4, AT_LATE + 4)[k - 6])
-            derivative_vector(k, 1)
         product(1, 0, at_s(11) + 2)
-        interleave_h(0, 1, AT_LATE + 6)
+        interleave_h(0, 1, at_s(9))
         quantize_h(0, 1, at_s(10) + 4, at_s(11))
         place(1, first)
         interleave_h(2, 1, at_s(2))

@@ -62,7 +62,7 @@ def tile_list_fibre_equaliser_backward_kernel(
             return arena.tile(shape, dtype, name=name, tag=name, align_bytes=64, offset=int(kib * KB))
 
         def bank(name, number):
-            return psum.tile([P, HALF], F32, name=name, tag=name, offset=number * 2 * KB)
+            return psum.tile([P, HALF], F32, name=name, tag="bank%d" % number)
 
         def at_s(k):
             return AT_S + 8 * k
@@ -223,7 +223,7 @@ def tile_list_fibre_equaliser_backward_kernel(
             if n < SPLIT_BLOCKS:
                 number = ((2, 2, 5, 2), (3, 4, 6, 7))[half][n]
             else:
-                number = (3, 4, 6, 7)[(2 * n + half) % 4]
+                number = (5, n % 2)[half]
             y = bank("y%d_%d" % (n, half), number)
             order = ((0, 1, 2), (0, 2, 1))[half]
             for a in order:
@@ -268,7 +268,7 @@ def tile_list_fibre_equaliser_backward_kernel(
         quantize_w2(0, at_s(0) + 4)
         for k in range(4):
             first_product(k, 0, k)
-        for k in (2, 0, 1, 3):
+        for k in range(4):
             first_product(k, 1, (4, 5, 6, 7)[k])
 
         rows_h(0, 0, at_w2(0))
@@ -278,12 +278,12 @@ def tile_list_fibre_equaliser_backward_kernel(
             if k == 3:
                 round_w2(1, AT_W2_BF)
             square_s(k, whole, (AT_SQUARE, AT_PICKED_MORE, AT_PICKED, at_w2(1))[k])
-            half_gpsimd(k, 0, (AT_D, AT_D + 2, at_w2(0) + 4, AT_PICKED + 4)[k])
+            half_gpsimd(k, 0, (AT_D, AT_D + 2, AT_PICKED + 8, AT_PICKED + 12)[k])
             if k == 2:
                 derivative_vector(0, 1)
                 derivative_vector(1, 1)
             if k >= 2:
-                half_gpsimd(k, 1, (AT_PICKED + 6, AT_PICKED + 8)[k - 2])
+                half_gpsimd(k, 1, AT_PICKED + 4 * k + 2)
 
         rows_h(1, 0, at_s(1))
         rows_h(1, 1, at_s(6))
@@ -299,7 +299,7 @@ def tile_list_fibre_equaliser_backward_kernel(
                 interleave_h(0, 0, AT_TAB + 4)
             if k == 7:
                 round_w2(2, AT_W2_BF)
-            square_s(k, whole, (AT_PICKED + 12, at_s(0), at_w2(0), at_w2(2))[k - 4])
+            square_s(k, whole, (AT_PICKED + 4, at_s(0), at_w2(0), at_w2(2))[k - 4])
             half_gpsimd(k, 0, (AT_D + 4, AT_D + 6, AT_LATE, AT_LATE + 4)[k - 4])
             if k == 6:
                 derivative_vector(4, 1)

@@ -42,11 +42,11 @@ AT_V_S = 190
 AT_W1_S = 191
 AT_W2_BF = 192
 AT_PICKED_MORE = 196
-AT_LATE = 160
+AT_LATE = 228
 AT_PICKED = 200
 AT_SQUARE = 216
 AT_D = 220
-AT_SMALL = 228
+AT_SMALL = 160
 
 
 def tile_list_fibre_equaliser_backward_kernel(
@@ -115,14 +115,13 @@ def tile_list_fibre_equaliser_backward_kernel(
         for k in range(SLICES):
             if k in (0, 3, 7):
                 load_w2((k + 1) // PACK)
-            if k == SLICES - 2:
-                nc.sync.dma_start(idx2[:], offs2)
-                for q in range(4):
-                    nc.sync.dma_start(
-                        w1_s[32 * q : 32 * q + 4 * PASSES, :].bitcast(I32),
-                        w1_scales[:, 4 * q : 4 * q + 4, :].bitcast(I32),
-                    )
             load_s(k)
+        nc.sync.dma_start(idx2[:], offs2)
+        for q in range(4):
+            nc.sync.dma_start(
+                w1_s[32 * q : 32 * q + 4 * PASSES, :].bitcast(I32),
+                w1_scales[:, 4 * q : 4 * q + 4, :].bitcast(I32),
+            )
         nc.sync.dma_start(w1_first[:], w1_rows[:, :, :first_cols])
         nc.sync.dma_start(wgo_sb[:], wgo)
         nc.sync.dma_start(w1_rest[:], w1_rows[:, :, first_cols:])
@@ -195,7 +194,7 @@ def tile_list_fibre_equaliser_backward_kernel(
             nc.gpsimd.tensor_tensor(target, factor, d_sb[:], ALU.mult)
 
         def less_one_gpsimd(k, half, kib=None):
-            factor = squares[k, half] if kib is None else place_tile("factor%d" % k, [P, HALF], F32, kib)[:]
+            factor = squares[k, half] if kib is None else place_tile("factor%d_%d" % (k, half), [P, HALF], F32, kib)[:]
             nc.gpsimd.tensor_scalar(factor, squares[k, half], 1.0, -1.0, ALU.mult, ALU.add)
             return factor
 
@@ -221,9 +220,9 @@ def tile_list_fibre_equaliser_backward_kernel(
             ncols = slice(n * P, (n + 1) * P)
             w1_w = w1_first[:, :, ncols] if n < SPLIT_BLOCKS else w1_rest[:, :, n * P - first_cols : (n + 1) * P - first_cols]
             if n < SPLIT_BLOCKS:
-                number = ((2, 2, 5, 2), (3, 4, 6, 7))[half][n]
+                number = ((2, 2, 0, 2), (3, 4, 6, 7))[half][n]
             else:
-                number = (5, n % 2)[half]
+                number = (3, 4, 6, 7)[(2 * n + half) % 4]
             y = bank("y%d_%d" % (n, half), number)
             order = ((0, 1, 2), (0, 2, 1))[half]
             for a in order:
@@ -243,10 +242,7 @@ def tile_list_fibre_equaliser_backward_kernel(
                 if half == 0:
                     y_sb[n] = place_tile("y_sb%d" % n, [P, S], F32, kib)[:]
                 target = y_sb[n][:, halves[half]]
-            if (n, half) == (0, 0):
-                nc.vector.tensor_scalar_mul(target, y[:], -1.0)
-            else:
-                nc.scalar.activation(target, y[:], ACT.Copy, scale=-1.0)
+            nc.scalar.activation(target, y[:], ACT.Copy, scale=-1.0)
 
         def place(n, cols):
             window = frames[n % FRAMES][:].indirect(listed(idx2, cols))
@@ -258,9 +254,19 @@ def tile_list_fibre_equaliser_backward_kernel(
         first, second = halves
         last = SLICES - 1
 
+        waiting = []
+
         def half_gpsimd(k, half, d_kib):
             d_sb = empty_d(k, half, d_kib)
-            multiply_gpsimd(k, half, less_one_gpsimd(k, half), d_sb)
+            if k in (3, 7):
+                waiting.append((k, half, d_sb))
+            else:
+                multiply_gpsimd(k, half, less_one_gpsimd(k, half, AT_W2_BF + 2 if k == 8 else None), d_sb)
+
+        def waiting_gpsimd():
+            for k, half, d_sb in waiting:
+                multiply_gpsimd(k, half, less_one_gpsimd(k, half, AT_W2_BF + 2 * half), d_sb)
+            waiting.clear()
 
         nc.vector.tensor_copy(v_w[:], tab_w[:].bitcast(U32).indirect(idx[:]))
         nc.vector.tensor_copy(v_s[:], tab_s[:].indirect(idx[:]))
@@ -268,8 +274,8 @@ def tile_list_fibre_equaliser_backward_kernel(
         quantize_w2(0, at_s(0) + 4)
         for k in range(4):
             first_product(k, 0, k)
-        for k in range(4):
-            first_product(k, 1, (4, 5, 6, 7)[k])
+        for k in range(3):
+            first_product(k, 1, 4 + k)
 
         rows_h(0, 0, at_w2(0))
         rows_h(0, 1, at_s(2))
@@ -282,15 +288,18 @@ def tile_list_fibre_equaliser_backward_kernel(
             if k == 2:
                 derivative_vector(0, 1)
                 derivative_vector(1, 1)
-            if k >= 2:
                 half_gpsimd(k, 1, AT_PICKED + 4 * k + 2)
 
         rows_h(1, 0, at_s(1))
         rows_h(1, 1, at_s(6))
         for k in range(4, 8):
-            gather_s(k, whole, (AT_TAB, AT_TAB + 4, AT_LATE, AT_LATE + 4)[k - 4])
+            cols = whole if k < 6 else first
+            gather_s(k, cols, (AT_TAB, AT_TAB + 4, AT_LATE, AT_LATE + 2)[k - 4])
+            if k >= 6:
+                gather_s(k, second, AT_LATE + 4 + 2 * (k - 6))
             if k == 4:
                 quantize_w2(1, at_s(k) + 4)
+                waiting_gpsimd()
                 for j in range(4, 8):
                     first_product(j, 0, j - 4)
                 for j in (4, 5):
@@ -299,8 +308,8 @@ def tile_list_fibre_equaliser_backward_kernel(
                 interleave_h(0, 0, AT_TAB + 4)
             if k == 7:
                 round_w2(2, AT_W2_BF)
-            square_s(k, whole, (AT_PICKED + 4, at_s(0), at_w2(0), at_w2(2))[k - 4])
-            half_gpsimd(k, 0, (AT_D + 4, AT_D + 6, AT_LATE, AT_LATE + 4)[k - 4])
+            square_s(k, cols, (AT_PICKED + 4, at_s(0), at_w2(0), at_w2(2))[k - 4])
+            half_gpsimd(k, 0, (AT_D + 4, AT_D + 6, AT_LATE, AT_LATE + 2)[k - 4])
             if k == 6:
                 derivative_vector(4, 1)
                 derivative_vector(5, 1)
@@ -311,6 +320,7 @@ def tile_list_fibre_equaliser_backward_kernel(
             gather_s(k, second, (at_s(4), at_s(4) + 2, at_s(3) + 4)[k - 8])
             if k == 8:
                 quantize_w2(2, at_s(k))
+                waiting_gpsimd()
                 for j in range(8, SLICES):
                     first_product(j, 0, j - 8)
                 for j in range(8, SLICES):
@@ -318,45 +328,48 @@ def tile_list_fibre_equaliser_backward_kernel(
             if k == 10:
                 interleave_h(1, 0, at_s(5))
             square_s(k, first, (AT_SMALL, AT_SMALL + 2, at_s(1))[k - 8])
-            half_gpsimd(k, 0, (AT_D, AT_D + 2, AT_LATE + 2)[k - 8])
+            half_gpsimd(k, 0, (AT_D, AT_D + 2, at_s(5) + 4)[k - 8])
             if k == 8:
                 square_s(8, second, AT_D + 4)
         for k in (6, 7):
             first_product(k, 1, k - 6)
-        d_late = {6: empty_d(6, 1, at_s(5) + 4)}
 
         gather_s(last, first, at_s(5) + 6)
-        gather_s(last, second, at_s(9))
-        square_s(last, first, AT_SMALL + 6)
+        gather_s(last, second, at_s(9) + 4)
+        square_s(last, first, at_s(3))
         derivative_vector(last, 0)
         square_s(9, second, at_s(5) + 6)
         square_s(10, second, at_s(4) + 2)
         interleave_h(2, 0, at_s(3) + 4)
-        d_late[7] = empty_d(7, 1, at_s(1) + 6)
         square_s(11, second, at_s(1) + 4)
-        quantize_h(0, 0, at_s(10) + 6, AT_SMALL + 6)
-        quantize_h(1, 0, at_s(10), AT_SMALL + 6.5)
-        rows_h(2, 1, at_s(5))
+        rows_h(2, 1, at_s(3))
         for k in range(8, SLICES):
             derivative_vector(k, 1)
+            if k == 8:
+                first_product(3, 1, 6)
+            if k == 9:
+                quantize_h(0, 0, at_s(10) + 6, at_s(5) + 6)
+                quantize_h(1, 0, at_s(10), at_s(5) + 6.5)
             if k == 10:
                 quantize_h(2, 0, at_s(10) + 2, at_s(7) + 2.5)
-        for k in (6, 7):
-            multiply_gpsimd(k, 1, less_one_gpsimd(k, 1, AT_LATE + 2 if k == 6 else at_s(5) + 4), d_late[k])
 
+        derivative_vector(3, 1)
         product(0, 0, at_s(11))
         place(0, first)
+        for k in (6, 7):
+            square_s(k, second, (at_s(9) + 4, AT_LATE + 4)[k - 6])
+            derivative_vector(k, 1)
         product(1, 0, at_s(11) + 2)
-        interleave_h(0, 1, at_s(9))
+        interleave_h(0, 1, AT_LATE + 6)
         quantize_h(0, 1, at_s(10) + 4, at_s(11))
         place(1, first)
         interleave_h(2, 1, at_s(2))
-        product(2, 0, at_s(5))
+        product(2, 0, at_s(3))
         quantize_h(2, 1, at_s(7) + 4, at_s(11) + 2)
         place(2, first)
-        interleave_h(1, 1, at_s(5) + 2)
+        interleave_h(1, 1, at_s(3) + 2)
         product(3, 0, at_s(6))
-        quantize_h(1, 1, at_s(7) + 6, at_s(5))
+        quantize_h(1, 1, at_s(7) + 6, at_s(3))
         place(3, first)
         for n in range(SPLIT_BLOCKS):
             product(n, 1, AT_D + 2 * n)
@@ -364,6 +377,6 @@ def tile_list_fibre_equaliser_backward_kernel(
             store(n)
         for n in range(SPLIT_BLOCKS, BLOCKS):
             for half in range(HALVES):
-                product(n, half, (at_s(5) + 2, at_s(9), at_s(3) + 4, at_s(2))[n - SPLIT_BLOCKS])
+                product(n, half, (at_s(3) + 2, at_s(9), at_s(5), at_s(2))[n - SPLIT_BLOCKS])
             place(n, whole)
             store(n)

@@ -27,6 +27,7 @@ BLOCKS = N // P
 PER_COLUMN = 16
 SPLIT_BLOCKS = 4
 FRAMES = 4
+FIRST_BLOCKS = 2
 KB = 1024
 PAIRED = ((0, 0), (1, 0))
 
@@ -76,7 +77,7 @@ def tile_list_fibre_equaliser_backward_kernel(
         tab_s = place_tile("tab_s", [P, T], U8, AT_TAB_S)
         v_w = place_tile("v_w", [P, S], U32, AT_V_W)
         v_s = place_tile("v_s", [P, S], U8, AT_V_S)
-        first_cols = SPLIT_BLOCKS * P
+        first_cols = FIRST_BLOCKS * P
         w1_first = place_tile("w1_first", [P, PASSES, first_cols], I32, AT_W1)
         w1_rest = place_tile("w1_rest", [P, PASSES, N - first_cols], I32, AT_W1 + PASSES * first_cols * 4 / KB)
         w1_s = place_tile("w1_s", [P, N], U8, AT_W1_S)
@@ -116,7 +117,6 @@ def tile_list_fibre_equaliser_backward_kernel(
             if k in (0, 3, 7):
                 load_w2((k + 1) // PACK)
             load_s(k)
-        nc.sync.dma_start(idx2[:], offs2)
         for q in range(4):
             nc.sync.dma_start(
                 w1_s[32 * q : 32 * q + 4 * PASSES, :].bitcast(I32),
@@ -124,6 +124,7 @@ def tile_list_fibre_equaliser_backward_kernel(
             )
         nc.sync.dma_start(w1_first[:], w1_rows[:, :, :first_cols])
         nc.sync.dma_start(wgo_sb[:], wgo)
+        nc.sync.dma_start(idx2[:], offs2)
         nc.sync.dma_start(w1_rest[:], w1_rows[:, :, first_cols:])
 
         w2_bf, w2_w, w2_s, h_rows, h_words, h_w, h_s, picked, squares, y_sb = {}, {}, {}, {}, {}, {}, {}, {}, {}, {}
@@ -138,9 +139,9 @@ def tile_list_fibre_equaliser_backward_kernel(
                 w2_raw[a][:].rearrange("p j (m t) -> p m j t", t=PACK),
             )
 
-        def quantize_w2(a, kib):
-            w2_w[a] = place_tile("w2_w%d" % a, [P, PASS], U32, kib)
-            w2_s[a] = place_tile("w2_s%d" % a, [P, PASS], U8, kib + 2)
+        def quantize_w2(a, codes_kib, scales_kib):
+            w2_w[a] = place_tile("w2_w%d" % a, [P, PASS], U32, codes_kib)
+            w2_s[a] = place_tile("w2_s%d" % a, [P, PASS], U8, scales_kib)
             nc.vector.quantize_mx(out=w2_w[a][:].bitcast(E4M3), scales=w2_s[a][:], in_=w2_bf[a][:])
 
         def gather_s(k, cols, kib):
@@ -218,7 +219,7 @@ def tile_list_fibre_equaliser_backward_kernel(
 
         def product(n, half, kib):
             ncols = slice(n * P, (n + 1) * P)
-            w1_w = w1_first[:, :, ncols] if n < SPLIT_BLOCKS else w1_rest[:, :, n * P - first_cols : (n + 1) * P - first_cols]
+            w1_w = w1_first[:, :, ncols] if n < FIRST_BLOCKS else w1_rest[:, :, n * P - first_cols : (n + 1) * P - first_cols]
             if n < SPLIT_BLOCKS:
                 number = ((2, 2, 0, 2), (3, 4, 6, 7))[half][n]
             else:
@@ -261,7 +262,7 @@ def tile_list_fibre_equaliser_backward_kernel(
             if k in (3, 7):
                 waiting.append((k, half, d_sb))
             else:
-                multiply_gpsimd(k, half, less_one_gpsimd(k, half, AT_W2_BF + 2 if k == 8 else None), d_sb)
+                multiply_gpsimd(k, half, less_one_gpsimd(k, half, {4: AT_PICKED + 12, 8: AT_W2_BF + 2}.get(k)), d_sb)
 
         def waiting_gpsimd():
             for k, half, d_sb in waiting:
@@ -271,10 +272,10 @@ def tile_list_fibre_equaliser_backward_kernel(
         nc.vector.tensor_copy(v_w[:], tab_w[:].bitcast(U32).indirect(idx[:]))
         nc.vector.tensor_copy(v_s[:], tab_s[:].indirect(idx[:]))
         round_w2(0, AT_W2_BF)
-        quantize_w2(0, at_s(0) + 4)
+        quantize_w2(0, AT_SMALL + 4, AT_LATE + 8)
         for k in range(4):
             first_product(k, 0, k)
-        for k in range(3):
+        for k in range(4):
             first_product(k, 1, 4 + k)
 
         rows_h(0, 0, at_w2(0))
@@ -289,6 +290,7 @@ def tile_list_fibre_equaliser_backward_kernel(
                 derivative_vector(0, 1)
                 derivative_vector(1, 1)
                 half_gpsimd(k, 1, AT_PICKED + 4 * k + 2)
+        d_late = empty_d(3, 1, AT_PICKED + 14)
 
         rows_h(1, 0, at_s(1))
         rows_h(1, 1, at_s(6))
@@ -298,7 +300,7 @@ def tile_list_fibre_equaliser_backward_kernel(
             if k >= 6:
                 gather_s(k, second, AT_LATE + 4 + 2 * (k - 6))
             if k == 4:
-                quantize_w2(1, at_s(k) + 4)
+                quantize_w2(1, at_s(k) + 4, at_s(k) + 6)
                 waiting_gpsimd()
                 for j in range(4, 8):
                     first_product(j, 0, j - 4)
@@ -316,60 +318,56 @@ def tile_list_fibre_equaliser_backward_kernel(
 
         rows_h(2, 0, at_s(1) + 4)
         for k in range(8, last):
-            gather_s(k, first, at_s(5) + 2 * (k - 8))
+            gather_s(k, first, (at_s(5), at_s(5) + 4, at_s(7))[k - 8])
             gather_s(k, second, (at_s(4), at_s(4) + 2, at_s(3) + 4)[k - 8])
+            square_s(k, first, (AT_SMALL, AT_SMALL + 2, AT_SMALL + 6)[k - 8])
             if k == 8:
-                quantize_w2(2, at_s(k))
+                quantize_w2(2, at_s(8) + 6, at_s(5) + 2)
                 waiting_gpsimd()
                 for j in range(8, SLICES):
                     first_product(j, 0, j - 8)
                 for j in range(8, SLICES):
                     first_product(j, 1, (6, 7, 4, 5)[j - 8])
-            if k == 10:
-                interleave_h(1, 0, at_s(5))
-            square_s(k, first, (AT_SMALL, AT_SMALL + 2, at_s(1))[k - 8])
-            half_gpsimd(k, 0, (AT_D, AT_D + 2, at_s(5) + 4)[k - 8])
-            if k == 8:
-                square_s(8, second, AT_D + 4)
+            if k < 10:
+                half_gpsimd(k, 0, AT_D + 2 * (k - 8))
+            else:
+                derivative_vector(k, 0)
+                interleave_h(1, 0, at_s(7))
+            square_s(k, second, (at_s(8), at_s(8) + 2, at_s(8) + 4)[k - 8])
+        multiply_gpsimd(3, 1, less_one_gpsimd(3, 1, AT_D + 2), d_late)
         for k in (6, 7):
             first_product(k, 1, k - 6)
 
-        gather_s(last, first, at_s(5) + 6)
+        gather_s(last, first, at_s(3))
         gather_s(last, second, at_s(9) + 4)
-        square_s(last, first, at_s(3))
+        square_s(last, first, at_s(5) + 6)
         derivative_vector(last, 0)
-        square_s(9, second, at_s(5) + 6)
-        square_s(10, second, at_s(4) + 2)
         interleave_h(2, 0, at_s(3) + 4)
         square_s(11, second, at_s(1) + 4)
         rows_h(2, 1, at_s(3))
         for k in range(8, SLICES):
             derivative_vector(k, 1)
-            if k == 8:
-                first_product(3, 1, 6)
-            if k == 9:
-                quantize_h(0, 0, at_s(10) + 6, at_s(5) + 6)
-                quantize_h(1, 0, at_s(10), at_s(5) + 6.5)
             if k == 10:
+                quantize_h(0, 0, at_s(10) + 6, at_s(8) + 2)
+                quantize_h(1, 0, at_s(10), at_s(8) + 2.5)
                 quantize_h(2, 0, at_s(10) + 2, at_s(7) + 2.5)
 
-        derivative_vector(3, 1)
+        for k in (6, 7):
+            square_s(k, second, (at_s(9) + 4, at_s(1) + 6)[k - 6])
+            derivative_vector(k, 1)
         product(0, 0, at_s(11))
         place(0, first)
-        for k in (6, 7):
-            square_s(k, second, (at_s(9) + 4, AT_LATE + 4)[k - 6])
-            derivative_vector(k, 1)
         product(1, 0, at_s(11) + 2)
-        interleave_h(0, 1, AT_LATE + 6)
-        quantize_h(0, 1, at_s(10) + 4, at_s(11))
+        interleave_h(0, 1, AT_LATE + 4)
+        quantize_h(0, 1, at_s(10) + 4, at_s(8) + 1)
         place(1, first)
         interleave_h(2, 1, at_s(2))
         product(2, 0, at_s(3))
-        quantize_h(2, 1, at_s(7) + 4, at_s(11) + 2)
+        quantize_h(2, 1, at_s(7) + 4, at_s(8) + 1.5)
         place(2, first)
         interleave_h(1, 1, at_s(3) + 2)
         product(3, 0, at_s(6))
-        quantize_h(1, 1, at_s(7) + 6, at_s(3))
+        quantize_h(1, 1, at_s(7) + 6, at_s(7) + 3)
         place(3, first)
         for n in range(SPLIT_BLOCKS):
             product(n, 1, AT_D + 2 * n)
@@ -377,6 +375,6 @@ def tile_list_fibre_equaliser_backward_kernel(
             store(n)
         for n in range(SPLIT_BLOCKS, BLOCKS):
             for half in range(HALVES):
-                product(n, half, (at_s(3) + 2, at_s(9), at_s(5), at_s(2))[n - SPLIT_BLOCKS])
+                product(n, half, (at_s(3) + 2, at_s(9), at_s(11) + 4, at_s(2))[n - SPLIT_BLOCKS])
             place(n, whole)
             store(n)

@@ -22,16 +22,15 @@ PASS = P * PACK
 PASSES = H // PASS
 SLICES = PASSES * PACK
 HALF = 512
-HALVES = S // HALF
 BLOCKS = N // P
 PER_COLUMN = 16
-SPLIT_BLOCKS = 4
-FRAMES = 4
+UNIT = 128
+UNITS = S // UNIT
+FRAMES = 5
+EARLY_FRAMES = 3
 FIRST_BLOCKS = 2
 KB = 1024
-PAIRED = ((0, 0), (1, 0))
 
-AT_S = 0
 AT_W2 = 96
 AT_TAB = 120
 AT_FRAME = 128
@@ -41,13 +40,7 @@ AT_TAB_S = 184
 AT_V_W = 186
 AT_V_S = 190
 AT_W1_S = 191
-AT_W2_BF = 192
-AT_PICKED_MORE = 196
-AT_LATE = 228
-AT_PICKED = 200
-AT_SQUARE = 216
-AT_D = 220
-AT_SMALL = 160
+AT_FREE = 192
 
 
 def tile_list_fibre_equaliser_backward_kernel(
@@ -66,7 +59,7 @@ def tile_list_fibre_equaliser_backward_kernel(
             return psum.tile([P, HALF], F32, name=name, tag="bank%d" % number)
 
         def at_s(k):
-            return AT_S + 8 * k
+            return 8 * k
 
         def at_w2(a):
             return AT_W2 + 8 * a
@@ -89,7 +82,7 @@ def tile_list_fibre_equaliser_backward_kernel(
 
         nc.gpsimd.memset(tab_s[:].bitcast(I32), 0)
         nc.gpsimd.memset(w1_s[:].bitcast(I32), 0)
-        for frame in frames:
+        for frame in frames[:EARLY_FRAMES]:
             nc.gpsimd.memset(frame[:], 0.0)
 
         s_rows = sT.rearrange("(a p t) c -> a p t c", p=P, t=PACK)
@@ -113,9 +106,10 @@ def tile_list_fibre_equaliser_backward_kernel(
             nc.sync.dma_start(
                 tab_s[32 * q : 32 * q + 4, :].bitcast(I32), tab_scales[0, 4 * q : 4 * q + 4, :].bitcast(I32)
             )
+        w2_before = {0: 0, 5: 1, 11: 2}
         for k in range(SLICES):
-            if k in (0, 3, 7):
-                load_w2((k + 1) // PACK)
+            if k in w2_before:
+                load_w2(w2_before[k])
             load_s(k)
         for q in range(4):
             nc.sync.dma_start(
@@ -127,254 +121,267 @@ def tile_list_fibre_equaliser_backward_kernel(
         nc.sync.dma_start(idx2[:], offs2)
         nc.sync.dma_start(w1_rest[:], w1_rows[:, :, first_cols:])
 
-        w2_bf, w2_w, w2_s, h_rows, h_words, h_w, h_s, picked, squares, y_sb = {}, {}, {}, {}, {}, {}, {}, {}, {}, {}
-        d_bank = {}
+        w2_bf, w2_w, w2_s, h_bf, h_w, h_s, picked, factor, d_sb, d_bank, y_bank, y_sb = ({} for i in range(12))
         whole = slice(0, S)
-        halves = [slice(h * HALF, (h + 1) * HALF) for h in range(HALVES)]
+        halves = [slice(0, HALF), slice(HALF, S)]
+        first, second = halves
 
-        def round_w2(a, kib):
+        def round_w2(a, kib, shared=False):
             w2_bf[a] = place_tile("w2_bf%d" % a, [P, PASS * PACK], BF16, kib)
-            nc.scalar.copy(
-                w2_bf[a][:].rearrange("p (t m j) -> p m j t", t=PACK, j=PACK),
-                w2_raw[a][:].rearrange("p j (m t) -> p m j t", t=PACK),
-            )
+            rounded = w2_bf[a][:].rearrange("p (t m j) -> p m j t", t=PACK, j=PACK)
+            raw = w2_raw[a][:].rearrange("p j (m t) -> p m j t", t=PACK)
+            if shared:
+                nc.scalar.copy(rounded[:, :, :, :2], raw[:, :, :, :2])
+                nc.vector.tensor_copy(rounded[:, :, :, 2:], raw[:, :, :, 2:])
+            else:
+                nc.scalar.copy(rounded, raw)
 
-        def quantize_w2(a, codes_kib, scales_kib):
-            w2_w[a] = place_tile("w2_w%d" % a, [P, PASS], U32, codes_kib)
-            w2_s[a] = place_tile("w2_s%d" % a, [P, PASS], U8, scales_kib)
+        def quantize_w2(a, kib):
+            w2_w[a] = place_tile("w2_w%d" % a, [P, PASS], U32, kib)
+            w2_s[a] = place_tile("w2_s%d" % a, [P, PASS], U8, kib + 2)
             nc.vector.quantize_mx(out=w2_w[a][:].bitcast(E4M3), scales=w2_s[a][:], in_=w2_bf[a][:])
 
-        def gather_s(k, cols, kib):
-            tile = place_tile("picked%d_%d" % (k, cols.start), [P, cols.stop - cols.start], F32, kib)
-            nc.vector.tensor_copy(tile[:], s_sb[k].indirect(listed(idx, cols)))
-            picked[k, cols.start] = tile
+        def place_picked(a, kibs):
+            for half in range(2):
+                picked[a, half] = place_tile("picked%d%d" % (a, half), [P, PACK, HALF], F32, kibs[half])
 
-        def square_s(k, cols, kib):
-            square = place_tile("square%d_%d" % (k, cols.start), [P, cols.stop - cols.start], F32, kib)
-            nc.scalar.activation(square[:], picked[k, cols.start][:], ACT.Square)
-            for half in range(cols.start // HALF, cols.stop // HALF):
-                lo = half * HALF - cols.start
-                squares[k, half] = square[:, lo : lo + HALF]
-
-        def first_product(k, half, number):
+        def gather_s(k):
             a, t = divmod(k, PACK)
-            rcols = slice(t * P, (t + 1) * P)
-            d = bank("d%d_%d" % (k, half), number)
-            d_bank[k, half] = d
-            nc.tensor.matmul_mx(
-                out=d[:],
-                lhsT=w2_w[a][:, rcols].bitcast(E4M3),
-                lhsT_scale=w2_s[a][:, rcols],
-                rhs=v_w[:, halves[half]].bitcast(E5M2),
-                rhs_scale=v_s[:, halves[half]],
-                start=True,
-                stop=True,
-            )
+            for half in range(2):
+                nc.vector.tensor_copy(picked[a, half][:, t, :], s_sb[k].indirect(listed(idx, halves[half])))
 
-        def rows_h(a, half, kib):
-            h_rows[a, half] = place_tile("h_rows%d%d" % (a, half), [P, PACK, HALF], BF16, kib)
-
-        def derivative_vector(k, half):
-            a, t = divmod(k, PACK)
-            d = d_bank[k, half]
-            nc.vector.scalar_tensor_tensor(h_rows[a, half][:, t, :], squares[k, half], 1.0, d[:], ALU.subtract, ALU.mult)
-
-        def empty_d(k, half, kib):
-            d = d_bank[k, half]
-            d_sb = place_tile("d_sb%d_%d" % (k, half), [P, HALF], F32, kib)
-            nc.scalar.copy(d_sb[:], d[:])
-            return d_sb
-
-        def multiply_gpsimd(k, half, factor, d_sb):
-            a, t = divmod(k, PACK)
-            if (a, half) in PAIRED:
-                pairs = h_rows[a, half][:].rearrange("p (u x) c -> p u (x c)", u=2).rearrange("p u (c e) -> p u c e", e=2)
-                target = pairs[:, t // 2, :, t % 2]
-            else:
-                target = h_rows[a, half][:, t, :]
-            nc.gpsimd.tensor_tensor(target, factor, d_sb[:], ALU.mult)
-
-        def less_one_gpsimd(k, half, kib=None):
-            factor = squares[k, half] if kib is None else place_tile("factor%d_%d" % (k, half), [P, HALF], F32, kib)[:]
-            nc.gpsimd.tensor_scalar(factor, squares[k, half], 1.0, -1.0, ALU.mult, ALU.add)
-            return factor
-
-        def interleave_h(a, half, kib):
-            h_words[a, half] = place_tile("h_words%d%d" % (a, half), [P, HALF * PACK], BF16, kib)
-            if (a, half) in PAIRED:
-                nc.scalar.copy(
-                    h_words[a, half][:].bitcast(U32).rearrange("p (c u) -> p c u", u=2),
-                    h_rows[a, half][:].rearrange("p t c -> p (t c)").bitcast(U32).rearrange("p (u c) -> p c u", u=2),
+        def first_product(a, u, number):
+            d_bank[a, u] = bank("d%d_%d" % (a, u), number)
+            cols = slice(u * UNIT, (u + 1) * UNIT)
+            for t in range(PACK):
+                rows = slice(t * P, (t + 1) * P)
+                nc.tensor.matmul_mx(
+                    out=d_bank[a, u][:, t * UNIT : (t + 1) * UNIT],
+                    lhsT=w2_w[a][:, rows].bitcast(E4M3),
+                    lhsT_scale=w2_s[a][:, rows],
+                    rhs=v_w[:, cols].bitcast(E5M2),
+                    rhs_scale=v_s[:, cols],
+                    start=True,
+                    stop=True,
                 )
-                return
-            nc.scalar.copy(
-                h_words[a, half][:].rearrange("p (c i t) -> p c t i", i=4, t=PACK),
-                h_rows[a, half][:].rearrange("p t (c i) -> p c t i", i=4),
+
+        def square(a, u, count, kib):
+            tile = place_tile("sq%d_%d" % (a, u), [P, count * HALF], F32, kib)
+            lo = u % 4 * UNIT
+            nc.scalar.activation(
+                tile[:].rearrange("p (c i t) -> p c t i", i=4, t=PACK),
+                picked[a, u // 4][:, :, lo : lo + count * UNIT].rearrange("p t (c i) -> p c t i", i=4),
+                ACT.Square,
+            )
+            factor[a, u] = tile
+
+        def empty_d(a, u, kib):
+            d_sb[a, u] = place_tile("d_sb%d_%d" % (a, u), [P, 2 * HALF], F32, kib)
+            for e in range(2):
+                nc.scalar.copy(
+                    d_sb[a, u][:, e * HALF : (e + 1) * HALF].rearrange("p (c t) -> p c t", t=PACK),
+                    d_bank[a, u + e][:].rearrange("p (t c) -> p c t", t=PACK),
+                )
+
+        def less_one_scalar(a, u):
+            nc.scalar.activation(factor[a, u][:], factor[a, u][:], ACT.Copy, bias=-1.0)
+
+        def less_one_gpsimd(a, u, kib=None):
+            squares = factor[a, u]
+            if kib is not None:
+                factor[a, u] = place_tile("f%d_%d" % (a, u), [P, 2 * HALF], F32, kib)
+            nc.gpsimd.tensor_scalar(factor[a, u][:], squares[:], 1.0, -1.0, ALU.mult, ALU.add)
+
+        def h_cols(a, u, count):
+            return h_bf[a, u // 4][:, u % 4 * HALF : (u % 4 + count) * HALF]
+
+        def multiply_gpsimd(a, u, e=0, count=2):
+            cols = slice(e * HALF, (e + count) * HALF)
+            nc.gpsimd.tensor_tensor(h_cols(a, u + e, count), factor[a, u][:, cols], d_sb[a, u][:, cols], ALU.mult)
+
+        def multiply_vector(a, u, e=0):
+            nc.vector.scalar_tensor_tensor(
+                h_cols(a, u + e, 1).rearrange("p (c t) -> p c t", t=PACK),
+                factor[a, u][:, e * HALF : (e + 1) * HALF].rearrange("p (c t) -> p c t", t=PACK),
+                1.0,
+                d_bank[a, u + e][:].rearrange("p (t c) -> p c t", t=PACK),
+                ALU.subtract,
+                ALU.mult,
             )
 
-        def quantize_h(a, half, codes_kib, scales_kib):
-            h_w[a, half] = place_tile("h_w%d%d" % (a, half), [P, HALF], U32, codes_kib)
-            h_s[a, half] = place_tile("h_s%d%d" % (a, half), [P, HALF], U8, scales_kib)
-            nc.vector.quantize_mx(out=h_w[a, half][:].bitcast(E4M3), scales=h_s[a, half][:], in_=h_words[a, half][:])
+        def place_h(a, half, kib):
+            h_bf[a, half] = place_tile("h_bf%d%d" % (a, half), [P, HALF * PACK], BF16, kib)[:]
 
-        def product(n, half, kib):
+        def quantize_h(a, half, kib):
+            h_w[a, half] = place_tile("h_w%d%d" % (a, half), [P, HALF], U32, kib)[:]
+            h_s[a, half] = place_tile("h_s%d%d" % (a, half), [P, HALF], U8, kib + 2)[:]
+            nc.vector.quantize_mx(out=h_w[a, half].bitcast(E4M3), scales=h_s[a, half], in_=h_bf[a, half])
+
+        def second_product(n, half, number, passes=range(PASSES)):
             ncols = slice(n * P, (n + 1) * P)
             w1_w = w1_first[:, :, ncols] if n < FIRST_BLOCKS else w1_rest[:, :, n * P - first_cols : (n + 1) * P - first_cols]
-            if n < SPLIT_BLOCKS:
-                number = ((2, 2, 0, 2), (3, 4, 6, 7))[half][n]
-            else:
-                number = (3, 4, 6, 7)[(2 * n + half) % 4]
-            y = bank("y%d_%d" % (n, half), number)
-            order = ((0, 1, 2), (0, 2, 1))[half]
-            for a in order:
+            for a in passes:
+                if a == 0:
+                    y_bank[n, half] = bank("y%d_%d" % (n, half), number)
                 nc.tensor.matmul_mx(
-                    out=y[:],
+                    out=y_bank[n, half][:],
                     lhsT=w1_w[:, a, :].bitcast(E4M3),
                     lhsT_scale=w1_s[4 * a :, ncols],
-                    rhs=h_w[a, half][:].bitcast(E4M3),
-                    rhs_scale=h_s[a, half][:],
-                    start=(a == order[0]),
-                    stop=(a == order[-1]),
+                    rhs=h_w[a, half].bitcast(E4M3),
+                    rhs_scale=h_s[a, half],
+                    start=(a == 0),
+                    stop=(a == PASSES - 1),
                 )
-            if n < SPLIT_BLOCKS:
-                y_sb[n] = place_tile("y_sb%d%d" % (n, half), [P, HALF], F32, kib)[:]
-                target = y_sb[n]
-            else:
-                if half == 0:
-                    y_sb[n] = place_tile("y_sb%d" % n, [P, S], F32, kib)[:]
-                target = y_sb[n][:, halves[half]]
-            nc.scalar.activation(target, y[:], ACT.Copy, scale=-1.0)
 
-        def place(n, cols):
+        def place_y(n, cols, kib):
+            y_sb[n] = place_tile("y_sb%d_%d" % (n, cols.start), [P, cols.stop - cols.start], F32, kib)[:]
+
+        def empty_y(n, half, target):
+            nc.scalar.activation(target, y_bank[n, half][:], ACT.Copy, scale=-1.0)
+
+        def weigh_gpsimd(n):
+            nc.gpsimd.tensor_tensor(y_sb[n], y_sb[n], wgo_sb[:, first], ALU.mult)
+
+        def put_weighed(n):
+            nc.vector.tensor_copy(frames[n][:].indirect(listed(idx2, first)), y_sb[n])
+
+        def weigh_and_put(n, cols):
             window = frames[n % FRAMES][:].indirect(listed(idx2, cols))
             nc.vector.tensor_tensor(window, y_sb[n], wgo_sb[:, cols], ALU.mult)
 
         def store(n):
             nc.sync.dma_start(out[n * P : (n + 1) * P, :], frames[n % FRAMES][:])
 
-        first, second = halves
-        last = SLICES - 1
-
-        waiting = []
-
-        def half_gpsimd(k, half, d_kib):
-            d_sb = empty_d(k, half, d_kib)
-            if k in (3, 7):
-                waiting.append((k, half, d_sb))
-            else:
-                multiply_gpsimd(k, half, less_one_gpsimd(k, half, {4: AT_PICKED + 12, 8: AT_W2_BF + 2}.get(k)), d_sb)
-
-        def waiting_gpsimd():
-            for k, half, d_sb in waiting:
-                multiply_gpsimd(k, half, less_one_gpsimd(k, half, AT_W2_BF + 2 * half), d_sb)
-            waiting.clear()
-
         nc.vector.tensor_copy(v_w[:], tab_w[:].bitcast(U32).indirect(idx[:]))
         nc.vector.tensor_copy(v_s[:], tab_s[:].indirect(idx[:]))
-        round_w2(0, AT_W2_BF)
-        quantize_w2(0, AT_SMALL + 4, AT_LATE + 8)
-        for k in range(4):
-            first_product(k, 0, k)
-        for k in range(4):
-            first_product(k, 1, 4 + k)
+        round_w2(0, AT_FRAME + 8 * (EARLY_FRAMES + 1) - 2, shared=True)
+        quantize_w2(0, AT_FREE)
+        for frame in frames[EARLY_FRAMES:]:
+            nc.gpsimd.memset(frame[:], 0.0)
+        place_picked(0, (AT_FREE + 8, AT_FREE + 16))
+        gather_s(0)
+        for u in range(UNITS):
+            first_product(0, u, u)
+        for u in (0, 2, 4):
+            empty_d(0, u, AT_FREE + 24 + 2 * u)
+        for k in (1, 2, 3):
+            gather_s(k)
+        place_h(0, 0, AT_FREE + 4)
+        square(0, 0, 2, AT_FREE + 36)
+        less_one_gpsimd(0, 0)
+        multiply_gpsimd(0, 0)
+        square(0, 2, 2, AT_FREE + 40)
+        square(0, 6, 2, AT_TAB)
+        less_one_scalar(0, 2)
+        multiply_gpsimd(0, 2)
 
-        rows_h(0, 0, at_w2(0))
-        rows_h(0, 1, at_s(2))
-        for k in range(4):
-            gather_s(k, whole, AT_PICKED + 4 * k)
-            if k == 3:
-                round_w2(1, AT_W2_BF)
-            square_s(k, whole, (AT_SQUARE, AT_PICKED_MORE, AT_PICKED, at_w2(1))[k])
-            half_gpsimd(k, 0, (AT_D, AT_D + 2, AT_PICKED + 8, AT_PICKED + 12)[k])
-            if k == 2:
-                derivative_vector(0, 1)
-                derivative_vector(1, 1)
-                half_gpsimd(k, 1, AT_PICKED + 4 * k + 2)
-        d_late = empty_d(3, 1, AT_PICKED + 14)
-
-        rows_h(1, 0, at_s(1))
-        rows_h(1, 1, at_s(6))
-        for k in range(4, 8):
-            cols = whole if k < 6 else first
-            gather_s(k, cols, (AT_TAB, AT_TAB + 4, AT_LATE, AT_LATE + 2)[k - 4])
-            if k >= 6:
-                gather_s(k, second, AT_LATE + 4 + 2 * (k - 6))
-            if k == 4:
-                quantize_w2(1, at_s(k) + 4, at_s(k) + 6)
-                waiting_gpsimd()
-                for j in range(4, 8):
-                    first_product(j, 0, j - 4)
-                for j in (4, 5):
-                    first_product(j, 1, j)
-            if k == 6:
-                interleave_h(0, 0, AT_TAB + 4)
-            if k == 7:
-                round_w2(2, AT_W2_BF)
-            square_s(k, cols, (AT_PICKED + 4, at_s(0), at_w2(0), at_w2(2))[k - 4])
-            half_gpsimd(k, 0, (AT_D + 4, AT_D + 6, AT_LATE, AT_LATE + 2)[k - 4])
-            if k == 6:
-                derivative_vector(4, 1)
-                derivative_vector(5, 1)
-
-        rows_h(2, 0, at_s(1) + 4)
-        for k in range(8, last):
-            gather_s(k, first, (at_s(5), at_s(5) + 4, at_s(7))[k - 8])
-            gather_s(k, second, (at_s(4), at_s(4) + 2, at_s(3) + 4)[k - 8])
-            square_s(k, first, (AT_SMALL, AT_SMALL + 2, AT_SMALL + 6)[k - 8])
-            if k == 8:
-                quantize_w2(2, at_s(8) + 6, at_s(5) + 2)
-                waiting_gpsimd()
-                for j in range(8, SLICES):
-                    first_product(j, 0, j - 8)
-                for j in range(8, SLICES):
-                    first_product(j, 1, (6, 7, 4, 5)[j - 8])
-            if k < 10:
-                half_gpsimd(k, 0, AT_D + 2 * (k - 8))
-            else:
-                derivative_vector(k, 0)
-                interleave_h(1, 0, at_s(7))
-            square_s(k, second, (at_s(8), at_s(8) + 2, at_s(8) + 4)[k - 8])
-        multiply_gpsimd(3, 1, less_one_gpsimd(3, 1, AT_D + 2), d_late)
+        place_picked(1, (at_s(1), at_s(2)))
+        gather_s(4)
+        place_h(0, 1, at_s(4))
+        for e in range(2):
+            multiply_vector(0, 6, e)
+        round_w2(1, at_w2(0))
+        square(0, 4, 2, at_w2(1) + 4)
+        gather_s(5)
+        quantize_w2(1, at_s(5))
+        less_one_gpsimd(0, 4, at_w2(0))
+        multiply_gpsimd(0, 4)
+        for u in range(UNITS):
+            first_product(1, u, u)
+        for u in (0, 2):
+            empty_d(1, u, AT_FREE + 24 + 2 * u)
         for k in (6, 7):
-            first_product(k, 1, k - 6)
+            gather_s(k)
+        place_h(1, 0, at_s(3))
+        square(1, 0, 2, AT_FREE + 36)
+        less_one_gpsimd(1, 0)
+        multiply_gpsimd(1, 0)
+        square(1, 2, 2, AT_FREE + 40)
+        less_one_scalar(1, 2)
+        multiply_gpsimd(1, 2)
+        empty_d(1, 4, at_s(1))
+        square(1, 4, 2, AT_TAB)
 
-        gather_s(last, first, at_s(3))
-        gather_s(last, second, at_s(9) + 4)
-        square_s(last, first, at_s(5) + 6)
-        derivative_vector(last, 0)
-        interleave_h(2, 0, at_s(3) + 4)
-        square_s(11, second, at_s(1) + 4)
-        rows_h(2, 1, at_s(3))
-        for k in range(8, SLICES):
-            derivative_vector(k, 1)
-            if k == 10:
-                quantize_h(0, 0, at_s(10) + 6, at_s(8) + 2)
-                quantize_h(1, 0, at_s(10), at_s(8) + 2.5)
-                quantize_h(2, 0, at_s(10) + 2, at_s(7) + 2.5)
+        place_picked(2, (at_s(0), AT_FREE + 8))
+        for k in (8, 9, 10):
+            gather_s(k)
+        quantize_h(0, 0, at_s(10))
+        quantize_h(1, 0, at_s(10) + 5)
+        round_w2(2, at_s(6))
+        quantize_w2(2, at_s(7))
+        square(1, 6, 2, at_w2(2))
+        late = place_tile("h_bf_late", [P, 2 * HALF * PACK], BF16, AT_FREE + 16)
+        h_bf[1, 1] = late[:, : HALF * PACK]
+        h_bf[2, 1] = late[:, HALF * PACK :]
+        less_one_gpsimd(1, 4, at_s(6))
+        multiply_gpsimd(1, 4)
+        for u in range(6):
+            first_product(2, u, u)
+        gather_s(11)
+        place_h(2, 0, at_s(8))
+        for u in range(4):
+            square(2, u, 1, AT_FREE + 36 + 2 * u)
+            multiply_vector(2, u)
+        for n in range(2):
+            second_product(n, 0, n, (0, 1))
+        quantize_h(2, 0, at_s(8) + 4)
+        quantize_h(0, 1, at_s(8))
+        for n in range(2):
+            second_product(n, 0, n, (2,))
+        place_y(0, first, AT_FREE + 44)
+        nc.vector.scalar_tensor_tensor(y_sb[0], y_bank[0, 0][:], -1.0, wgo_sb[:, first], ALU.mult, ALU.mult)
+        put_weighed(0)
 
-        for k in (6, 7):
-            square_s(k, second, (at_s(9) + 4, at_s(1) + 6)[k - 6])
-            derivative_vector(k, 1)
-        product(0, 0, at_s(11))
-        place(0, first)
-        product(1, 0, at_s(11) + 2)
-        interleave_h(0, 1, AT_LATE + 4)
-        quantize_h(0, 1, at_s(10) + 4, at_s(8) + 1)
-        place(1, first)
-        interleave_h(2, 1, at_s(2))
-        product(2, 0, at_s(3))
-        quantize_h(2, 1, at_s(7) + 4, at_s(8) + 1.5)
-        place(2, first)
-        interleave_h(1, 1, at_s(3) + 2)
-        product(3, 0, at_s(6))
-        quantize_h(1, 1, at_s(7) + 6, at_s(7) + 3)
-        place(3, first)
-        for n in range(SPLIT_BLOCKS):
-            product(n, 1, AT_D + 2 * n)
-            place(n, second)
+        square(2, 4, 2, at_w2(2) + 4)
+        empty_d(1, 6, at_s(0))
+        for u in (6, 7):
+            first_product(2, u, u)
+        less_one_gpsimd(1, 6, at_s(4))
+        multiply_gpsimd(1, 6, 0, 1)
+        place_y(1, first, AT_FREE + 4)
+        empty_y(1, 0, y_sb[1])
+        weigh_gpsimd(1)
+        put_weighed(1)
+        multiply_gpsimd(1, 6, 1, 1)
+        second_product(2, 0, 0)
+        place_y(2, first, AT_FREE + 6)
+        empty_y(2, 0, y_sb[2])
+        weigh_gpsimd(2)
+        put_weighed(2)
+        less_one_scalar(2, 4)
+        empty_d(2, 4, AT_FREE + 24)
+        multiply_gpsimd(2, 4)
+        second_product(3, 0, 1)
+        place_y(3, first, at_s(3))
+        empty_y(3, 0, y_sb[3])
+        weigh_gpsimd(3)
+        put_weighed(3)
+        square(2, 6, 2, AT_TAB + 4)
+        less_one_scalar(2, 6)
+        empty_d(2, 6, AT_FREE + 28)
+        multiply_gpsimd(2, 6)
+        second_product(4, 0, 0)
+        place_y(4, first, AT_FREE + 4)
+        empty_y(4, 0, y_sb[4])
+        weigh_gpsimd(4)
+        late_w = place_tile("h_w_late", [P, 2 * HALF], U32, at_s(9))
+        late_s = place_tile("h_s_late", [P, 2 * HALF], U8, at_s(9) + 4)
+        nc.vector.quantize_mx(out=late_w[:].bitcast(E4M3), scales=late_s[:], in_=late[:])
+        for a in (1, 2):
+            h_w[a, 1] = late_w[:, halves[a - 1]]
+            h_s[a, 1] = late_s[:, halves[a - 1]]
+        put_weighed(4)
+
+        for n in range(FRAMES):
+            second_product(n, 1, (2, 3, 5, 7, 1)[n])
+            place_y(n, second, at_w2(1) + 2 * n - 2)
+            empty_y(n, 1, y_sb[n])
+            weigh_and_put(n, second)
             store(n)
-        for n in range(SPLIT_BLOCKS, BLOCKS):
-            for half in range(HALVES):
-                product(n, half, (at_s(3) + 2, at_s(9), at_s(11) + 4, at_s(2))[n - SPLIT_BLOCKS])
-            place(n, whole)
+        for n in range(FRAMES, BLOCKS):
+            place_y(n, whole, AT_FREE + 16 + 4 * (n - FRAMES))
+            for half in range(2):
+                second_product(n, half, (0, 4, 6, 2, 3, 5)[2 * (n - FRAMES) + half])
+                empty_y(n, half, y_sb[n][:, halves[half]])
+            weigh_and_put(n, whole)
             store(n)

@@ -26,20 +26,20 @@ BLOCKS = N // P
 PER_COLUMN = 16
 UNIT = 128
 UNITS = S // UNIT
-FRAMES = 5
+FRAMES = 6
 EARLY_FRAMES = 3
-FIRST_BLOCKS = 2
+FIRST_BLOCKS = 3
 KB = 1024
 
 AT_W2 = 96
 AT_TAB = 120
 AT_FRAME = 128
-AT_W1 = 168
-AT_WGO = 180
-AT_TAB_S = 184
-AT_V_W = 186
-AT_V_S = 190
-AT_W1_S = 191
+AT_W1 = 176
+AT_WGO = 188
+AT_TAB_S = 192
+AT_V_W = 194
+AT_V_S = 198
+AT_W1_S = 199
 AT_FREE = 192
 
 
@@ -239,8 +239,11 @@ def tile_list_fibre_equaliser_backward_kernel(
         def empty_y(n, half, target):
             nc.scalar.activation(target, y_bank[n, half][:], ACT.Copy, scale=-1.0)
 
-        def weigh_gpsimd(n):
-            nc.gpsimd.tensor_tensor(y_sb[n], y_sb[n], wgo_sb[:, first], ALU.mult)
+        def weigh_gpsimd(n, kib=None):
+            raw = y_sb[n]
+            if kib is not None:
+                y_sb[n] = place_tile("y_weighed%d" % n, [P, HALF], F32, kib)[:]
+            nc.gpsimd.tensor_tensor(y_sb[n], raw, wgo_sb[:, first], ALU.mult)
 
         def put_weighed(n):
             nc.vector.tensor_copy(frames[n][:].indirect(listed(idx2, first)), y_sb[n])
@@ -255,18 +258,18 @@ def tile_list_fibre_equaliser_backward_kernel(
         nc.vector.tensor_copy(v_w[:], tab_w[:].bitcast(U32).indirect(idx[:]))
         nc.vector.tensor_copy(v_s[:], tab_s[:].indirect(idx[:]))
         round_w2(0, AT_FRAME + 8 * (EARLY_FRAMES + 1) - 2, shared=True)
-        quantize_w2(0, AT_FREE)
-        for frame in frames[EARLY_FRAMES:]:
-            nc.gpsimd.memset(frame[:], 0.0)
-        place_picked(0, (AT_FREE + 8, AT_FREE + 16))
+        quantize_w2(0, AT_FRAME + 8 * (FRAMES - 1))
+        place_picked(0, (at_w2(0), AT_FREE + 16))
         gather_s(0)
         for u in range(UNITS):
             first_product(0, u, u)
+        for frame in frames[EARLY_FRAMES:]:
+            nc.gpsimd.memset(frame[:], 0.0)
         for u in (0, 2, 4):
             empty_d(0, u, AT_FREE + 24 + 2 * u)
         for k in (1, 2, 3):
             gather_s(k)
-        place_h(0, 0, AT_FREE + 4)
+        place_h(0, 0, AT_FREE + 8)
         square(0, 0, 2, AT_FREE + 36)
         less_one_gpsimd(0, 0)
         multiply_gpsimd(0, 0)
@@ -292,7 +295,7 @@ def tile_list_fibre_equaliser_backward_kernel(
             empty_d(1, u, AT_FREE + 24 + 2 * u)
         for k in (6, 7):
             gather_s(k)
-        place_h(1, 0, at_s(3))
+        place_h(1, 0, AT_FREE + 12)
         square(1, 0, 2, AT_FREE + 36)
         less_one_gpsimd(1, 0)
         multiply_gpsimd(1, 0)
@@ -302,7 +305,7 @@ def tile_list_fibre_equaliser_backward_kernel(
         empty_d(1, 4, at_s(1))
         square(1, 4, 2, AT_TAB)
 
-        place_picked(2, (at_s(0), AT_FREE + 8))
+        place_picked(2, (at_s(0), at_s(3)))
         for k in (8, 9, 10):
             gather_s(k)
         quantize_h(0, 0, at_s(10))
@@ -322,11 +325,11 @@ def tile_list_fibre_equaliser_backward_kernel(
         for u in range(4):
             square(2, u, 1, AT_FREE + 36 + 2 * u)
             multiply_vector(2, u)
-        for n in range(2):
+        for n in range(3):
             second_product(n, 0, n, (0, 1))
         quantize_h(2, 0, at_s(8) + 4)
         quantize_h(0, 1, at_s(8))
-        for n in range(2):
+        for n in range(3):
             second_product(n, 0, n, (2,))
         place_y(0, first, AT_FREE + 44)
         nc.vector.scalar_tensor_tensor(y_sb[0], y_bank[0, 0][:], -1.0, wgo_sb[:, first], ALU.mult, ALU.mult)
@@ -336,52 +339,47 @@ def tile_list_fibre_equaliser_backward_kernel(
         empty_d(1, 6, at_s(0))
         for u in (6, 7):
             first_product(2, u, u)
-        less_one_gpsimd(1, 6, at_s(4))
-        multiply_gpsimd(1, 6, 0, 1)
-        place_y(1, first, AT_FREE + 4)
-        empty_y(1, 0, y_sb[1])
-        weigh_gpsimd(1)
-        put_weighed(1)
-        multiply_gpsimd(1, 6, 1, 1)
-        second_product(2, 0, 0)
-        place_y(2, first, AT_FREE + 6)
-        empty_y(2, 0, y_sb[2])
-        weigh_gpsimd(2)
-        put_weighed(2)
+        for n in (1, 2):
+            place_y(n, first, AT_FREE + 6 + 2 * n)
+            empty_y(n, 0, y_sb[n])
+            weigh_gpsimd(n, at_s(4) + 2 * n - 2)
+            put_weighed(n)
+        less_one_gpsimd(1, 6, AT_FREE + 8)
+        multiply_gpsimd(1, 6)
         less_one_scalar(2, 4)
-        empty_d(2, 4, AT_FREE + 24)
+        for n in (3, 4):
+            second_product(n, 0, n - 3)
+            place_y(n, first, AT_FREE + 6 + 2 * n)
+            empty_y(n, 0, y_sb[n])
+            weigh_gpsimd(n)
+            put_weighed(n)
+        empty_d(2, 4, at_s(0))
         multiply_gpsimd(2, 4)
-        second_product(3, 0, 1)
-        place_y(3, first, at_s(3))
-        empty_y(3, 0, y_sb[3])
-        weigh_gpsimd(3)
-        put_weighed(3)
         square(2, 6, 2, AT_TAB + 4)
         less_one_scalar(2, 6)
-        empty_d(2, 6, AT_FREE + 28)
+        empty_d(2, 6, AT_FREE + 8)
         multiply_gpsimd(2, 6)
-        second_product(4, 0, 0)
-        place_y(4, first, AT_FREE + 4)
-        empty_y(4, 0, y_sb[4])
-        weigh_gpsimd(4)
+        second_product(5, 0, 2)
+        place_y(5, first, AT_FREE + 8)
+        empty_y(5, 0, y_sb[5])
         late_w = place_tile("h_w_late", [P, 2 * HALF], U32, at_s(9))
         late_s = place_tile("h_s_late", [P, 2 * HALF], U8, at_s(9) + 4)
         nc.vector.quantize_mx(out=late_w[:].bitcast(E4M3), scales=late_s[:], in_=late[:])
         for a in (1, 2):
             h_w[a, 1] = late_w[:, halves[a - 1]]
             h_s[a, 1] = late_s[:, halves[a - 1]]
-        put_weighed(4)
+        weigh_and_put(5, first)
 
         for n in range(FRAMES):
-            second_product(n, 1, (2, 3, 5, 7, 1)[n])
-            place_y(n, second, at_w2(1) + 2 * n - 2)
+            second_product(n, 1, (2, 3, 5, 7, 4, 6)[n])
+            place_y(n, second, at_w2(0) + 2 * n)
             empty_y(n, 1, y_sb[n])
             weigh_and_put(n, second)
             store(n)
         for n in range(FRAMES, BLOCKS):
             place_y(n, whole, AT_FREE + 16 + 4 * (n - FRAMES))
             for half in range(2):
-                second_product(n, half, (0, 4, 6, 2, 3, 5)[2 * (n - FRAMES) + half])
+                second_product(n, half, (0, 1, 2, 3)[2 * (n - FRAMES) + half])
                 empty_y(n, half, y_sb[n][:, halves[half]])
             weigh_and_put(n, whole)
             store(n)

@@ -217,11 +217,11 @@ def tile_list_fibre_equaliser_backward_kernel(
             h_s[a, half] = place_tile("h_s%d%d" % (a, half), [P, HALF], U8, kib + 2)[:]
             nc.vector.quantize_mx(out=h_w[a, half].bitcast(E4M3), scales=h_s[a, half], in_=h_bf[a, half])
 
-        def second_product(n, half, number, passes=range(PASSES)):
+        def second_product(n, half, number, order, part=slice(0, PASSES)):
             ncols = slice(n * P, (n + 1) * P)
             w1_w = w1_first[:, :, ncols] if n < FIRST_BLOCKS else w1_rest[:, :, n * P - first_cols : (n + 1) * P - first_cols]
-            for a in passes:
-                if a == 0:
+            for a in order[part]:
+                if a == order[0]:
                     y_bank[n, half] = bank("y%d_%d" % (n, half), number)
                 nc.tensor.matmul_mx(
                     out=y_bank[n, half][:],
@@ -229,8 +229,8 @@ def tile_list_fibre_equaliser_backward_kernel(
                     lhsT_scale=w1_s[4 * a :, ncols],
                     rhs=h_w[a, half].bitcast(E4M3),
                     rhs_scale=h_s[a, half],
-                    start=(a == 0),
-                    stop=(a == PASSES - 1),
+                    start=(a == order[0]),
+                    stop=(a == order[-1]),
                 )
 
         def place_y(n, cols, kib):
@@ -318,27 +318,25 @@ def tile_list_fibre_equaliser_backward_kernel(
         h_bf[2, 1] = late[:, HALF * PACK :]
         less_one_gpsimd(1, 4, at_s(6))
         multiply_gpsimd(1, 4)
-        for u in range(6):
+        for u in range(4):
             first_product(2, u, u)
         gather_s(11)
         place_h(2, 0, at_s(8))
         for u in range(4):
             square(2, u, 1, AT_FREE + 36 + 2 * u)
             multiply_vector(2, u)
-        for n in range(3):
-            second_product(n, 0, n, (0, 1))
+        second_product(0, 0, 4, (0, 1, 2), slice(0, 2))
         quantize_h(2, 0, at_s(8) + 4)
         quantize_h(0, 1, at_s(8))
-        for n in range(3):
-            second_product(n, 0, n, (2,))
+        second_product(0, 0, 4, (0, 1, 2), slice(2, 3))
+        for n in range(1, 5):
+            second_product(n, 0, (5, 3, 0, 1)[n - 1], (2, 0, 1))
         place_y(0, first, AT_FREE + 44)
         nc.vector.scalar_tensor_tensor(y_sb[0], y_bank[0, 0][:], -1.0, wgo_sb[:, first], ALU.mult, ALU.mult)
         put_weighed(0)
 
         square(2, 4, 2, at_w2(2) + 4)
         empty_d(1, 6, at_s(0))
-        for u in (6, 7):
-            first_product(2, u, u)
         for n in (1, 2):
             place_y(n, first, AT_FREE + 6 + 2 * n)
             empty_y(n, 0, y_sb[n])
@@ -348,18 +346,19 @@ def tile_list_fibre_equaliser_backward_kernel(
         multiply_gpsimd(1, 6)
         less_one_scalar(2, 4)
         for n in (3, 4):
-            second_product(n, 0, n - 3)
             place_y(n, first, AT_FREE + 6 + 2 * n)
             empty_y(n, 0, y_sb[n])
             weigh_gpsimd(n)
             put_weighed(n)
+        for u in range(4, UNITS):
+            first_product(2, u, (4, 5, 3, 0)[u - 4])
         empty_d(2, 4, at_s(0))
         multiply_gpsimd(2, 4)
         square(2, 6, 2, AT_TAB + 4)
         less_one_scalar(2, 6)
         empty_d(2, 6, AT_FREE + 8)
         multiply_gpsimd(2, 6)
-        second_product(5, 0, 2)
+        second_product(5, 0, 1, (2, 0, 1))
         place_y(5, first, AT_FREE + 8)
         empty_y(5, 0, y_sb[5])
         late_w = place_tile("h_w_late", [P, 2 * HALF], U32, at_s(9))
@@ -371,7 +370,7 @@ def tile_list_fibre_equaliser_backward_kernel(
         weigh_and_put(5, first)
 
         for n in range(FRAMES):
-            second_product(n, 1, (2, 3, 5, 7, 4, 6)[n])
+            second_product(n, 1, (2, 6, 7, 4, 5, 3)[n], (1, 2, 0))
             place_y(n, second, at_w2(0) + 2 * n)
             empty_y(n, 1, y_sb[n])
             weigh_and_put(n, second)
@@ -379,7 +378,7 @@ def tile_list_fibre_equaliser_backward_kernel(
         for n in range(FRAMES, BLOCKS):
             place_y(n, whole, AT_FREE + 16 + 4 * (n - FRAMES))
             for half in range(2):
-                second_product(n, half, (0, 1, 2, 3)[2 * (n - FRAMES) + half])
+                second_product(n, half, (0, 2, 1, 6)[2 * (n - FRAMES) + half], (1, 2, 0))
                 empty_y(n, half, y_sb[n][:, halves[half]])
             weigh_and_put(n, whole)
             store(n)

@@ -26,8 +26,8 @@ BLOCKS = N // P
 PER_COLUMN = 16
 UNIT = 128
 UNITS = S // UNIT
-FRAMES = 6
-EARLY_FRAMES = 3
+FRAMES = 7
+EARLY_FRAMES = 4
 FIRST_BLOCKS = 3
 KB = 1024
 
@@ -75,7 +75,7 @@ def tile_list_fibre_equaliser_backward_kernel(
         w1_rest = place_tile("w1_rest", [P, PASSES, N - first_cols], I32, AT_W1 + PASSES * first_cols * 4 / KB)
         w1_s = place_tile("w1_s", [P, N], U8, AT_W1_S)
         wgo_sb = place_tile("wgo_sb", [P, S], F32, AT_WGO)
-        frames = [place_tile("frame%d" % f, [P, T2], F32, AT_FRAME + 8 * f) for f in range(FRAMES)]
+        frames = [place_tile("frame%d" % f, [P, T2], F32, AT_FRAME + 8 * f if f < FRAMES - 1 else AT_FREE + 16) for f in range(FRAMES)]
 
         def listed(tile, cols):
             return tile[:, cols.start // PER_COLUMN : cols.stop // PER_COLUMN]
@@ -258,15 +258,16 @@ def tile_list_fibre_equaliser_backward_kernel(
         nc.vector.tensor_copy(v_w[:], tab_w[:].bitcast(U32).indirect(idx[:]))
         nc.vector.tensor_copy(v_s[:], tab_s[:].indirect(idx[:]))
         round_w2(0, AT_FRAME + 8 * (EARLY_FRAMES + 1) - 2, shared=True)
-        quantize_w2(0, AT_FRAME + 8 * (FRAMES - 1))
-        place_picked(0, (at_w2(0), AT_FREE + 16))
+        quantize_w2(0, AT_FREE + 16)
+        place_picked(0, (at_w2(0), AT_TAB))
         gather_s(0)
         for u in range(UNITS):
             first_product(0, u, u)
         for frame in frames[EARLY_FRAMES:]:
             nc.gpsimd.memset(frame[:], 0.0)
-        for u in (0, 2, 4):
+        for u in (0, 2):
             empty_d(0, u, AT_FREE + 24 + 2 * u)
+        empty_d(0, 4, AT_FREE + 32)
         for k in (1, 2, 3):
             gather_s(k)
         place_h(0, 0, AT_FREE + 8)
@@ -274,7 +275,7 @@ def tile_list_fibre_equaliser_backward_kernel(
         less_one_gpsimd(0, 0)
         multiply_gpsimd(0, 0)
         square(0, 2, 2, AT_FREE + 40)
-        square(0, 6, 2, AT_TAB)
+        square(0, 6, 2, at_s(3))
         less_one_scalar(0, 2)
         multiply_gpsimd(0, 2)
 
@@ -285,100 +286,105 @@ def tile_list_fibre_equaliser_backward_kernel(
             multiply_vector(0, 6, e)
         round_w2(1, at_w2(0))
         square(0, 4, 2, at_w2(1) + 4)
-        gather_s(5)
-        quantize_w2(1, at_s(5))
+        for k in (5, 6):
+            gather_s(k)
+        quantize_w2(1, at_s(6) + 4)
         less_one_gpsimd(0, 4, at_w2(0))
         multiply_gpsimd(0, 4)
         for u in range(UNITS):
             first_product(1, u, u)
-        for u in (0, 2):
-            empty_d(1, u, AT_FREE + 24 + 2 * u)
-        for k in (6, 7):
-            gather_s(k)
+        empty_d(1, 0, AT_FREE + 24)
+        gather_s(7)
         place_h(1, 0, AT_FREE + 12)
         square(1, 0, 2, AT_FREE + 36)
-        less_one_gpsimd(1, 0)
+        less_one_scalar(1, 0)
         multiply_gpsimd(1, 0)
         square(1, 2, 2, AT_FREE + 40)
+        empty_d(1, 2, at_s(7))
         less_one_scalar(1, 2)
         multiply_gpsimd(1, 2)
-        empty_d(1, 4, at_s(1))
-        square(1, 4, 2, AT_TAB)
+        square(1, 6, 2, at_s(1))
+        round_w2(2, at_s(5))
+        square(1, 4, 2, at_w2(2))
 
         place_picked(2, (at_s(0), at_s(3)))
         for k in (8, 9, 10):
             gather_s(k)
-        quantize_h(0, 0, at_s(10))
-        quantize_h(1, 0, at_s(10) + 5)
-        round_w2(2, at_s(6))
-        quantize_w2(2, at_s(7))
-        square(1, 6, 2, at_w2(2))
-        late = place_tile("h_bf_late", [P, 2 * HALF * PACK], BF16, AT_FREE + 16)
+        late = place_tile("h_bf_late", [P, 2 * HALF * PACK], BF16, at_s(10))
         h_bf[1, 1] = late[:, : HALF * PACK]
         h_bf[2, 1] = late[:, HALF * PACK :]
-        less_one_gpsimd(1, 4, at_s(6))
-        multiply_gpsimd(1, 4)
+        for e in range(2):
+            multiply_vector(1, 6, e)
+        gather_s(11)
+        quantize_w2(2, at_s(11))
+        quantize_h(0, 0, at_s(11) + 2.5)
+        quantize_h(1, 0, at_s(11) + 5)
+        less_one_gpsimd(1, 4, AT_FREE + 12)
         for u in range(4):
             first_product(2, u, u)
-        gather_s(11)
         place_h(2, 0, at_s(8))
         for u in range(4):
             square(2, u, 1, AT_FREE + 36 + 2 * u)
             multiply_vector(2, u)
-        second_product(0, 0, 4, (0, 1, 2), slice(0, 2))
+        for n in range(2):
+            second_product(n, 0, 6 + n, (0, 1, 2), slice(0, 2))
         quantize_h(2, 0, at_s(8) + 4)
         quantize_h(0, 1, at_s(8))
-        second_product(0, 0, 4, (0, 1, 2), slice(2, 3))
-        for n in range(1, 5):
-            second_product(n, 0, (5, 3, 0, 1)[n - 1], (2, 0, 1))
+        for n in range(2):
+            second_product(n, 0, 6 + n, (0, 1, 2), slice(2, 3))
+        for n in range(2, 6):
+            second_product(n, 0, n - 2, (2, 0, 1))
         place_y(0, first, AT_FREE + 44)
         nc.vector.scalar_tensor_tensor(y_sb[0], y_bank[0, 0][:], -1.0, wgo_sb[:, first], ALU.mult, ALU.mult)
         put_weighed(0)
 
-        square(2, 4, 2, at_w2(2) + 4)
-        empty_d(1, 6, at_s(0))
+        square(2, 4, 2, at_s(1))
         for n in (1, 2):
-            place_y(n, first, AT_FREE + 6 + 2 * n)
+            place_y(n, first, AT_FREE + 20 + 4 * n)
             empty_y(n, 0, y_sb[n])
             weigh_gpsimd(n, at_s(4) + 2 * n - 2)
             put_weighed(n)
-        less_one_gpsimd(1, 6, AT_FREE + 8)
-        multiply_gpsimd(1, 6)
-        less_one_scalar(2, 4)
+        empty_d(1, 4, AT_FREE + 24)
+        multiply_gpsimd(1, 4)
         for n in (3, 4):
-            place_y(n, first, AT_FREE + 6 + 2 * n)
+            place_y(n, first, AT_FREE + 24 + 2 * n)
             empty_y(n, 0, y_sb[n])
             weigh_gpsimd(n)
             put_weighed(n)
         for u in range(4, UNITS):
-            first_product(2, u, (4, 5, 3, 0)[u - 4])
-        empty_d(2, 4, at_s(0))
-        multiply_gpsimd(2, 4)
-        square(2, 6, 2, AT_TAB + 4)
+            first_product(2, u, (6, 7, 0, 1)[u - 4])
+        less_one_scalar(2, 4)
+        square(2, 6, 2, at_s(1) + 4)
         less_one_scalar(2, 6)
-        empty_d(2, 6, AT_FREE + 8)
-        multiply_gpsimd(2, 6)
-        second_product(5, 0, 1, (2, 0, 1))
-        place_y(5, first, AT_FREE + 8)
+        empty_d(2, 4, AT_FREE + 12)
+        multiply_gpsimd(2, 4)
+        place_y(5, first, AT_FREE + 34)
         empty_y(5, 0, y_sb[5])
+        weigh_gpsimd(5)
+        put_weighed(5)
+        empty_d(2, 6, AT_FREE + 24)
+        multiply_gpsimd(2, 6)
+        second_product(6, 0, 2, (2, 0, 1))
+        place_y(6, first, AT_FREE + 24)
+        empty_y(6, 0, y_sb[6])
         late_w = place_tile("h_w_late", [P, 2 * HALF], U32, at_s(9))
         late_s = place_tile("h_s_late", [P, 2 * HALF], U8, at_s(9) + 4)
         nc.vector.quantize_mx(out=late_w[:].bitcast(E4M3), scales=late_s[:], in_=late[:])
         for a in (1, 2):
             h_w[a, 1] = late_w[:, halves[a - 1]]
             h_s[a, 1] = late_s[:, halves[a - 1]]
-        weigh_and_put(5, first)
+        weigh_and_put(6, first)
 
         for n in range(FRAMES):
-            second_product(n, 1, (2, 6, 7, 4, 5, 3)[n], (1, 2, 0))
+            second_product(n, 1, (3, 4, 5, 6, 7, 0, 1)[n], (1, 2, 0))
             place_y(n, second, at_w2(0) + 2 * n)
             empty_y(n, 1, y_sb[n])
             weigh_and_put(n, second)
             store(n)
         for n in range(FRAMES, BLOCKS):
-            place_y(n, whole, AT_FREE + 16 + 4 * (n - FRAMES))
+            place_y(n, whole, at_s(10))
             for half in range(2):
-                second_product(n, half, (0, 2, 1, 6)[2 * (n - FRAMES) + half], (1, 2, 0))
+                second_product(n, half, 2 + half, (1, 2, 0))
                 empty_y(n, half, y_sb[n][:, halves[half]])
             weigh_and_put(n, whole)
             store(n)

@@ -27,13 +27,13 @@ PER_COLUMN = 16
 UNIT = 128
 UNITS = S // UNIT
 FRAMES = 7
-EARLY_FRAMES = 4
+EARLY_FRAMES = 5
 FIRST_BLOCKS = 3
 KB = 1024
 
 AT_W2 = 96
-AT_TAB = 120
-AT_FRAME = 128
+AT_TAB = 200
+AT_FRAME = 120
 AT_W1 = 176
 AT_WGO = 188
 AT_TAB_S = 192
@@ -75,7 +75,7 @@ def tile_list_fibre_equaliser_backward_kernel(
         w1_rest = place_tile("w1_rest", [P, PASSES, N - first_cols], I32, AT_W1 + PASSES * first_cols * 4 / KB)
         w1_s = place_tile("w1_s", [P, N], U8, AT_W1_S)
         wgo_sb = place_tile("wgo_sb", [P, S], F32, AT_WGO)
-        frames = [place_tile("frame%d" % f, [P, T2], F32, AT_FRAME + 8 * f if f < FRAMES - 1 else AT_FREE + 16) for f in range(FRAMES)]
+        frames = [place_tile("frame%d" % f, [P, T2], F32, AT_FRAME + 8 * f) for f in range(FRAMES)]
 
         def listed(tile, cols):
             return tile[:, cols.start // PER_COLUMN : cols.stop // PER_COLUMN]
@@ -126,29 +126,24 @@ def tile_list_fibre_equaliser_backward_kernel(
         halves = [slice(0, HALF), slice(HALF, S)]
         first, second = halves
 
-        def round_w2(a, kib, shared=False):
+        def round_w2(a, kib):
             w2_bf[a] = place_tile("w2_bf%d" % a, [P, PASS * PACK], BF16, kib)
             rounded = w2_bf[a][:].rearrange("p (t m j) -> p m j t", t=PACK, j=PACK)
             raw = w2_raw[a][:].rearrange("p j (m t) -> p m j t", t=PACK)
-            if shared:
-                nc.scalar.copy(rounded[:, :, :, :2], raw[:, :, :, :2])
-                nc.vector.tensor_copy(rounded[:, :, :, 2:], raw[:, :, :, 2:])
-            else:
-                nc.scalar.copy(rounded, raw)
+            nc.scalar.copy(rounded, raw)
 
         def quantize_w2(a, kib):
             w2_w[a] = place_tile("w2_w%d" % a, [P, PASS], U32, kib)
             w2_s[a] = place_tile("w2_s%d" % a, [P, PASS], U8, kib + 2)
             nc.vector.quantize_mx(out=w2_w[a][:].bitcast(E4M3), scales=w2_s[a][:], in_=w2_bf[a][:])
 
-        def place_picked(a, kibs):
-            for half in range(2):
-                picked[a, half] = place_tile("picked%d%d" % (a, half), [P, PACK, HALF], F32, kibs[half])
+        def place_picked(a, kib):
+            picked[a] = place_tile("picked%d" % a, [P, PACK, S], F32, kib)
 
         def gather_s(k):
             a, t = divmod(k, PACK)
-            for half in range(2):
-                nc.vector.tensor_copy(picked[a, half][:, t, :], s_sb[k].indirect(listed(idx, halves[half])))
+            for cols in halves if k in (3, 7) else [whole]:
+                nc.vector.tensor_copy(picked[a][:, t, cols], s_sb[k].indirect(listed(idx, cols)))
 
         def first_product(a, u, number):
             d_bank[a, u] = bank("d%d_%d" % (a, u), number)
@@ -167,10 +162,9 @@ def tile_list_fibre_equaliser_backward_kernel(
 
         def square(a, u, count, kib):
             tile = place_tile("sq%d_%d" % (a, u), [P, count * HALF], F32, kib)
-            lo = u % 4 * UNIT
             nc.scalar.activation(
                 tile[:].rearrange("p (c i t) -> p c t i", i=4, t=PACK),
-                picked[a, u // 4][:, :, lo : lo + count * UNIT].rearrange("p t (c i) -> p c t i", i=4),
+                picked[a][:, :, u * UNIT : (u + count) * UNIT].rearrange("p t (c i) -> p c t i", i=4),
                 ACT.Square,
             )
             factor[a, u] = tile
@@ -212,9 +206,9 @@ def tile_list_fibre_equaliser_backward_kernel(
         def place_h(a, half, kib):
             h_bf[a, half] = place_tile("h_bf%d%d" % (a, half), [P, HALF * PACK], BF16, kib)[:]
 
-        def quantize_h(a, half, kib):
+        def quantize_h(a, half, kib, scales_kib):
             h_w[a, half] = place_tile("h_w%d%d" % (a, half), [P, HALF], U32, kib)[:]
-            h_s[a, half] = place_tile("h_s%d%d" % (a, half), [P, HALF], U8, kib + 2)[:]
+            h_s[a, half] = place_tile("h_s%d%d" % (a, half), [P, HALF], U8, scales_kib)[:]
             nc.vector.quantize_mx(out=h_w[a, half].bitcast(E4M3), scales=h_s[a, half], in_=h_bf[a, half])
 
         def second_product(n, half, number, order, part=slice(0, PASSES)):
@@ -257,10 +251,10 @@ def tile_list_fibre_equaliser_backward_kernel(
 
         nc.vector.tensor_copy(v_w[:], tab_w[:].bitcast(U32).indirect(idx[:]))
         nc.vector.tensor_copy(v_s[:], tab_s[:].indirect(idx[:]))
-        round_w2(0, AT_FRAME + 8 * (EARLY_FRAMES + 1) - 2, shared=True)
-        quantize_w2(0, AT_FREE + 16)
-        place_picked(0, (at_w2(0), AT_TAB))
+        round_w2(0, AT_FRAME + 8 * (EARLY_FRAMES + 1) - 2)
+        place_picked(0, AT_TAB)
         gather_s(0)
+        quantize_w2(0, AT_FREE + 44)
         for u in range(UNITS):
             first_product(0, u, u)
         for frame in frames[EARLY_FRAMES:]:
@@ -270,7 +264,7 @@ def tile_list_fibre_equaliser_backward_kernel(
         empty_d(0, 4, AT_FREE + 32)
         for k in (1, 2, 3):
             gather_s(k)
-        place_h(0, 0, AT_FREE + 8)
+        place_h(0, 0, at_w2(0) + 4)
         square(0, 0, 2, AT_FREE + 36)
         less_one_gpsimd(0, 0)
         multiply_gpsimd(0, 0)
@@ -279,7 +273,7 @@ def tile_list_fibre_equaliser_backward_kernel(
         less_one_scalar(0, 2)
         multiply_gpsimd(0, 2)
 
-        place_picked(1, (at_s(1), at_s(2)))
+        place_picked(1, at_s(1))
         gather_s(4)
         place_h(0, 1, at_s(4))
         for e in range(2):
@@ -295,7 +289,7 @@ def tile_list_fibre_equaliser_backward_kernel(
             first_product(1, u, u)
         empty_d(1, 0, AT_FREE + 24)
         gather_s(7)
-        place_h(1, 0, AT_FREE + 12)
+        place_h(1, 0, at_s(4) + 4)
         square(1, 0, 2, AT_FREE + 36)
         less_one_scalar(1, 0)
         multiply_gpsimd(1, 0)
@@ -303,11 +297,11 @@ def tile_list_fibre_equaliser_backward_kernel(
         empty_d(1, 2, at_s(7))
         less_one_scalar(1, 2)
         multiply_gpsimd(1, 2)
-        square(1, 6, 2, at_s(1))
+        square(1, 6, 2, at_w2(0))
         round_w2(2, at_s(5))
         square(1, 4, 2, at_w2(2))
 
-        place_picked(2, (at_s(0), at_s(3)))
+        place_picked(2, AT_TAB)
         for k in (8, 9, 10):
             gather_s(k)
         late = place_tile("h_bf_late", [P, 2 * HALF * PACK], BF16, at_s(10))
@@ -317,21 +311,21 @@ def tile_list_fibre_equaliser_backward_kernel(
             multiply_vector(1, 6, e)
         gather_s(11)
         quantize_w2(2, at_s(11))
-        quantize_h(0, 0, at_s(11) + 2.5)
-        quantize_h(1, 0, at_s(11) + 5)
-        less_one_gpsimd(1, 4, AT_FREE + 12)
+        quantize_h(0, 0, at_s(11) + 3, at_s(11) + 5)
+        less_one_gpsimd(1, 4, at_w2(0) + 4)
         for u in range(4):
             first_product(2, u, u)
         place_h(2, 0, at_s(8))
         for u in range(4):
             square(2, u, 1, AT_FREE + 36 + 2 * u)
             multiply_vector(2, u)
-        for n in range(2):
-            second_product(n, 0, 6 + n, (0, 1, 2), slice(0, 2))
-        quantize_h(2, 0, at_s(8) + 4)
-        quantize_h(0, 1, at_s(8))
-        for n in range(2):
-            second_product(n, 0, 6 + n, (0, 1, 2), slice(2, 3))
+        quantize_h(1, 0, AT_FREE + 40, at_s(11) + 5.5)
+        quantize_h(2, 0, at_s(8) + 4, at_s(8) + 6)
+        quantize_h(0, 1, AT_FREE + 42, at_s(11) + 6)
+        orders = ((0, 1, 2), (0, 2, 1))
+        for part in (slice(0, 1), slice(1, PASSES)):
+            for n in range(2):
+                second_product(n, 0, 6 + n, orders[n], part)
         for n in range(2, 6):
             second_product(n, 0, n - 2, (2, 0, 1))
         place_y(0, first, AT_FREE + 44)
@@ -356,7 +350,7 @@ def tile_list_fibre_equaliser_backward_kernel(
         less_one_scalar(2, 4)
         square(2, 6, 2, at_s(1) + 4)
         less_one_scalar(2, 6)
-        empty_d(2, 4, AT_FREE + 12)
+        empty_d(2, 4, at_w2(0) + 4)
         multiply_gpsimd(2, 4)
         place_y(5, first, AT_FREE + 34)
         empty_y(5, 0, y_sb[5])

@@ -26,7 +26,7 @@ BLOCKS = N // P
 PER_COLUMN = 16
 UNIT = 128
 UNITS = S // UNIT
-FRAMES = 7
+FRAMES = 8
 EARLY_FRAMES = 5
 FIRST_BLOCKS = 3
 KB = 1024
@@ -75,7 +75,7 @@ def tile_list_fibre_equaliser_backward_kernel(
         w1_rest = place_tile("w1_rest", [P, PASSES, N - first_cols], I32, AT_W1 + PASSES * first_cols * 4 / KB)
         w1_s = place_tile("w1_s", [P, N], U8, AT_W1_S)
         wgo_sb = place_tile("wgo_sb", [P, S], F32, AT_WGO)
-        frames = [place_tile("frame%d" % f, [P, T2], F32, AT_FRAME + 8 * f) for f in range(FRAMES)]
+        frames = [place_tile("frame%d" % f, [P, T2], F32, AT_FRAME + 8 * f if f < FRAMES - 1 else at_s(2)) for f in range(FRAMES)]
 
         def listed(tile, cols):
             return tile[:, cols.start // PER_COLUMN : cols.stop // PER_COLUMN]
@@ -142,7 +142,7 @@ def tile_list_fibre_equaliser_backward_kernel(
 
         def gather_s(k):
             a, t = divmod(k, PACK)
-            for cols in halves if k in (3, 7) else [whole]:
+            for cols in halves if k % PACK == PACK - 1 else [whole]:
                 nc.vector.tensor_copy(picked[a][:, t, cols], s_sb[k].indirect(listed(idx, cols)))
 
         def first_product(a, u, number):
@@ -177,8 +177,11 @@ def tile_list_fibre_equaliser_backward_kernel(
                     d_bank[a, u + e][:].rearrange("p (t c) -> p c t", t=PACK),
                 )
 
-        def less_one_scalar(a, u):
-            nc.scalar.activation(factor[a, u][:], factor[a, u][:], ACT.Copy, bias=-1.0)
+        def less_one_scalar(a, u, kib=None):
+            squares = factor[a, u]
+            if kib is not None:
+                factor[a, u] = place_tile("f%d_%d" % (a, u), [P, 2 * HALF], F32, kib)
+            nc.scalar.activation(factor[a, u][:], squares[:], ACT.Copy, bias=-1.0)
 
         def less_one_gpsimd(a, u, kib=None):
             squares = factor[a, u]
@@ -187,6 +190,8 @@ def tile_list_fibre_equaliser_backward_kernel(
             nc.gpsimd.tensor_scalar(factor[a, u][:], squares[:], 1.0, -1.0, ALU.mult, ALU.add)
 
         def h_cols(a, u, count):
+            if (a, u) == (1, 2):
+                return h_apart[:]
             return h_bf[a, u // 4][:, u % 4 * HALF : (u % 4 + count) * HALF]
 
         def multiply_gpsimd(a, u, e=0, count=2):
@@ -257,23 +262,24 @@ def tile_list_fibre_equaliser_backward_kernel(
         quantize_w2(0, AT_FREE + 44)
         for u in range(UNITS):
             first_product(0, u, u)
-        for frame in frames[EARLY_FRAMES:]:
-            nc.gpsimd.memset(frame[:], 0.0)
         for u in (0, 2):
             empty_d(0, u, AT_FREE + 24 + 2 * u)
         empty_d(0, 4, AT_FREE + 32)
-        for k in (1, 2, 3):
+        for k in (1, 2):
             gather_s(k)
+        for frame in frames[EARLY_FRAMES:]:
+            nc.gpsimd.memset(frame[:], 0.0)
+        gather_s(3)
         place_h(0, 0, at_w2(0) + 4)
         square(0, 0, 2, AT_FREE + 36)
         less_one_gpsimd(0, 0)
         multiply_gpsimd(0, 0)
-        square(0, 2, 2, AT_FREE + 40)
         square(0, 6, 2, at_s(3))
+        square(0, 2, 2, AT_FREE + 40)
         less_one_scalar(0, 2)
         multiply_gpsimd(0, 2)
 
-        place_picked(1, at_s(1))
+        place_picked(1, at_s(0))
         gather_s(4)
         place_h(0, 1, at_s(4))
         for e in range(2):
@@ -296,89 +302,89 @@ def tile_list_fibre_equaliser_backward_kernel(
         square(1, 2, 2, AT_FREE + 40)
         empty_d(1, 2, at_s(7))
         less_one_scalar(1, 2)
-        multiply_gpsimd(1, 2)
-        square(1, 6, 2, at_w2(0))
         round_w2(2, at_s(5))
         square(1, 4, 2, at_w2(2))
 
         place_picked(2, AT_TAB)
         for k in (8, 9, 10):
             gather_s(k)
-        late = place_tile("h_bf_late", [P, 2 * HALF * PACK], BF16, at_s(10))
-        h_bf[1, 1] = late[:, : HALF * PACK]
-        h_bf[2, 1] = late[:, HALF * PACK :]
-        for e in range(2):
-            multiply_vector(1, 6, e)
-        gather_s(11)
-        quantize_w2(2, at_s(11))
-        quantize_h(0, 0, at_s(11) + 3, at_s(11) + 5)
-        less_one_gpsimd(1, 4, at_w2(0) + 4)
+        quantize_h(0, 0, at_s(10), at_s(10) + 2)
+        quantize_w2(2, at_s(10) + 3)
+        h_apart = place_tile("h_apart", [P, 2 * HALF], BF16, at_s(5))
+        multiply_gpsimd(1, 2)
         for u in range(4):
             first_product(2, u, u)
+        gather_s(11)
         place_h(2, 0, at_s(8))
         for u in range(4):
-            square(2, u, 1, AT_FREE + 36 + 2 * u)
+            square(2, u, 1, at_s(9) + 2 * u)
             multiply_vector(2, u)
-        quantize_h(1, 0, AT_FREE + 40, at_s(11) + 5.5)
+        h_w[1, 0] = place_tile("h_w10", [P, HALF], U32, at_s(9) + 4)[:]
+        h_s[1, 0] = place_tile("h_s10", [P, HALF], U8, at_s(10) + 6)[:]
+        for part, source in enumerate((h_bf[1, 0][:, : 2 * HALF], h_apart[:])):
+            cols = slice(part * 2 * UNIT, (part + 1) * 2 * UNIT)
+            nc.vector.quantize_mx(out=h_w[1, 0][:, cols].bitcast(E4M3), scales=h_s[1, 0][:, cols], in_=source)
         quantize_h(2, 0, at_s(8) + 4, at_s(8) + 6)
-        quantize_h(0, 1, AT_FREE + 42, at_s(11) + 6)
+        quantize_h(0, 1, at_s(9) + 6, at_s(10) + 6.5)
         orders = ((0, 1, 2), (0, 2, 1))
         for part in (slice(0, 1), slice(1, PASSES)):
             for n in range(2):
-                second_product(n, 0, 6 + n, orders[n], part)
-        for n in range(2, 6):
-            second_product(n, 0, n - 2, (2, 0, 1))
+                second_product(n, 0, n, orders[n], part)
+        for n in (2, 3):
+            second_product(n, 0, n, (2, 0, 1))
         place_y(0, first, AT_FREE + 44)
         nc.vector.scalar_tensor_tensor(y_sb[0], y_bank[0, 0][:], -1.0, wgo_sb[:, first], ALU.mult, ALU.mult)
         put_weighed(0)
 
-        square(2, 4, 2, at_s(1))
+        late = place_tile("h_bf_late", [P, 2 * HALF * PACK], BF16, at_s(11))
+        h_bf[1, 1] = late[:, : HALF * PACK]
+        h_bf[2, 1] = late[:, HALF * PACK :]
+        square(1, 6, 2, at_s(9))
+        less_one_scalar(1, 4, at_s(4) + 4)
         for n in (1, 2):
             place_y(n, first, AT_FREE + 20 + 4 * n)
             empty_y(n, 0, y_sb[n])
             weigh_gpsimd(n, at_s(4) + 2 * n - 2)
             put_weighed(n)
+        for n in (4, 5):
+            second_product(n, 0, n - 4, (2, 0, 1))
         empty_d(1, 4, AT_FREE + 24)
         multiply_gpsimd(1, 4)
+        less_one_scalar(1, 6)
+        empty_d(1, 6, AT_FREE + 28)
         for n in (3, 4):
-            place_y(n, first, AT_FREE + 24 + 2 * n)
+            place_y(n, first, AT_FREE + 26 + 2 * n)
             empty_y(n, 0, y_sb[n])
             weigh_gpsimd(n)
             put_weighed(n)
+        multiply_gpsimd(1, 6)
+        for n in (6, 7):
+            second_product(n, 0, n - 4, (2, 0, 1))
         for u in range(4, UNITS):
-            first_product(2, u, (6, 7, 0, 1)[u - 4])
-        less_one_scalar(2, 4)
-        square(2, 6, 2, at_s(1) + 4)
-        less_one_scalar(2, 6)
-        empty_d(2, 4, at_w2(0) + 4)
-        multiply_gpsimd(2, 4)
-        place_y(5, first, AT_FREE + 34)
-        empty_y(5, 0, y_sb[5])
-        weigh_gpsimd(5)
-        put_weighed(5)
-        empty_d(2, 6, AT_FREE + 24)
-        multiply_gpsimd(2, 6)
-        second_product(6, 0, 2, (2, 0, 1))
-        place_y(6, first, AT_FREE + 24)
-        empty_y(6, 0, y_sb[6])
-        late_w = place_tile("h_w_late", [P, 2 * HALF], U32, at_s(9))
-        late_s = place_tile("h_s_late", [P, 2 * HALF], U8, at_s(9) + 4)
+            first_product(2, u, u)
+        for u in (4, 6):
+            n = 3 + u // 2
+            square(2, u, 2, at_s(1) + 2 * u - 8)
+            less_one_scalar(2, u)
+            place_y(n, first, at_s(3) + u - 4)
+            empty_y(n, 0, y_sb[n])
+            weigh_gpsimd(n)
+            put_weighed(n)
+            empty_d(2, u, AT_FREE + 16 + 2 * u)
+            multiply_gpsimd(2, u)
+        place_y(7, first, AT_FREE + 28)
+        empty_y(7, 0, y_sb[7])
+        late_w = place_tile("h_w_late", [P, 2 * HALF], U32, at_s(7))
+        late_s = place_tile("h_s_late", [P, 2 * HALF], U8, at_s(7) + 4)
         nc.vector.quantize_mx(out=late_w[:].bitcast(E4M3), scales=late_s[:], in_=late[:])
         for a in (1, 2):
             h_w[a, 1] = late_w[:, halves[a - 1]]
             h_s[a, 1] = late_s[:, halves[a - 1]]
-        weigh_and_put(6, first)
+        weigh_and_put(7, first)
 
-        for n in range(FRAMES):
-            second_product(n, 1, (3, 4, 5, 6, 7, 0, 1)[n], (1, 2, 0))
+        for n in range(BLOCKS):
+            second_product(n, 1, (n + 4) % 8, (1, 2, 0))
             place_y(n, second, at_w2(0) + 2 * n)
             empty_y(n, 1, y_sb[n])
             weigh_and_put(n, second)
-            store(n)
-        for n in range(FRAMES, BLOCKS):
-            place_y(n, whole, at_s(10))
-            for half in range(2):
-                second_product(n, half, 2 + half, (1, 2, 0))
-                empty_y(n, half, y_sb[n][:, halves[half]])
-            weigh_and_put(n, whole)
             store(n)

@@ -27,7 +27,7 @@ PER_COLUMN = 16
 UNIT = 128
 UNITS = S // UNIT
 FRAMES = 8
-EARLY_FRAMES = 5
+EARLY_FRAMES = 4
 FIRST_BLOCKS = 3
 KB = 1024
 
@@ -91,7 +91,7 @@ def tile_list_fibre_equaliser_backward_kernel(
 
         def load_s(k):
             a, t = divmod(k, PACK)
-            s_sb[k] = place_tile("s%d" % k, [P, T], F32, at_s(k))[:]
+            s_sb[k] = place_tile("s%d" % k, [P, T], F32, AT_FRAME + 8 * EARLY_FRAMES if k == 1 else at_s(k))[:]
             nc.sync.dma_start(s_sb[k], s_rows[a][:, t, :])
 
         def load_w2(a):
@@ -256,7 +256,7 @@ def tile_list_fibre_equaliser_backward_kernel(
 
         nc.vector.tensor_copy(v_w[:], tab_w[:].bitcast(U32).indirect(idx[:]))
         nc.vector.tensor_copy(v_s[:], tab_s[:].indirect(idx[:]))
-        round_w2(0, AT_FRAME + 8 * (EARLY_FRAMES + 1) - 2)
+        round_w2(0, AT_FRAME + 8 * (EARLY_FRAMES + 2) - 2)
         place_picked(0, AT_TAB)
         gather_s(0)
         quantize_w2(0, AT_FREE + 44)
@@ -267,14 +267,14 @@ def tile_list_fibre_equaliser_backward_kernel(
         empty_d(0, 4, AT_FREE + 32)
         for k in (1, 2):
             gather_s(k)
-        for frame in frames[EARLY_FRAMES:]:
-            nc.gpsimd.memset(frame[:], 0.0)
+        for f in (5, 6, 4, 7):
+            nc.gpsimd.memset(frames[f][:], 0.0)
         gather_s(3)
         place_h(0, 0, at_w2(0) + 4)
         square(0, 0, 2, AT_FREE + 36)
-        less_one_gpsimd(0, 0)
-        multiply_gpsimd(0, 0)
         square(0, 6, 2, at_s(3))
+        less_one_scalar(0, 0)
+        multiply_gpsimd(0, 0)
         square(0, 2, 2, AT_FREE + 40)
         less_one_scalar(0, 2)
         multiply_gpsimd(0, 2)
@@ -300,9 +300,9 @@ def tile_list_fibre_equaliser_backward_kernel(
         less_one_scalar(1, 0)
         multiply_gpsimd(1, 0)
         square(1, 2, 2, AT_FREE + 40)
-        empty_d(1, 2, at_s(7))
         less_one_scalar(1, 2)
         round_w2(2, at_s(5))
+        empty_d(1, 2, at_w2(2) + 4)
         square(1, 4, 2, at_w2(2))
 
         place_picked(2, AT_TAB)

@@ -183,12 +183,6 @@ def tile_list_fibre_equaliser_backward_kernel(
                 factor[a, u] = place_tile("f%d_%d" % (a, u), [P, 2 * HALF], F32, kib)
             nc.scalar.activation(factor[a, u][:], squares[:], ACT.Copy, bias=-1.0)
 
-        def less_one_gpsimd(a, u, kib=None):
-            squares = factor[a, u]
-            if kib is not None:
-                factor[a, u] = place_tile("f%d_%d" % (a, u), [P, 2 * HALF], F32, kib)
-            nc.gpsimd.tensor_scalar(factor[a, u][:], squares[:], 1.0, -1.0, ALU.mult, ALU.add)
-
         def h_cols(a, u, count):
             if (a, u) == (1, 2):
                 return h_apart[:]
@@ -289,7 +283,7 @@ def tile_list_fibre_equaliser_backward_kernel(
         for k in (5, 6):
             gather_s(k)
         quantize_w2(1, at_s(6) + 4)
-        less_one_gpsimd(0, 4, at_w2(0))
+        less_one_scalar(0, 4, at_w2(0))
         multiply_gpsimd(0, 4)
         for u in range(UNITS):
             first_product(1, u, u)
@@ -319,6 +313,7 @@ def tile_list_fibre_equaliser_backward_kernel(
         for u in range(4):
             square(2, u, 1, at_s(9) + 2 * u)
             multiply_vector(2, u)
+        empty_d(1, 4, at_s(9))
         h_w[1, 0] = place_tile("h_w10", [P, HALF], U32, at_s(9) + 4)[:]
         h_s[1, 0] = place_tile("h_s10", [P, HALF], U8, at_s(10) + 6)[:]
         for part, source in enumerate((h_bf[1, 0][:, : 2 * HALF], h_apart[:])):
@@ -331,56 +326,57 @@ def tile_list_fibre_equaliser_backward_kernel(
             for n in range(2):
                 second_product(n, 0, n, orders[n], part)
         for n in (2, 3):
-            second_product(n, 0, n, (2, 0, 1))
+            second_product(n, 0, n + 2, (2, 0, 1))
         place_y(0, first, AT_FREE + 44)
         nc.vector.scalar_tensor_tensor(y_sb[0], y_bank[0, 0][:], -1.0, wgo_sb[:, first], ALU.mult, ALU.mult)
         put_weighed(0)
 
-        late = place_tile("h_bf_late", [P, 2 * HALF * PACK], BF16, at_s(11))
+        late = place_tile("h_bf_late", [P, 2 * HALF * PACK], BF16, at_s(3) + 4)
         h_bf[1, 1] = late[:, : HALF * PACK]
         h_bf[2, 1] = late[:, HALF * PACK :]
-        square(1, 6, 2, at_s(9))
         less_one_scalar(1, 4, at_s(4) + 4)
+        multiply_gpsimd(1, 4)
+        square(1, 6, 2, at_s(8))
         for n in (1, 2):
             place_y(n, first, AT_FREE + 20 + 4 * n)
             empty_y(n, 0, y_sb[n])
-            weigh_gpsimd(n, at_s(4) + 2 * n - 2)
+            weigh_gpsimd(n, at_s(11) + 2 * n)
             put_weighed(n)
         for n in (4, 5):
-            second_product(n, 0, n - 4, (2, 0, 1))
-        empty_d(1, 4, AT_FREE + 24)
-        multiply_gpsimd(1, 4)
-        less_one_scalar(1, 6)
+            second_product(n, 0, n - 2, (2, 0, 1))
+        less_one_scalar(1, 6, AT_FREE + 24)
         empty_d(1, 6, AT_FREE + 28)
+        multiply_gpsimd(1, 6)
         for n in (3, 4):
             place_y(n, first, AT_FREE + 26 + 2 * n)
             empty_y(n, 0, y_sb[n])
             weigh_gpsimd(n)
             put_weighed(n)
-        multiply_gpsimd(1, 6)
         for n in (6, 7):
-            second_product(n, 0, n - 4, (2, 0, 1))
+            second_product(n, 0, n - 2, (2, 0, 1))
         for u in range(4, UNITS):
-            first_product(2, u, u)
+            first_product(2, u, u if u > 5 else u - 4)
         for u in (4, 6):
-            n = 3 + u // 2
             square(2, u, 2, at_s(1) + 2 * u - 8)
             less_one_scalar(2, u)
-            place_y(n, first, at_s(3) + u - 4)
-            empty_y(n, 0, y_sb[n])
-            weigh_gpsimd(n)
-            put_weighed(n)
             empty_d(2, u, AT_FREE + 16 + 2 * u)
             multiply_gpsimd(2, u)
-        place_y(7, first, AT_FREE + 28)
-        empty_y(7, 0, y_sb[7])
+            if u == 4:
+                place_y(5, first, at_s(3))
+                empty_y(5, 0, y_sb[5])
+                weigh_gpsimd(5)
+                put_weighed(5)
+        for n in (6, 7):
+            place_y(n, first, AT_FREE + 16 + 2 * n)
+            empty_y(n, 0, y_sb[n])
         late_w = place_tile("h_w_late", [P, 2 * HALF], U32, at_s(7))
         late_s = place_tile("h_s_late", [P, 2 * HALF], U8, at_s(7) + 4)
         nc.vector.quantize_mx(out=late_w[:].bitcast(E4M3), scales=late_s[:], in_=late[:])
         for a in (1, 2):
             h_w[a, 1] = late_w[:, halves[a - 1]]
             h_s[a, 1] = late_s[:, halves[a - 1]]
-        weigh_and_put(7, first)
+        for n in (6, 7):
+            weigh_and_put(n, first)
 
         for n in range(BLOCKS):
             second_product(n, 1, (n + 4) % 8, (1, 2, 0))

@@ -27,8 +27,9 @@ PER_COLUMN = 16
 UNIT = 128
 UNITS = S // UNIT
 FRAMES = 8
-EARLY_FRAMES = 4
+EARLY_FRAMES = 3
 FIRST_BLOCKS = 3
+LEAD = 512
 KB = 1024
 
 AT_W2 = 96
@@ -36,10 +37,10 @@ AT_TAB = 200
 AT_FRAME = 120
 AT_W1 = 176
 AT_WGO = 188
-AT_TAB_S = 192
-AT_V_W = 194
-AT_V_S = 198
-AT_W1_S = 199
+AT_TAB_S = 168
+AT_V_W = 170
+AT_V_S = 174
+AT_W1_S = 175
 AT_FREE = 192
 
 
@@ -66,7 +67,7 @@ def tile_list_fibre_equaliser_backward_kernel(
 
         idx = lists.tile([P, S // PER_COLUMN], U16, name="idx")
         idx2 = lists.tile([P, S // PER_COLUMN], U16, name="idx2")
-        tab_w = place_tile("tab_w", [P, T], I32, AT_TAB)
+        tab_w = place_tile("tab_w", [P, T], I32, AT_FREE + 24)
         tab_s = place_tile("tab_s", [P, T], U8, AT_TAB_S)
         v_w = place_tile("v_w", [P, S], U32, AT_V_W)
         v_s = place_tile("v_s", [P, S], U8, AT_V_S)
@@ -75,7 +76,7 @@ def tile_list_fibre_equaliser_backward_kernel(
         w1_rest = place_tile("w1_rest", [P, PASSES, N - first_cols], I32, AT_W1 + PASSES * first_cols * 4 / KB)
         w1_s = place_tile("w1_s", [P, N], U8, AT_W1_S)
         wgo_sb = place_tile("wgo_sb", [P, S], F32, AT_WGO)
-        frames = [place_tile("frame%d" % f, [P, T2], F32, AT_FRAME + 8 * f if f < FRAMES - 1 else at_s(2)) for f in range(FRAMES)]
+        frames = [place_tile("frame%d" % f, [P, T2], F32, {6: AT_TAB - 8, 7: at_s(2)}.get(f, AT_FRAME + 8 * f)) for f in range(FRAMES)]
 
         def listed(tile, cols):
             return tile[:, cols.start // PER_COLUMN : cols.stop // PER_COLUMN]
@@ -91,8 +92,16 @@ def tile_list_fibre_equaliser_backward_kernel(
 
         def load_s(k):
             a, t = divmod(k, PACK)
-            s_sb[k] = place_tile("s%d" % k, [P, T], F32, AT_FRAME + 8 * EARLY_FRAMES if k == 1 else at_s(k))[:]
+            s_sb[k] = place_tile("s%d" % k, [P, T], F32, {0: AT_FRAME + 8 * (EARLY_FRAMES + 1) + 4, 1: AT_FRAME + 8 * EARLY_FRAMES}.get(k, at_s(k)))[:]
             nc.sync.dma_start(s_sb[k], s_rows[a][:, t, :])
+
+        def load_last_w2():
+            rows = w2[:, (PASSES - 1) * PASS :].rearrange("(p j) c -> p j c", j=PACK)
+            for e in range(2):
+                w2_raw[PASSES - 1, e] = place_tile(
+                    "w2_last%d" % e, [P, PACK, PASS // 2], F32, at_w2(PASSES - 1) + 4 * (1 - e)
+                )
+                nc.sync.dma_start(w2_raw[PASSES - 1, e][:], rows[:, :, e * PASS // 2 : (e + 1) * PASS // 2])
 
         def load_w2(a):
             w2_raw[a] = place_tile("w2_raw%d" % a, [P, PACK, PASS], F32, at_w2(a))
@@ -101,15 +110,19 @@ def tile_list_fibre_equaliser_backward_kernel(
             )
 
         nc.sync.dma_start(idx[:], offs)
-        nc.sync.dma_start(tab_w[:], tab_words[0].rearrange("p t i -> p (t i)").bitcast(I32))
+        words = tab_words[0].rearrange("p t i -> p (t i)").bitcast(I32)
+        nc.sync.dma_start(tab_w[:, :LEAD], words[:, :LEAD])
         for q in range(4):
             nc.sync.dma_start(
                 tab_s[32 * q : 32 * q + 4, :].bitcast(I32), tab_scales[0, 4 * q : 4 * q + 4, :].bitcast(I32)
             )
-        w2_before = {0: 0, 5: 1, 11: 2}
+        nc.sync.dma_start(tab_w[:, LEAD:], words[:, LEAD:])
+        w2_before = {0: 0, 7: 1}
         for k in range(SLICES):
             if k in w2_before:
                 load_w2(w2_before[k])
+            if k == SLICES - 1:
+                load_last_w2()
             load_s(k)
         for q in range(4):
             nc.sync.dma_start(
@@ -126,11 +139,23 @@ def tile_list_fibre_equaliser_backward_kernel(
         halves = [slice(0, HALF), slice(HALF, S)]
         first, second = halves
 
-        def round_w2(a, kib):
+        def round_w2(a, kib, shared=False):
             w2_bf[a] = place_tile("w2_bf%d" % a, [P, PASS * PACK], BF16, kib)
             rounded = w2_bf[a][:].rearrange("p (t m j) -> p m j t", t=PACK, j=PACK)
             raw = w2_raw[a][:].rearrange("p j (m t) -> p m j t", t=PACK)
-            nc.scalar.copy(rounded, raw)
+            if shared:
+                nc.scalar.copy(rounded[:, :, :, :2], raw[:, :, :, :2])
+                nc.vector.tensor_copy(rounded[:, :, :, 2:], raw[:, :, :, 2:])
+            else:
+                nc.scalar.copy(rounded, raw)
+
+        def round_last_w2(kib):
+            a = PASSES - 1
+            w2_bf[a] = place_tile("w2_bf%d" % a, [P, PASS * PACK], BF16, kib)
+            rounded = w2_bf[a][:].rearrange("p (t m j) -> p m j t", t=PACK, j=PACK)
+            for e in range(2):
+                raw = w2_raw[a, e][:].rearrange("p j (m t) -> p m j t", t=PACK)
+                nc.scalar.copy(rounded[:, e * P // 2 : (e + 1) * P // 2], raw)
 
         def quantize_w2(a, kib):
             w2_w[a] = place_tile("w2_w%d" % a, [P, PASS], U32, kib)
@@ -248,12 +273,12 @@ def tile_list_fibre_equaliser_backward_kernel(
         def store(n):
             nc.sync.dma_start(out[n * P : (n + 1) * P, :], frames[n % FRAMES][:])
 
-        nc.vector.tensor_copy(v_w[:], tab_w[:].bitcast(U32).indirect(idx[:]))
         nc.vector.tensor_copy(v_s[:], tab_s[:].indirect(idx[:]))
-        round_w2(0, AT_FRAME + 8 * (EARLY_FRAMES + 2) - 2)
+        nc.vector.tensor_copy(v_w[:], tab_w[:].bitcast(U32).indirect(idx[:]))
+        round_w2(0, AT_TAB - 2, shared=True)
+        quantize_w2(0, AT_FREE + 44)
         place_picked(0, AT_TAB)
         gather_s(0)
-        quantize_w2(0, AT_FREE + 44)
         for u in range(UNITS):
             first_product(0, u, u)
         for u in (0, 2):
@@ -261,43 +286,43 @@ def tile_list_fibre_equaliser_backward_kernel(
         empty_d(0, 4, AT_FREE + 32)
         for k in (1, 2):
             gather_s(k)
-        for f in (5, 6, 4, 7):
+        for f in (6, 4, 5, 3, 7):
             nc.gpsimd.memset(frames[f][:], 0.0)
         gather_s(3)
         place_h(0, 0, at_w2(0) + 4)
         square(0, 0, 2, AT_FREE + 36)
-        square(0, 6, 2, at_s(3))
         less_one_scalar(0, 0)
         multiply_gpsimd(0, 0)
         square(0, 2, 2, AT_FREE + 40)
+        square(0, 6, 2, at_s(3))
         less_one_scalar(0, 2)
         multiply_gpsimd(0, 2)
+        square(0, 4, 2, at_s(3) + 4)
+        less_one_scalar(0, 4)
 
         place_picked(1, at_s(0))
-        gather_s(4)
-        place_h(0, 1, at_s(4))
+        for k in (4, 5):
+            gather_s(k)
+        place_h(0, 1, at_s(5) + 4)
+        multiply_gpsimd(0, 4)
         for e in range(2):
             multiply_vector(0, 6, e)
         round_w2(1, at_w2(0))
-        square(0, 4, 2, at_w2(1) + 4)
-        for k in (5, 6):
+        for k in (6, 7):
             gather_s(k)
-        quantize_w2(1, at_s(6) + 4)
-        less_one_scalar(0, 4, at_w2(0))
-        multiply_gpsimd(0, 4)
+        square(1, 0, 2, AT_FREE + 36)
+        less_one_scalar(1, 0)
+        quantize_w2(1, at_s(7) + 5)
         for u in range(UNITS):
             first_product(1, u, u)
         empty_d(1, 0, AT_FREE + 24)
-        gather_s(7)
         place_h(1, 0, at_s(4) + 4)
-        square(1, 0, 2, AT_FREE + 36)
-        less_one_scalar(1, 0)
         multiply_gpsimd(1, 0)
         square(1, 2, 2, AT_FREE + 40)
         less_one_scalar(1, 2)
-        round_w2(2, at_s(5))
-        empty_d(1, 2, at_w2(2) + 4)
-        square(1, 4, 2, at_w2(2))
+        round_last_w2(at_s(5))
+        empty_d(1, 2, at_w2(2) + 2)
+        square(1, 4, 2, at_w2(2) - 2)
 
         place_picked(2, AT_TAB)
         for k in (8, 9, 10):
@@ -311,43 +336,64 @@ def tile_list_fibre_equaliser_backward_kernel(
         gather_s(11)
         place_h(2, 0, at_s(8))
         for u in range(4):
-            square(2, u, 1, at_s(9) + 2 * u)
+            square(2, u, 1, at_s(9) + 2 + 2 * u if u < 2 else at_s(3) + 2 * u)
             multiply_vector(2, u)
-        empty_d(1, 4, at_s(9))
-        h_w[1, 0] = place_tile("h_w10", [P, HALF], U32, at_s(9) + 4)[:]
-        h_s[1, 0] = place_tile("h_s10", [P, HALF], U8, at_s(10) + 6)[:]
-        for part, source in enumerate((h_bf[1, 0][:, : 2 * HALF], h_apart[:])):
-            cols = slice(part * 2 * UNIT, (part + 1) * 2 * UNIT)
-            nc.vector.quantize_mx(out=h_w[1, 0][:, cols].bitcast(E4M3), scales=h_s[1, 0][:, cols], in_=source)
-        quantize_h(2, 0, at_s(8) + 4, at_s(8) + 6)
-        quantize_h(0, 1, at_s(9) + 6, at_s(10) + 6.5)
-        orders = ((0, 1, 2), (0, 2, 1))
-        for part in (slice(0, 1), slice(1, PASSES)):
-            for n in range(2):
-                second_product(n, 0, n, orders[n], part)
+        less_one_scalar(1, 4, at_s(9))
+        empty_d(1, 4, at_s(9) + 4)
+        for a, kib, scales_kib in ((1, at_s(3) + 4, at_s(10) + 6), (2, at_s(4) + 4, at_s(8) + 6)):
+            h_w[a, 0] = place_tile("h_w%d0" % a, [P, HALF], U32, kib)[:]
+            h_s[a, 0] = place_tile("h_s%d0" % a, [P, HALF], U8, scales_kib)[:]
+        pairs = {(1, 0): h_bf[1, 0][:, : 2 * HALF], (1, 1): h_apart[:]}
+        pairs.update({(2, part): h_bf[2, 0][:, part * 2 * HALF : (part + 1) * 2 * HALF] for part in range(2)})
+        quarters = [slice(part * 2 * UNIT, (part + 1) * 2 * UNIT) for part in range(2)]
+        y_first = [bank("y_first%d" % part, part)[:, : 2 * UNIT] for part in range(2)]
+
+        def first_block_pass(a, part):
+            nc.tensor.matmul_mx(
+                out=y_first[part],
+                lhsT=w1_first[:, a, :P].bitcast(E4M3),
+                lhsT_scale=w1_s[4 * a :, :P],
+                rhs=h_w[a, 0][:, quarters[part]].bitcast(E4M3),
+                rhs_scale=h_s[a, 0][:, quarters[part]],
+                start=(a == 0),
+                stop=(a == PASSES - 1),
+            )
+
+        for part in range(2):
+            first_block_pass(0, part)
+        second_product(1, 0, 2, (0, 2, 1), slice(0, 1))
+        for a in (1, 2):
+            for part, cols in enumerate(quarters):
+                nc.vector.quantize_mx(
+                    out=h_w[a, 0][:, cols].bitcast(E4M3), scales=h_s[a, 0][:, cols], in_=pairs[a, part]
+                )
+                first_block_pass(a, part)
+        quantize_h(0, 1, at_s(3) + 6, at_s(10) + 6.5)
+        second_product(1, 0, 2, (0, 2, 1), slice(1, PASSES))
         for n in (2, 3):
             second_product(n, 0, n + 2, (2, 0, 1))
         place_y(0, first, AT_FREE + 44)
-        nc.vector.scalar_tensor_tensor(y_sb[0], y_bank[0, 0][:], -1.0, wgo_sb[:, first], ALU.mult, ALU.mult)
+        for part, cols in enumerate(quarters):
+            nc.vector.scalar_tensor_tensor(y_sb[0][:, cols], y_first[part], -1.0, wgo_sb[:, cols], ALU.mult, ALU.mult)
         put_weighed(0)
 
-        late = place_tile("h_bf_late", [P, 2 * HALF * PACK], BF16, at_s(3) + 4)
+        late = place_tile("h_bf_late", [P, 2 * HALF * PACK], BF16, at_s(7) + 4)
         h_bf[1, 1] = late[:, : HALF * PACK]
         h_bf[2, 1] = late[:, HALF * PACK :]
-        less_one_scalar(1, 4, at_s(4) + 4)
         multiply_gpsimd(1, 4)
-        square(1, 6, 2, at_s(8))
+        square(1, 6, 2, at_s(5) + 4)
         for n in (1, 2):
             place_y(n, first, AT_FREE + 20 + 4 * n)
             empty_y(n, 0, y_sb[n])
             weigh_gpsimd(n, at_s(11) + 2 * n)
             put_weighed(n)
         for n in (4, 5):
-            second_product(n, 0, n - 2, (2, 0, 1))
+            second_product(n, 0, 7 - n, (2, 0, 1))
         less_one_scalar(1, 6, AT_FREE + 24)
-        empty_d(1, 6, AT_FREE + 28)
-        multiply_gpsimd(1, 6)
         for n in (3, 4):
+            if n == 4:
+                empty_d(1, 6, AT_FREE + 28)
+                multiply_gpsimd(1, 6)
             place_y(n, first, AT_FREE + 26 + 2 * n)
             empty_y(n, 0, y_sb[n])
             weigh_gpsimd(n)
@@ -369,8 +415,8 @@ def tile_list_fibre_equaliser_backward_kernel(
         for n in (6, 7):
             place_y(n, first, AT_FREE + 16 + 2 * n)
             empty_y(n, 0, y_sb[n])
-        late_w = place_tile("h_w_late", [P, 2 * HALF], U32, at_s(7))
-        late_s = place_tile("h_s_late", [P, 2 * HALF], U8, at_s(7) + 4)
+        late_w = place_tile("h_w_late", [P, 2 * HALF], U32, at_s(6) + 4)
+        late_s = place_tile("h_s_late", [P, 2 * HALF], U8, at_s(7))
         nc.vector.quantize_mx(out=late_w[:].bitcast(E4M3), scales=late_s[:], in_=late[:])
         for a in (1, 2):
             h_w[a, 1] = late_w[:, halves[a - 1]]

@@ -76,7 +76,7 @@ def tile_list_fibre_equaliser_backward_kernel(
         w1_rest = place_tile("w1_rest", [P, PASSES, N - first_cols], I32, AT_W1 + PASSES * first_cols * 4 / KB)
         w1_s = place_tile("w1_s", [P, N], U8, AT_W1_S)
         wgo_sb = place_tile("wgo_sb", [P, S], F32, AT_WGO)
-        frames = [place_tile("frame%d" % f, [P, T2], F32, {6: AT_TAB - 8, 7: at_s(2)}.get(f, AT_FRAME + 8 * f)) for f in range(FRAMES)]
+        frames = [place_tile("frame%d" % f, [P, T2], F32, {6: AT_TAB - 8, 7: at_s(7) + 4}.get(f, AT_FRAME + 8 * f)) for f in range(FRAMES)]
 
         def listed(tile, cols):
             return tile[:, cols.start // PER_COLUMN : cols.stop // PER_COLUMN]
@@ -95,13 +95,11 @@ def tile_list_fibre_equaliser_backward_kernel(
             s_sb[k] = place_tile("s%d" % k, [P, T], F32, {0: AT_FRAME + 8 * (EARLY_FRAMES + 1) + 4, 1: AT_FRAME + 8 * EARLY_FRAMES}.get(k, at_s(k)))[:]
             nc.sync.dma_start(s_sb[k], s_rows[a][:, t, :])
 
-        def load_last_w2():
-            rows = w2[:, (PASSES - 1) * PASS :].rearrange("(p j) c -> p j c", j=PACK)
+        def load_w2_halves(a):
+            rows = w2[:, a * PASS : (a + 1) * PASS].rearrange("(p j) c -> p j c", j=PACK)
             for e in range(2):
-                w2_raw[PASSES - 1, e] = place_tile(
-                    "w2_last%d" % e, [P, PACK, PASS // 2], F32, at_w2(PASSES - 1) + 4 * (1 - e)
-                )
-                nc.sync.dma_start(w2_raw[PASSES - 1, e][:], rows[:, :, e * PASS // 2 : (e + 1) * PASS // 2])
+                w2_raw[a, e] = place_tile("w2_raw%d%d" % (a, e), [P, PACK, PASS // 2], F32, at_w2(a) + 4 * (1 - e))
+                nc.sync.dma_start(w2_raw[a, e][:], rows[:, :, e * PASS // 2 : (e + 1) * PASS // 2])
 
         def load_w2(a):
             w2_raw[a] = place_tile("w2_raw%d" % a, [P, PACK, PASS], F32, at_w2(a))
@@ -117,12 +115,11 @@ def tile_list_fibre_equaliser_backward_kernel(
                 tab_s[32 * q : 32 * q + 4, :].bitcast(I32), tab_scales[0, 4 * q : 4 * q + 4, :].bitcast(I32)
             )
         nc.sync.dma_start(tab_w[:, LEAD:], words[:, LEAD:])
-        w2_before = {0: 0, 7: 1}
+        load_w2(0)
+        w2_before = {7: 1, 11: 2}
         for k in range(SLICES):
             if k in w2_before:
-                load_w2(w2_before[k])
-            if k == SLICES - 1:
-                load_last_w2()
+                load_w2_halves(w2_before[k])
             load_s(k)
         for q in range(4):
             nc.sync.dma_start(
@@ -134,10 +131,11 @@ def tile_list_fibre_equaliser_backward_kernel(
         nc.sync.dma_start(idx2[:], offs2)
         nc.sync.dma_start(w1_rest[:], w1_rows[:, :, first_cols:])
 
-        w2_bf, w2_w, w2_s, h_bf, h_w, h_s, picked, factor, d_sb, d_bank, y_bank, y_sb = ({} for i in range(12))
+        w2_bf, w2_w, w2_s, h_pair, h_codes, picked, factor, d_sb, d_bank, y_bank, y_sb = ({} for i in range(11))
         whole = slice(0, S)
         halves = [slice(0, HALF), slice(HALF, S)]
         first, second = halves
+        quarters = [slice(part * 2 * UNIT, (part + 1) * 2 * UNIT) for part in range(2)]
 
         def round_w2(a, kib, shared=False):
             w2_bf[a] = place_tile("w2_bf%d" % a, [P, PASS * PACK], BF16, kib)
@@ -149,8 +147,7 @@ def tile_list_fibre_equaliser_backward_kernel(
             else:
                 nc.scalar.copy(rounded, raw)
 
-        def round_last_w2(kib):
-            a = PASSES - 1
+        def round_w2_halves(a, kib):
             w2_bf[a] = place_tile("w2_bf%d" % a, [P, PASS * PACK], BF16, kib)
             rounded = w2_bf[a][:].rearrange("p (t m j) -> p m j t", t=PACK, j=PACK)
             for e in range(2):
@@ -167,7 +164,10 @@ def tile_list_fibre_equaliser_backward_kernel(
 
         def gather_s(k):
             a, t = divmod(k, PACK)
-            for cols in halves if k % PACK == PACK - 1 else [whole]:
+            pieces = halves if k % PACK == PACK - 1 else [whole]
+            if k == SLICES - 1:
+                pieces = [slice(0, UNIT), slice(UNIT, HALF), slice(HALF, S - 2 * UNIT)]
+            for cols in pieces:
                 nc.vector.tensor_copy(picked[a][:, t, cols], s_sb[k].indirect(listed(idx, cols)))
 
         def first_product(a, u, number):
@@ -194,6 +194,19 @@ def tile_list_fibre_equaliser_backward_kernel(
             )
             factor[a, u] = tile
 
+        def square_rows(a, t, cols):
+            nc.scalar.activation(picked[a][:, t, cols], picked[a][:, t, cols], ACT.Square)
+
+        def less_one_from_rows(name, rows, kib):
+            tile = place_tile(name, [P, 2 * HALF], F32, kib)
+            nc.scalar.activation(
+                tile[:].rearrange("p (c i t) -> p c t i", i=4, t=PACK),
+                rows.rearrange("p t (c i) -> p c t i", i=4),
+                ACT.Copy,
+                bias=-1.0,
+            )
+            return tile
+
         def empty_d(a, u, kib):
             d_sb[a, u] = place_tile("d_sb%d_%d" % (a, u), [P, 2 * HALF], F32, kib)
             for e in range(2):
@@ -209,9 +222,7 @@ def tile_list_fibre_equaliser_backward_kernel(
             nc.scalar.activation(factor[a, u][:], squares[:], ACT.Copy, bias=-1.0)
 
         def h_cols(a, u, count):
-            if (a, u) == (1, 2):
-                return h_apart[:]
-            return h_bf[a, u // 4][:, u % 4 * HALF : (u % 4 + count) * HALF]
+            return h_pair[a, u // 2][:, u % 2 * HALF : (u % 2 + count) * HALF]
 
         def multiply_gpsimd(a, u, e=0, count=2):
             cols = slice(e * HALF, (e + count) * HALF)
@@ -227,29 +238,44 @@ def tile_list_fibre_equaliser_backward_kernel(
                 ALU.mult,
             )
 
-        def place_h(a, half, kib):
-            h_bf[a, half] = place_tile("h_bf%d%d" % (a, half), [P, HALF * PACK], BF16, kib)[:]
+        def place_h(pairs, kib):
+            a, pair = pairs[0]
+            tile = place_tile("h_bf%d%d" % (a, pair), [P, len(pairs) * 2 * HALF], BF16, kib)
+            for e, key in enumerate(pairs):
+                h_pair[key] = tile[:, e * 2 * HALF : (e + 1) * 2 * HALF]
+            return tile[:]
 
-        def quantize_h(a, half, kib, scales_kib):
-            h_w[a, half] = place_tile("h_w%d%d" % (a, half), [P, HALF], U32, kib)[:]
-            h_s[a, half] = place_tile("h_s%d%d" % (a, half), [P, HALF], U8, scales_kib)[:]
-            nc.vector.quantize_mx(out=h_w[a, half].bitcast(E4M3), scales=h_s[a, half], in_=h_bf[a, half])
+        def place_codes(name, columns, kib, scales_kib):
+            words = place_tile("h_w" + name, [P, columns], U32, kib)
+            return words[:], place_tile("h_s" + name, [P, columns], U8, scales_kib)[:]
 
-        def second_product(n, half, number, order, part=slice(0, PASSES)):
+        def quantize_h(source, codes):
+            nc.vector.quantize_mx(out=codes[0].bitcast(E4M3), scales=codes[1], in_=source)
+
+        def columns_of(codes, cols):
+            return codes[0][:, cols], codes[1][:, cols]
+
+        def product_pass(target, n, a, codes, start, stop):
             ncols = slice(n * P, (n + 1) * P)
             w1_w = w1_first[:, :, ncols] if n < FIRST_BLOCKS else w1_rest[:, :, n * P - first_cols : (n + 1) * P - first_cols]
+            nc.tensor.matmul_mx(
+                out=target,
+                lhsT=w1_w[:, a, :].bitcast(E4M3),
+                lhsT_scale=w1_s[4 * a :, ncols],
+                rhs=codes[0].bitcast(E4M3),
+                rhs_scale=codes[1],
+                start=start,
+                stop=stop,
+            )
+
+        def second_product(n, half, number, order, part=slice(0, PASSES)):
             for a in order[part]:
                 if a == order[0]:
                     y_bank[n, half] = bank("y%d_%d" % (n, half), number)
-                nc.tensor.matmul_mx(
-                    out=y_bank[n, half][:],
-                    lhsT=w1_w[:, a, :].bitcast(E4M3),
-                    lhsT_scale=w1_s[4 * a :, ncols],
-                    rhs=h_w[a, half].bitcast(E4M3),
-                    rhs_scale=h_s[a, half],
-                    start=(a == order[0]),
-                    stop=(a == order[-1]),
-                )
+                pieces = h_codes[a, half]
+                for e, (cols, codes) in enumerate(pieces):
+                    last = a == order[-1] and e == len(pieces) - 1
+                    product_pass(y_bank[n, half][:, cols], n, a, codes, a == order[0], last)
 
         def place_y(n, cols, kib):
             y_sb[n] = place_tile("y_sb%d_%d" % (n, cols.start), [P, cols.stop - cols.start], F32, kib)[:]
@@ -281,94 +307,88 @@ def tile_list_fibre_equaliser_backward_kernel(
         gather_s(0)
         for u in range(UNITS):
             first_product(0, u, u)
-        for u in (0, 2):
+        for u in (0, 2, 4):
             empty_d(0, u, AT_FREE + 24 + 2 * u)
-        empty_d(0, 4, AT_FREE + 32)
+        square_rows(0, 0, whole)
         for k in (1, 2):
             gather_s(k)
-        for f in (6, 4, 5, 3, 7):
+            square_rows(0, k, whole)
+        for f in (6, 4, 5, 3):
             nc.gpsimd.memset(frames[f][:], 0.0)
         gather_s(3)
-        place_h(0, 0, at_w2(0) + 4)
-        square(0, 0, 2, AT_FREE + 36)
-        less_one_scalar(0, 0)
-        multiply_gpsimd(0, 0)
-        square(0, 2, 2, AT_FREE + 40)
-        square(0, 6, 2, at_s(3))
-        less_one_scalar(0, 2)
-        multiply_gpsimd(0, 2)
-        square(0, 4, 2, at_s(3) + 4)
-        less_one_scalar(0, 4)
+        h_00 = place_h([(0, 0), (0, 1)], at_w2(0) + 4)
+        for u, kib in ((0, AT_FREE + 36), (2, AT_FREE + 40), (4, at_s(4))):
+            for cols in {0: quarters, 4: [second]}.get(u, []):
+                square_rows(0, PACK - 1, cols)
+            factor[0, u] = less_one_from_rows("f0_%d" % u, picked[0][:, :, u * UNIT : (u + 2) * UNIT], kib)
+            if u < 4:
+                multiply_gpsimd(0, u)
 
         place_picked(1, at_s(0))
-        for k in (4, 5):
+        for k in (4, 5, 6):
             gather_s(k)
-        place_h(0, 1, at_s(5) + 4)
-        multiply_gpsimd(0, 4)
-        for e in range(2):
-            multiply_vector(0, 6, e)
-        round_w2(1, at_w2(0))
-        for k in (6, 7):
-            gather_s(k)
-        square(1, 0, 2, AT_FREE + 36)
-        less_one_scalar(1, 0)
-        quantize_w2(1, at_s(7) + 5)
+        round_w2_halves(1, at_w2(0))
+        empty_d(0, 6, at_w2(1) + 2)
+        codes_00 = place_codes("00", HALF, at_s(6), at_s(6) + 2)
+        h_codes[0, 0] = [(first, codes_00)]
+        quantize_h(h_00, codes_00)
+        quantize_w2(1, at_s(6) + 4)
+        h_01 = place_h([(0, 2), (0, 3)], at_w2(0))
+        factor[0, 6] = less_one_from_rows("f0_6", picked[0][:, :, 6 * UNIT :], at_w2(1) - 2)
+        for u in (4, 6):
+            multiply_gpsimd(0, u)
         for u in range(UNITS):
             first_product(1, u, u)
         empty_d(1, 0, AT_FREE + 24)
-        place_h(1, 0, at_s(4) + 4)
+        gather_s(7)
+        square(1, 0, 2, AT_FREE + 36)
+        less_one_scalar(1, 0)
+        place_h([(1, 0)], at_s(4) + 4)
         multiply_gpsimd(1, 0)
         square(1, 2, 2, AT_FREE + 40)
         less_one_scalar(1, 2)
-        round_last_w2(at_s(5))
+        round_w2_halves(2, at_s(5))
         empty_d(1, 2, at_w2(2) + 2)
-        square(1, 4, 2, at_w2(2) - 2)
 
-        place_picked(2, AT_TAB)
+        place_picked(2, at_s(2))
         for k in (8, 9, 10):
             gather_s(k)
-        quantize_h(0, 0, at_s(10), at_s(10) + 2)
+        codes_01 = place_codes("01", HALF, at_s(10), at_s(10) + 2)
+        h_codes[0, 1] = [(first, codes_01)]
+        quantize_h(h_01, codes_01)
+        codes_10 = [place_codes("10", 2 * UNIT, at_s(10) + 6, at_s(10) + 7)]
+        quantize_h(h_pair[1, 0], codes_10[0])
         quantize_w2(2, at_s(10) + 3)
-        h_apart = place_tile("h_apart", [P, 2 * HALF], BF16, at_s(5))
+        place_h([(1, 1)], at_s(5))
         multiply_gpsimd(1, 2)
         for u in range(4):
             first_product(2, u, u)
         gather_s(11)
-        place_h(2, 0, at_s(8))
+        place_h([(2, 0)], at_s(8) + 4)
+        place_h([(2, 1)], at_s(8) + 2)
         for u in range(4):
-            square(2, u, 1, at_s(9) + 2 + 2 * u if u < 2 else at_s(3) + 2 * u)
+            square(2, u, 1, at_s(9) + 2 + 2 * u if u < 2 else AT_TAB + 2 * u)
             multiply_vector(2, u)
-        less_one_scalar(1, 4, at_s(9))
+        square(1, 4, 2, at_s(9))
+        less_one_scalar(1, 4)
         empty_d(1, 4, at_s(9) + 4)
-        for a, kib, scales_kib in ((1, at_s(3) + 4, at_s(10) + 6), (2, at_s(4) + 4, at_s(8) + 6)):
-            h_w[a, 0] = place_tile("h_w%d0" % a, [P, HALF], U32, kib)[:]
-            h_s[a, 0] = place_tile("h_s%d0" % a, [P, HALF], U8, scales_kib)[:]
-        pairs = {(1, 0): h_bf[1, 0][:, : 2 * HALF], (1, 1): h_apart[:]}
-        pairs.update({(2, part): h_bf[2, 0][:, part * 2 * HALF : (part + 1) * 2 * HALF] for part in range(2)})
-        quarters = [slice(part * 2 * UNIT, (part + 1) * 2 * UNIT) for part in range(2)]
+        codes_10.append(place_codes("11", 2 * UNIT, AT_TAB + 4, at_s(10) + 7.25))
+        h_codes[1, 0] = list(zip(quarters, codes_10))
+        codes_20 = place_codes("20", HALF, AT_TAB + 5, at_s(8) + 6)
+        h_codes[2, 0] = [(first, codes_20)]
         y_first = [bank("y_first%d" % part, part)[:, : 2 * UNIT] for part in range(2)]
-
-        def first_block_pass(a, part):
-            nc.tensor.matmul_mx(
-                out=y_first[part],
-                lhsT=w1_first[:, a, :P].bitcast(E4M3),
-                lhsT_scale=w1_s[4 * a :, :P],
-                rhs=h_w[a, 0][:, quarters[part]].bitcast(E4M3),
-                rhs_scale=h_s[a, 0][:, quarters[part]],
-                start=(a == 0),
-                stop=(a == PASSES - 1),
-            )
-
-        for part in range(2):
-            first_block_pass(0, part)
+        for part, cols in enumerate(quarters):
+            product_pass(y_first[part], 0, 0, columns_of(codes_00, cols), True, False)
+        product_pass(y_first[0], 0, 1, codes_10[0], False, False)
         second_product(1, 0, 2, (0, 2, 1), slice(0, 1))
-        for a in (1, 2):
-            for part, cols in enumerate(quarters):
-                nc.vector.quantize_mx(
-                    out=h_w[a, 0][:, cols].bitcast(E4M3), scales=h_s[a, 0][:, cols], in_=pairs[a, part]
-                )
-                first_block_pass(a, part)
-        quantize_h(0, 1, at_s(3) + 6, at_s(10) + 6.5)
+        quantize_h(h_pair[1, 1], codes_10[1])
+        product_pass(y_first[1], 0, 1, codes_10[1], False, False)
+        for part, cols in enumerate(quarters):
+            quantize_h(h_pair[2, part], columns_of(codes_20, cols))
+            product_pass(y_first[part], 0, 2, columns_of(codes_20, cols), False, True)
+        last_cols = slice(S - 2 * UNIT, S)
+        picked_last = place_tile("picked_last", [P, 2 * UNIT], F32, at_s(8) + 4)
+        nc.vector.tensor_copy(picked_last[:], s_sb[SLICES - 1].indirect(listed(idx, last_cols)))
         second_product(1, 0, 2, (0, 2, 1), slice(1, PASSES))
         for n in (2, 3):
             second_product(n, 0, n + 2, (2, 0, 1))
@@ -377,19 +397,18 @@ def tile_list_fibre_equaliser_backward_kernel(
             nc.vector.scalar_tensor_tensor(y_sb[0][:, cols], y_first[part], -1.0, wgo_sb[:, cols], ALU.mult, ALU.mult)
         put_weighed(0)
 
-        late = place_tile("h_bf_late", [P, 2 * HALF * PACK], BF16, at_s(7) + 4)
-        h_bf[1, 1] = late[:, : HALF * PACK]
-        h_bf[2, 1] = late[:, HALF * PACK :]
-        multiply_gpsimd(1, 4)
-        square(1, 6, 2, at_s(5) + 4)
-        for n in (1, 2):
-            place_y(n, first, AT_FREE + 20 + 4 * n)
+        for n, kib in ((1, at_s(7) + 3), (2, AT_FREE + 28)):
+            place_y(n, first, kib)
             empty_y(n, 0, y_sb[n])
             weigh_gpsimd(n, at_s(11) + 2 * n)
             put_weighed(n)
+            if n == 1:
+                late = place_h([(1, 2), (1, 3), (2, 2), (2, 3)], at_s(7) + 4)
+                multiply_gpsimd(1, 4)
+                square(1, 6, 2, at_s(7))
         for n in (4, 5):
             second_product(n, 0, 7 - n, (2, 0, 1))
-        less_one_scalar(1, 6, AT_FREE + 24)
+        less_one_scalar(1, 6)
         for n in (3, 4):
             if n == 4:
                 empty_d(1, 6, AT_FREE + 28)
@@ -403,29 +422,37 @@ def tile_list_fibre_equaliser_backward_kernel(
         for u in range(4, UNITS):
             first_product(2, u, u if u > 5 else u - 4)
         for u in (4, 6):
-            square(2, u, 2, at_s(1) + 2 * u - 8)
-            less_one_scalar(2, u)
+            if u == 4:
+                square(2, u, 2, at_s(1))
+                less_one_scalar(2, u)
+            else:
+                rows = place_tile("sq_rows", [P, PACK, 2 * UNIT], F32, at_s(1) + 4)
+                nc.scalar.activation(rows[:, : PACK - 1], picked[2][:, : PACK - 1, last_cols], ACT.Square)
+                nc.scalar.activation(rows[:, PACK - 1], picked_last[:], ACT.Square)
+                factor[2, u] = less_one_from_rows("f2_6", rows[:], at_s(0))
             empty_d(2, u, AT_FREE + 16 + 2 * u)
             multiply_gpsimd(2, u)
             if u == 4:
-                place_y(5, first, at_s(3))
+                place_y(5, first, AT_TAB)
                 empty_y(5, 0, y_sb[5])
                 weigh_gpsimd(5)
                 put_weighed(5)
         for n in (6, 7):
             place_y(n, first, AT_FREE + 16 + 2 * n)
             empty_y(n, 0, y_sb[n])
-        late_w = place_tile("h_w_late", [P, 2 * HALF], U32, at_s(6) + 4)
-        late_s = place_tile("h_s_late", [P, 2 * HALF], U8, at_s(7))
-        nc.vector.quantize_mx(out=late_w[:].bitcast(E4M3), scales=late_s[:], in_=late[:])
+        codes_late = place_codes("late", S, at_s(6) + 4, at_s(7))
+        quantize_h(late, codes_late)
         for a in (1, 2):
-            h_w[a, 1] = late_w[:, halves[a - 1]]
-            h_s[a, 1] = late_s[:, halves[a - 1]]
-        for n in (6, 7):
-            weigh_and_put(n, first)
+            h_codes[a, 1] = [(first, columns_of(codes_late, halves[a - 1]))]
+        nc.gpsimd.memset(frames[7][:], 0.0)
+        weigh_and_put(6, first)
+        y_last_first = y_sb[7]
 
         for n in range(BLOCKS):
             second_product(n, 1, (n + 4) % 8, (1, 2, 0))
+            if n == 1:
+                y_sb[7] = y_last_first
+                weigh_and_put(7, first)
             place_y(n, second, at_w2(0) + 2 * n)
             empty_y(n, 1, y_sb[n])
             weigh_and_put(n, second)

@@ -102,7 +102,7 @@ def tile_list_fibre_equaliser_backward_kernel(
                 nc.sync.dma_start(w2_raw[a, e][:], rows[:, :, e * PASS // 2 : (e + 1) * PASS // 2])
 
         def load_w2(a):
-            w2_raw[a] = place_tile("w2_raw%d" % a, [P, PACK, PASS], F32, at_w2(a))
+            w2_raw[a] = place_tile("w2_raw%d" % a, [P, PACK, PASS], F32, AT_TAB)
             nc.sync.dma_start(
                 w2_raw[a][:], w2[:, a * PASS : (a + 1) * PASS].rearrange("(p j) c -> p j c", j=PACK)
             )
@@ -301,7 +301,7 @@ def tile_list_fibre_equaliser_backward_kernel(
 
         nc.vector.tensor_copy(v_s[:], tab_s[:].indirect(idx[:]))
         nc.vector.tensor_copy(v_w[:], tab_w[:].bitcast(U32).indirect(idx[:]))
-        round_w2(0, AT_TAB - 2, shared=True)
+        round_w2(0, AT_TAB - 4, shared=True)
         quantize_w2(0, AT_FREE + 44)
         place_picked(0, AT_TAB)
         gather_s(0)
@@ -329,10 +329,10 @@ def tile_list_fibre_equaliser_backward_kernel(
             gather_s(k)
         round_w2_halves(1, at_w2(0))
         empty_d(0, 6, at_w2(1) + 2)
-        codes_00 = place_codes("00", HALF, at_s(6), at_s(6) + 2)
+        codes_00 = place_codes("00", HALF, at_w2(1) + 6, at_s(4) + 6)
         h_codes[0, 0] = [(first, codes_00)]
         quantize_h(h_00, codes_00)
-        quantize_w2(1, at_s(6) + 4)
+        quantize_w2(1, at_s(5) + 4)
         h_01 = place_h([(0, 2), (0, 3)], at_w2(0))
         factor[0, 6] = less_one_from_rows("f0_6", picked[0][:, :, 6 * UNIT :], at_w2(1) - 2)
         for u in (4, 6):
@@ -348,17 +348,17 @@ def tile_list_fibre_equaliser_backward_kernel(
         square(1, 2, 2, AT_FREE + 40)
         less_one_scalar(1, 2)
         round_w2_halves(2, at_s(5))
-        empty_d(1, 2, at_w2(2) + 2)
+        empty_d(1, 2, at_w2(2) + 1)
 
         place_picked(2, at_s(2))
         for k in (8, 9, 10):
             gather_s(k)
-        codes_01 = place_codes("01", HALF, at_s(10), at_s(10) + 2)
+        codes_01 = place_codes("01", HALF, at_w2(2) + 5, at_s(4) + 6.5)
         h_codes[0, 1] = [(first, codes_01)]
         quantize_h(h_01, codes_01)
-        codes_10 = [place_codes("10", 2 * UNIT, at_s(10) + 6, at_s(10) + 7)]
+        codes_10 = [place_codes("10", 2 * UNIT, at_w2(2) + 7, at_s(4) + 7)]
         quantize_h(h_pair[1, 0], codes_10[0])
-        quantize_w2(2, at_s(10) + 3)
+        quantize_w2(2, at_s(6))
         place_h([(1, 1)], at_s(5))
         multiply_gpsimd(1, 2)
         for u in range(4):

from contextlib import ExitStack

import concourse.mybir as mybir

K, H, N, T, S, T2 = 512, 1536, 1024, 2048, 1024, 2048
FLOPS = 2 * K * H * S + 2 * H * N * S

F32 = mybir.dt.float32
BF16 = mybir.dt.bfloat16
I32 = mybir.dt.int32
U32 = mybir.dt.uint32
U16 = mybir.dt.uint16
U8 = mybir.dt.uint8
E4M3 = mybir.dt.float8_e4m3fn_x4
E5M2 = mybir.dt.float8_e5m2_x4
ACT = mybir.ActivationFunctionType
ALU = mybir.AluOpType

P = 128
PACK = 4
PASS = P * PACK
PASSES = H // PASS
SLICES = PASSES * PACK
HALF = 512
BLOCKS = N // P
PER_COLUMN = 16
UNIT = 128
UNITS = S // UNIT
FRAMES = 8
EARLY_FRAMES = 3
FIRST_BLOCKS = 3
LEAD = 512
KB = 1024

AT_W2 = 96
AT_TAB = 200
AT_FRAME = 120
AT_W1 = 176
AT_WGO = 188
AT_TAB_S = 168
AT_V_W = 170
AT_V_S = 174
AT_W1_S = 175
AT_FREE = 192


def tile_list_fibre_equaliser_backward_kernel(
    tc, tab_words, tab_scales, offs, offs2, w2, w1_words, w1_scales, sT, wgo, out
):
    nc = tc.nc
    with ExitStack() as ctx:
        lists = ctx.enter_context(tc.tile_pool(name="lists", bufs=1))
        arena = ctx.enter_context(tc.tile_pool(name="arena", bufs=1))
        psum = ctx.enter_context(tc.psum_pool(name="psum", bufs=1))

        def place_tile(name, shape, dtype, kib):
            return arena.tile(shape, dtype, name=name, tag=name, align_bytes=64, offset=int(kib * KB))

        def bank(name, number):
            return psum.tile([P, HALF], F32, name=name, tag="bank%d" % number)

        def at_s(k):
            return 8 * k

        def at_w2(a):
            return AT_W2 + 8 * a

        idx = lists.tile([P, S // PER_COLUMN], U16, name="idx")
        idx2 = lists.tile([P, S // PER_COLUMN], U16, name="idx2")
        tab_w = place_tile("tab_w", [P, T], I32, AT_FREE + 24)
        tab_s = place_tile("tab_s", [P, T], U8, AT_TAB_S)
        v_w = place_tile("v_w", [P, S], U32, AT_V_W)
        v_s = place_tile("v_s", [P, S], U8, AT_V_S)
        first_cols = FIRST_BLOCKS * P
        w1_first = place_tile("w1_first", [P, PASSES, first_cols], I32, AT_W1)
        w1_rest = place_tile("w1_rest", [P, PASSES, N - first_cols], I32, AT_W1 + PASSES * first_cols * 4 / KB)
        w1_s = place_tile("w1_s", [P, N], U8, AT_W1_S)
        wgo_sb = place_tile("wgo_sb", [P, S], F32, AT_WGO)
        frames = [place_tile("frame%d" % f, [P, T2], F32, {6: AT_TAB - 8, 7: at_s(7) + 4}.get(f, AT_FRAME + 8 * f)) for f in range(FRAMES)]

        def listed(tile, cols):
            return tile[:, cols.start // PER_COLUMN : cols.stop // PER_COLUMN]

        nc.gpsimd.memset(tab_s[:].bitcast(I32), 0)
        nc.gpsimd.memset(w1_s[:].bitcast(I32), 0)
        for frame in frames[:EARLY_FRAMES]:
            nc.gpsimd.memset(frame[:], 0.0)

        s_rows = sT.rearrange("(a p t) c -> a p t c", p=P, t=PACK)
        w1_rows = w1_words.rearrange("a p n i -> p a (n i)").bitcast(I32)
        s_sb, w2_raw = {}, {}

        def load_s(k):
            a, t = divmod(k, PACK)
            s_sb[k] = place_tile("s%d" % k, [P, T], F32, {0: AT_FRAME + 8 * (EARLY_FRAMES + 1) + 4, 1: AT_FRAME + 8 * EARLY_FRAMES}.get(k, at_s(k)))[:]
            nc.sync.dma_start(s_sb[k], s_rows[a][:, t, :])

        def load_w2_halves(a):
            rows = w2[:, a * PASS : (a + 1) * PASS].rearrange("(p j) c -> p j c", j=PACK)
            for e in range(2):
                w2_raw[a, e] = place_tile("w2_raw%d%d" % (a, e), [P, PACK, PASS // 2], F32, at_w2(a) + 4 * (1 - e))
                nc.sync.dma_start(w2_raw[a, e][:], rows[:, :, e * PASS // 2 : (e + 1) * PASS // 2])

        def load_w2(a):
            w2_raw[a] = place_tile("w2_raw%d" % a, [P, PACK, PASS], F32, AT_TAB)
            nc.sync.dma_start(
                w2_raw[a][:], w2[:, a * PASS : (a + 1) * PASS].rearrange("(p j) c -> p j c", j=PACK)
            )

        nc.sync.dma_start(idx[:], offs)
        words = tab_words[0].rearrange("p t i -> p (t i)").bitcast(I32)
        nc.sync.dma_start(tab_w[:, :LEAD], words[:, :LEAD])
        for q in range(4):
            nc.sync.dma_start(
                tab_s[32 * q : 32 * q + 4, :].bitcast(I32), tab_scales[0, 4 * q : 4 * q + 4, :].bitcast(I32)
            )
        nc.sync.dma_start(tab_w[:, LEAD:], words[:, LEAD:])
        load_w2(0)
        w2_before = {7: 1, 11: 2}
        for k in range(SLICES):
            if k in w2_before:
                load_w2_halves(w2_before[k])
            load_s(k)
        for q in range(4):
            nc.sync.dma_start(
                w1_s[32 * q : 32 * q + 4 * PASSES, :].bitcast(I32),
                w1_scales[:, 4 * q : 4 * q + 4, :].bitcast(I32),
            )
        nc.sync.dma_start(w1_first[:], w1_rows[:, :, :first_cols])
        nc.sync.dma_start(wgo_sb[:], wgo)
        nc.sync.dma_start(idx2[:], offs2)
        nc.sync.dma_start(w1_rest[:], w1_rows[:, :, first_cols:])

        w2_bf, w2_w, w2_s, h_pair, h_codes, picked, factor, d_sb, d_bank, y_bank, y_sb = ({} for i in range(11))
        whole = slice(0, S)
        halves = [slice(0, HALF), slice(HALF, S)]
        first, second = halves
        quarters = [slice(part * 2 * UNIT, (part + 1) * 2 * UNIT) for part in range(2)]

        def round_w2(a, kib, shared=False):
            w2_bf[a] = place_tile("w2_bf%d" % a, [P, PASS * PACK], BF16, kib)
            rounded = w2_bf[a][:].rearrange("p (t m j) -> p m j t", t=PACK, j=PACK)
            raw = w2_raw[a][:].rearrange("p j (m t) -> p m j t", t=PACK)
            if shared:
                nc.scalar.copy(rounded[:, :, :, :2], raw[:, :, :, :2])
                nc.vector.tensor_copy(rounded[:, :, :, 2:], raw[:, :, :, 2:])
            else:
                nc.scalar.copy(rounded, raw)

        def round_w2_halves(a, kib):
            w2_bf[a] = place_tile("w2_bf%d" % a, [P, PASS * PACK], BF16, kib)
            rounded = w2_bf[a][:].rearrange("p (t m j) -> p m j t", t=PACK, j=PACK)
            for e in range(2):
                raw = w2_raw[a, e][:].rearrange("p j (m t) -> p m j t", t=PACK)
                nc.scalar.copy(rounded[:, e * P // 2 : (e + 1) * P // 2], raw)

        def quantize_w2(a, kib):
            w2_w[a] = place_tile("w2_w%d" % a, [P, PASS], U32, kib)
            w2_s[a] = place_tile("w2_s%d" % a, [P, PASS], U8, kib + 2)
            nc.vector.quantize_mx(out=w2_w[a][:].bitcast(E4M3), scales=w2_s[a][:], in_=w2_bf[a][:])

        def place_picked(a, kib):
            picked[a] = place_tile("picked%d" % a, [P, PACK, S], F32, kib)

        def gather_s(k):
            a, t = divmod(k, PACK)
            pieces = halves if k % PACK == PACK - 1 else [whole]
            if k == SLICES - 1:
                pieces = [slice(0, UNIT), slice(UNIT, HALF), slice(HALF, S - 2 * UNIT)]
            for cols in pieces:
                nc.vector.tensor_copy(picked[a][:, t, cols], s_sb[k].indirect(listed(idx, cols)))

        def first_product(a, u, number):
            d_bank[a, u] = bank("d%d_%d" % (a, u), number)
            cols = slice(u * UNIT, (u + 1) * UNIT)
            for t in range(PACK):
                rows = slice(t * P, (t + 1) * P)
                nc.tensor.matmul_mx(
                    out=d_bank[a, u][:, t * UNIT : (t + 1) * UNIT],
                    lhsT=w2_w[a][:, rows].bitcast(E4M3),
                    lhsT_scale=w2_s[a][:, rows],
                    rhs=v_w[:, cols].bitcast(E5M2),
                    rhs_scale=v_s[:, cols],
                    start=True,
                    stop=True,
                )

        def square(a, u, count, kib):
            tile = place_tile("sq%d_%d" % (a, u), [P, count * HALF], F32, kib)
            nc.scalar.activation(
                tile[:].rearrange("p (c i t) -> p c t i", i=4, t=PACK),
                picked[a][:, :, u * UNIT : (u + count) * UNIT].rearrange("p t (c i) -> p c t i", i=4),
                ACT.Square,
            )
            factor[a, u] = tile

        def square_rows(a, t, cols):
            nc.scalar.activation(picked[a][:, t, cols], picked[a][:, t, cols], ACT.Square)

        def less_one_from_rows(name, rows, kib):
            tile = place_tile(name, [P, 2 * HALF], F32, kib)
            nc.scalar.activation(
                tile[:].rearrange("p (c i t) -> p c t i", i=4, t=PACK),
                rows.rearrange("p t (c i) -> p c t i", i=4),
                ACT.Copy,
                bias=-1.0,
            )
            return tile

        def empty_d(a, u, kib):
            d_sb[a, u] = place_tile("d_sb%d_%d" % (a, u), [P, 2 * HALF], F32, kib)
            for e in range(2):
                nc.scalar.copy(
                    d_sb[a, u][:, e * HALF : (e + 1) * HALF].rearrange("p (c t) -> p c t", t=PACK),
                    d_bank[a, u + e][:].rearrange("p (t c) -> p c t", t=PACK),
                )

        def less_one_scalar(a, u, kib=None):
            squares = factor[a, u]
            if kib is not None:
                factor[a, u] = place_tile("f%d_%d" % (a, u), [P, 2 * HALF], F32, kib)
            nc.scalar.activation(factor[a, u][:], squares[:], ACT.Copy, bias=-1.0)

        def h_cols(a, u, count):
            return h_pair[a, u // 2][:, u % 2 * HALF : (u % 2 + count) * HALF]

        def multiply_gpsimd(a, u, e=0, count=2):
            cols = slice(e * HALF, (e + count) * HALF)
            nc.gpsimd.tensor_tensor(h_cols(a, u + e, count), factor[a, u][:, cols], d_sb[a, u][:, cols], ALU.mult)

        def multiply_vector(a, u, e=0):
            nc.vector.scalar_tensor_tensor(
                h_cols(a, u + e, 1).rearrange("p (c t) -> p c t", t=PACK),
                factor[a, u][:, e * HALF : (e + 1) * HALF].rearrange("p (c t) -> p c t", t=PACK),
                1.0,
                d_bank[a, u + e][:].rearrange("p (t c) -> p c t", t=PACK),
                ALU.subtract,
                ALU.mult,
            )

        def place_h(pairs, kib):
            a, pair = pairs[0]
            tile = place_tile("h_bf%d%d" % (a, pair), [P, len(pairs) * 2 * HALF], BF16, kib)
            for e, key in enumerate(pairs):
                h_pair[key] = tile[:, e * 2 * HALF : (e + 1) * 2 * HALF]
            return tile[:]

        def place_codes(name, columns, kib, scales_kib):
            words = place_tile("h_w" + name, [P, columns], U32, kib)
            return words[:], place_tile("h_s" + name, [P, columns], U8, scales_kib)[:]

        def quantize_h(source, codes):
            nc.vector.quantize_mx(out=codes[0].bitcast(E4M3), scales=codes[1], in_=source)

        def columns_of(codes, cols):
            return codes[0][:, cols], codes[1][:, cols]

        def product_pass(target, n, a, codes, start, stop):
            ncols = slice(n * P, (n + 1) * P)
            w1_w = w1_first[:, :, ncols] if n < FIRST_BLOCKS else w1_rest[:, :, n * P - first_cols : (n + 1) * P - first_cols]
            nc.tensor.matmul_mx(
                out=target,
                lhsT=w1_w[:, a, :].bitcast(E4M3),
                lhsT_scale=w1_s[4 * a :, ncols],
                rhs=codes[0].bitcast(E4M3),
                rhs_scale=codes[1],
                start=start,
                stop=stop,
            )

        def second_product(n, half, number, order, part=slice(0, PASSES)):
            for a in order[part]:
                if a == order[0]:
                    y_bank[n, half] = bank("y%d_%d" % (n, half), number)
                pieces = h_codes[a, half]
                for e, (cols, codes) in enumerate(pieces):
                    last = a == order[-1] and e == len(pieces) - 1
                    product_pass(y_bank[n, half][:, cols], n, a, codes, a == order[0], last)

        def place_y(n, cols, kib):
            y_sb[n] = place_tile("y_sb%d_%d" % (n, cols.start), [P, cols.stop - cols.start], F32, kib)[:]

        def empty_y(n, half, target):
            nc.scalar.activation(target, y_bank[n, half][:], ACT.Copy, scale=-1.0)

        def weigh_gpsimd(n, kib=None):
            raw = y_sb[n]
            if kib is not None:
                y_sb[n] = place_tile("y_weighed%d" % n, [P, HALF], F32, kib)[:]
            nc.gpsimd.tensor_tensor(y_sb[n], raw, wgo_sb[:, first], ALU.mult)

        def put_weighed(n):
            nc.vector.tensor_copy(frames[n][:].indirect(listed(idx2, first)), y_sb[n])

        def weigh_and_put(n, cols):
            window = frames[n % FRAMES][:].indirect(listed(idx2, cols))
            nc.vector.tensor_tensor(window, y_sb[n], wgo_sb[:, cols], ALU.mult)

        def store(n):
            nc.sync.dma_start(out[n * P : (n + 1) * P, :], frames[n % FRAMES][:])

        nc.vector.tensor_copy(v_s[:], tab_s[:].indirect(idx[:]))
        nc.vector.tensor_copy(v_w[:], tab_w[:].bitcast(U32).indirect(idx[:]))
        round_w2(0, AT_TAB - 4, shared=True)
        quantize_w2(0, AT_FREE + 44)
        place_picked(0, AT_TAB)
        gather_s(0)
        for u in range(UNITS):
            first_product(0, u, u)
        for u in (0, 2, 4):
            empty_d(0, u, AT_FREE + 24 + 2 * u)
        square_rows(0, 0, whole)
        for k in (1, 2):
            gather_s(k)
            square_rows(0, k, whole)
        for f in (6, 4, 5, 3):
            nc.gpsimd.memset(frames[f][:], 0.0)
        gather_s(3)
        h_00 = place_h([(0, 0), (0, 1)], at_w2(0) + 4)
        for u, kib in ((0, AT_FREE + 36), (2, AT_FREE + 40), (4, at_s(4))):
            for cols in {0: quarters, 4: [second]}.get(u, []):
                square_rows(0, PACK - 1, cols)
            factor[0, u] = less_one_from_rows("f0_%d" % u, picked[0][:, :, u * UNIT : (u + 2) * UNIT], kib)
            if u < 4:
                multiply_gpsimd(0, u)

        place_picked(1, at_s(0))
        for k in (4, 5, 6):
            gather_s(k)
        round_w2_halves(1, at_w2(0))
        empty_d(0, 6, at_w2(1) + 2)
        codes_00 = place_codes("00", HALF, at_w2(1) + 6, at_s(4) + 6)
        h_codes[0, 0] = [(first, codes_00)]
        quantize_h(h_00, codes_00)
        quantize_w2(1, at_s(5) + 4)
        h_01 = place_h([(0, 2), (0, 3)], at_w2(0))
        factor[0, 6] = less_one_from_rows("f0_6", picked[0][:, :, 6 * UNIT :], at_w2(1) - 2)
        for u in (4, 6):
            multiply_gpsimd(0, u)
        for u in range(UNITS):
            first_product(1, u, u)
        empty_d(1, 0, AT_FREE + 24)
        gather_s(7)
        square(1, 0, 2, AT_FREE + 36)
        less_one_scalar(1, 0)
        place_h([(1, 0)], at_s(4) + 4)
        multiply_gpsimd(1, 0)
        square(1, 2, 2, AT_FREE + 40)
        less_one_scalar(1, 2)
        round_w2_halves(2, at_s(5))
        empty_d(1, 2, at_w2(2) + 1)

        place_picked(2, at_s(2))
        for k in (8, 9, 10):
            gather_s(k)
        codes_01 = place_codes("01", HALF, at_w2(2) + 5, at_s(4) + 6.5)
        h_codes[0, 1] = [(first, codes_01)]
        quantize_h(h_01, codes_01)
        codes_10 = [place_codes("10", 2 * UNIT, at_w2(2) + 7, at_s(4) + 7)]
        quantize_h(h_pair[1, 0], codes_10[0])
        quantize_w2(2, at_s(6))
        place_h([(1, 1)], at_s(5))
        multiply_gpsimd(1, 2)
        for u in range(4):
            first_product(2, u, u)
        gather_s(11)
        place_h([(2, 0)], at_s(8) + 4)
        place_h([(2, 1)], at_s(8) + 2)
        for u in range(4):
            square(2, u, 1, at_s(9) + 2 + 2 * u if u < 2 else AT_TAB + 2 * u)
            multiply_vector(2, u)
        square(1, 4, 2, at_s(9))
        less_one_scalar(1, 4)
        empty_d(1, 4, at_s(9) + 4)
        codes_10.append(place_codes("11", 2 * UNIT, AT_TAB + 4, at_s(10) + 7.25))
        h_codes[1, 0] = list(zip(quarters, codes_10))
        codes_20 = place_codes("20", HALF, AT_TAB + 5, at_s(8) + 6)
        h_codes[2, 0] = [(first, codes_20)]
        y_first = [bank("y_first%d" % part, part)[:, : 2 * UNIT] for part in range(2)]
        for part, cols in enumerate(quarters):
            product_pass(y_first[part], 0, 0, columns_of(codes_00, cols), True, False)
        product_pass(y_first[0], 0, 1, codes_10[0], False, False)
        second_product(1, 0, 2, (0, 2, 1), slice(0, 1))
        quantize_h(h_pair[1, 1], codes_10[1])
        product_pass(y_first[1], 0, 1, codes_10[1], False, False)
        for part, cols in enumerate(quarters):
            quantize_h(h_pair[2, part], columns_of(codes_20, cols))
            product_pass(y_first[part], 0, 2, columns_of(codes_20, cols), False, True)
        last_cols = slice(S - 2 * UNIT, S)
        picked_last = place_tile("picked_last", [P, 2 * UNIT], F32, at_s(8) + 4)
        nc.vector.tensor_copy(picked_last[:], s_sb[SLICES - 1].indirect(listed(idx, last_cols)))
        second_product(1, 0, 2, (0, 2, 1), slice(1, PASSES))
        for n in (2, 3):
            second_product(n, 0, n + 2, (2, 0, 1))
        place_y(0, first, AT_FREE + 44)
        for part, cols in enumerate(quarters):
            nc.vector.scalar_tensor_tensor(y_sb[0][:, cols], y_first[part], -1.0, wgo_sb[:, cols], ALU.mult, ALU.mult)
        put_weighed(0)

        for n, kib in ((1, at_s(7) + 3), (2, AT_FREE + 28)):
            place_y(n, first, kib)
            empty_y(n, 0, y_sb[n])
            weigh_gpsimd(n, at_s(11) + 2 * n)
            put_weighed(n)
            if n == 1:
                late = place_h([(1, 2), (1, 3), (2, 2), (2, 3)], at_s(7) + 4)
                multiply_gpsimd(1, 4)
                square(1, 6, 2, at_s(7))
        for n in (4, 5):
            second_product(n, 0, 7 - n, (2, 0, 1))
        less_one_scalar(1, 6)
        for n in (3, 4):
            if n == 4:
                empty_d(1, 6, AT_FREE + 28)
                multiply_gpsimd(1, 6)
            place_y(n, first, AT_FREE + 26 + 2 * n)
            empty_y(n, 0, y_sb[n])
            weigh_gpsimd(n)
            put_weighed(n)
        for n in (6, 7):
            second_product(n, 0, n - 2, (2, 0, 1))
        for u in range(4, UNITS):
            first_product(2, u, u if u > 5 else u - 4)
        for u in (4, 6):
            if u == 4:
                square(2, u, 2, at_s(1))
                less_one_scalar(2, u)
            else:
                rows = place_tile("sq_rows", [P, PACK, 2 * UNIT], F32, at_s(1) + 4)
                nc.scalar.activation(rows[:, : PACK - 1], picked[2][:, : PACK - 1, last_cols], ACT.Square)
                nc.scalar.activation(rows[:, PACK - 1], picked_last[:], ACT.Square)
                factor[2, u] = less_one_from_rows("f2_6", rows[:], at_s(0))
            empty_d(2, u, AT_FREE + 16 + 2 * u)
            multiply_gpsimd(2, u)
            if u == 4:
                place_y(5, first, AT_TAB)
                empty_y(5, 0, y_sb[5])
                weigh_gpsimd(5)
                put_weighed(5)
        for n in (6, 7):
            place_y(n, first, AT_FREE + 16 + 2 * n)
            empty_y(n, 0, y_sb[n])
        codes_late = place_codes("late", S, at_s(6) + 4, at_s(7))
        quantize_h(late, codes_late)
        for a in (1, 2):
            h_codes[a, 1] = [(first, columns_of(codes_late, halves[a - 1]))]
        nc.gpsimd.memset(frames[7][:], 0.0)
        weigh_and_put(6, first)
        y_last_first = y_sb[7]

        for n in range(BLOCKS):
            second_product(n, 1, (n + 4) % 8, (1, 2, 0))
            if n == 1:
                y_sb[7] = y_last_first
                weigh_and_put(7, first)
            place_y(n, second, at_w2(0) + 2 * n)
            empty_y(n, 1, y_sb[n])
            weigh_and_put(n, second)
            store(n)
